import numpy as np, ml_dtypes
CORES = [9,25,41,57]
N = 4
BF = ml_dtypes.bfloat16
T, NB, C, RO = 2, 12, 4096, 3
V, W, CN = 8 * N * T, 2 ** NB, C // N
def scores(rng):
    w = rng.choice(np.array([0.0, 0.25, 0.5, 0.75], np.float32), (N, 8, T, 1, 1))
    a = rng.integers(0, 256, (N, 8, T, 1, W)).astype(np.float32); b = rng.integers(0, 256, (N, 8, T, 16, W)).astype(np.float32)
    return np.floor(w * a + (1 - w) * b)
def parents(rng):
    return np.argsort(rng.random((V, V)) + 2 * np.eye(V), axis=1)[:, :NB]
def orders(rng):
    return np.argsort(rng.random((V, C)), axis=0)
def full(rng, cd):
    v = int(rng.integers(0, V)); m = rng.permutation(C) & (W - 1)
    key = 2 * rng.random((V, C)); bit = (m[None, :] >> np.arange(NB)[:, None]) & 1
    key[v] = 1.0; key[cd[v]] = 0.9 * rng.random((NB, C)) + 1.1 * (1 - bit)
    return np.argsort(np.argsort(key, axis=0), axis=0)
def moves(rng):
    return 2 * rng.integers(0, V // 2, (RO, C)) + 1, rng.integers(0, V, (RO, C)), rng.integers(0, 18, (RO, C))
def pack(rng, v, cd, p, fa, ic, t):
    t = np.array(t)
    for k in range(N):
        i = k * CN + rng.permutation(CN)[:2]; t[:, i[0]] = 0; t[:, i[1]] = 17
    same = lambda a: np.repeat(np.asarray(a)[None], N, axis=0).astype(np.int32)
    return {"tab": np.ascontiguousarray(v.transpose(0, 1, 3, 2, 4)).reshape(N, 128, T * W).astype(np.float32).astype(BF),
            "cand": np.ascontiguousarray(np.reshape(cd, (N, 8, T * NB))).astype(np.int32),
            "pos0": same(p), "fac": same(fa), "inc": same(ic), "th": same(t)}
def setup_inputs(rng):
    fa, ic, t = moves(rng)
    t = np.where(rng.random((RO, C)) < 0.7, rng.integers(5, 12, (RO, C)), t)
    return pack(rng, scores(rng), parents(rng), orders(rng), fa, ic, t)
def setup_inputs_ties(rng):
    v = rng.integers(0, 2 + rng.integers(0, 2, (N, 8, T, 1, 1)), (N, 8, T, 16, W))
    fa, ic, t = moves(rng); u = rng.integers(0, 3, (RO, C))
    fa = np.where(u < 2, 1, fa); ic = np.where(u == 0, 0, ic)
    t = np.where(rng.random((RO, C)) < 0.6, rng.choice(np.array([1, 8, 15, 16, 17]), (RO, C)), t)
    o = rng.permutation(V); b = V // 16; cd = np.empty((V, NB), np.int64); p = np.empty((V, C), np.int64)
    j = np.argsort(rng.random((V, 16)) + 2 * np.tile(np.eye(16), (b, 1)), axis=1)[:, :NB]
    cd[o] = o[16 * (np.arange(V) >> 4)[:, None] + j]
    p[o] = (16 * np.argsort(rng.random((b, C)), axis=0)[:, None, :] + np.argsort(rng.random((b, 16, C)), axis=1)).reshape(V, C)
    al = rng.random(C) < 0.5; p = np.where(al[None, :], p, orders(rng))
    fa[0] = np.where(al, 1, fa[0]); ic[0] = np.where(al, 16 * rng.integers(1, b, C), ic[0])
    return pack(rng, v, cd, p, fa, ic, t)
def setup_inputs_ends(rng):
    v = scores(rng); cd = parents(rng); p = orders(rng); fa, ic, t = moves(rng)
    v[..., 0] = 255 * rng.integers(0, 2, v.shape[:-1]); v[..., W - 1] = 255 * rng.integers(0, 2, v.shape[:-1])
    v[:, :, :, 0] = 0; v[:, :, :, 15] = 255
    o = rng.permutation(V); n = V // 8; me = np.arange(V)[:, None]
    cd[o[:n]] = me[o[:n]]; cd[o[n:2 * n]] = cd[o[n:2 * n], :1]; cd[o[2 * n:3 * n]] = rng.choice(np.array([0, V - 1]), (n, NB)); cd[o[3 * n:4 * n], NB - 1] = o[3 * n:4 * n]
    cd[o[3 * n:], 0] = int(rng.integers(0, V))
    u = rng.integers(0, 4, C)[None, :]
    p = np.where(u == 0, me, np.where(u == 1, V - 1 - me, np.where(u == 2, (me + rng.integers(0, V, C)[None, :]) & (V - 1), p)))
    fa = np.where(rng.random((RO, C)) < 0.5, rng.choice(np.array([1, V - 1]), (RO, C)), fa); ic = np.where(rng.random((RO, C)) < 0.5, rng.choice(np.array([0, 1, V - 1]), (RO, C)), ic)
    return pack(rng, v, cd, p, fa, ic, t)
def setup_inputs_lone(rng):
    v = scores(rng); k = int(rng.integers(0, N)); c = 255 * rng.integers(0, 2, N)
    for r in range(N):
        if r != k: v[r] = c[r]
    p = orders(rng)[:, :3][:, rng.integers(0, 3, C)]; fa, ic, t = moves(rng)
    u = rng.integers(0, 2, (RO, C)); fa = np.take_along_axis(fa[:, :2], u, 1); ic = np.take_along_axis(ic[:, :2], u, 1)
    d = pack(rng, v, parents(rng), p, fa, ic, t); h = d["th"]; o = [int(a) * CN for a in rng.permutation(N)]
    for a, i, x in ((o[0], 1, 17), (o[1], 0, 17), (o[1], 1, 0), (o[3], RO - 1, 17)): h[:, i, a:a + CN] = x
    h[:, :, o[2]:o[2] + CN] = np.minimum(h[:, :, o[2]:o[2] + CN], 16)
    return d
def setup_inputs_votes(rng):
    base = rng.permutation(V); cd = np.empty((V, NB), np.int64); pb = np.empty((V, 1), np.int64); pb[base, 0] = np.arange(V)
    for j in range(V): cd[base[j]] = base[np.resize(rng.permutation(max(j, 1)), NB)]
    pop = np.add.reduce((np.arange(W)[None, :] >> np.arange(NB)[:, None]) & 1, axis=0)
    opp = np.concatenate([rng.permutation(12) < 6, rng.permutation(4) < 2])
    a = rng.integers(52, 73, (N, 8, T, 16, 1)); a[:, :, :, ~opp] = 255; a[N - 1] = 255
    up = (np.arange(16) < 12)[:, None] ^ (opp[:, None] & (np.arange(N) < N - 1)[:, None, None, None, None])
    w = (a * pop) // NB; v = (rng.random(a.shape) * (256 - a)).astype(np.int64) + np.where(up, w, a - w)
    u = rng.integers(0, 6, C)[None, :]
    p = np.where(u < 2, pb, np.where(u == 2, V - 1 - pb, np.where(u == 3, (pb + rng.integers(0, V, C)[None, :]) & (V - 1), orders(rng))))
    fa, ic, t = moves(rng); back = rng.random((RO, C)) < 0.6
    fa = np.where(back, V - 1, fa); ic = np.where(back, V - 1, ic)
    t = np.where(rng.random((RO, C)) < 0.7, rng.choice(np.array([4, 5, 12, 13]), (RO, C)), t)
    return pack(rng, v, cd, p, fa, ic, t)
def setup_inputs_spread(rng):
    s = np.exp2(8 * rng.random((N, 8, T, 1, W), dtype=np.float32)) * (rng.random((N, 8, T, 1, W)) > 0.0625)
    v = np.minimum(np.floor(s * rng.random((N, 8, T, 16, W), dtype=np.float32)), 255)
    fa, ic, t = moves(rng); cd = parents(rng)
    return pack(rng, v, cd, full(rng, cd), fa, ic, t)
def check_inputs(d):
    bad = []
    x = np.asarray(d["tab"]).astype(np.float32)
    if not np.all((x >= 0) & (x <= 255) & (x == np.floor(x))): bad.append("whole numbers of tab")
    for k, lo, hi in (("cand", 0, V - 1), ("pos0", 0, V - 1), ("fac", 1, V - 1), ("inc", 0, V - 1), ("th", 0, 17)):
        if np.min(d[k]) < lo or np.max(d[k]) > hi: bad.append("range of " + k)
    if not np.all(np.sort(d["pos0"], axis=1) == np.arange(V)[None, :, None]): bad.append("orders of pos0")
    if not np.all((np.asarray(d["fac"]) & 1) == 1): bad.append("odd numbers of fac")
    for k in ("pos0", "fac", "inc", "th"):
        if np.any(d[k] != d[k][:1]): bad.append("one " + k + " on all ranks")
    return bad
def reference(tab, cand, pos0, fac, inc, th):
    tb = np.ascontiguousarray(tab.astype(np.float32).astype(np.int32).reshape(N, 8, 16, T, W).transpose(0, 1, 3, 2, 4)).reshape(V, 16, W)
    cd = cand.astype(np.int64).reshape(V, NB)
    def score(p):
        before = (p[cd] < p[:, None, :]).astype(np.int64)
        m = np.add.reduce(before << np.arange(NB)[None, :, None], axis=1)
        return np.add.reduce(np.take_along_axis(tb, m[:, None, :], 2).astype(np.int64), axis=0)
    p = pos0[0].astype(np.int64); F = score(p); flags = []
    for k in range(RO):
        q = (fac[0, k].astype(np.int64) * p + inc[0, k]) & (V - 1)
        G = score(q)
        ok = np.add.reduce((G >= F).astype(np.int64), axis=0) >= th[0, k]
        p = np.where(ok, q, p); F = np.where(ok, G, F); flags.append(ok)
    A = np.stack(flags).astype(np.float32)
    return {"yf": np.ascontiguousarray(F.reshape(16, N, CN).transpose(1, 0, 2)).astype(np.float32), "ya": np.ascontiguousarray(A.reshape(RO, N, CN).transpose(1, 0, 2))}

@@ -1,0 +1,553 @@
+from concourse.bass import DstId, RemoteDMATransfer
+from concourse.mybir import AluOpType as OP, ActivationFunctionType as AF
+
+N = 4
+CB = dict(FR=0, GT=144, CR=336, WR=656, ON=976, NH=1104, ID=1296, IN=1424, SEL=1552, U=1568, W=1760, CAND=2480, CO=2672, SBD=2800)
+WI = dict(PI=0, MOD=16, CAND=96, CO=288, POS=416)
+SCRATCH = {
+    "tabs": ("sbuf", [128, 8192], "bfloat16"),
+    "cb": ("sbuf", [128, 2928], "bfloat16"),
+    "wi": ("sbuf", [128, 2464], "int32"),
+    "wf": ("sbuf", [128, 7424], "float32"),
+    "i2": ("sbuf", [128, 128], "float16"),
+    "yb": ("sbuf", [128, 1536], "float16"),
+    "flb": ("sbuf", [128, 1536], "bfloat16"),
+    "pos2": ("sbuf", [128, 2048], "bfloat16"),
+    "pz": ("sbuf", [128, 2048], "bfloat16"),
+    "pt": ("sbuf", [128, 512], "bfloat16"),
+    "sall": ("sbuf", [128, 768], "bfloat16"),
+    "bits": ("sbuf", [128, 48 * 512], "bfloat16"),
+    "gat": ("sbuf", [128, 32 * 1024], "bfloat16"),
+    "mo": ("sbuf", [128, 2048], "uint16"),
+    "mi": ("sbuf", [128, 2048], "uint16"),
+    "so": ("sbuf", [128, 2048], "float32"),
+    "si": ("sbuf", [128, 2048], "float32"),
+    "ob": ("sbuf", [128, 256], "float32"),
+}
+for _b in range(8):
+    SCRATCH["ps%d" % _b] = ("psum", [128, 512], "float32")
+SEMAPHORES = (["eP", "eV", "eA", "eG", "sent", "dc", "dp0", "dp1", "dp2", "dp3", "dco", "dt", "do", "sS"]
+              + ["%s%d%d%d" % (w, a, h, k) for w in "ms" for a in range(3) for h in range(2) for k in range(3)])
+
+MODES = {"per": [[(0, 1)], [(1, 1)], [(2, 1)]], "two": [[(0, 2), (1, 2)], [(2, 1)]], "one": [[(0, 4), (1, 4), (2, 2)]]}
+CFG = dict(mm="per", sm="per", tsplit=4096, slack=0.15, maxd=3, ba=3.5, bo=5.0, bd=1.0)
+NOM = dict(f=1.25, gr=1.56, pc=0.5, pf=0.02, fix=0.03, fixa=0.06, sem=0.1, iss=0.5, st=1.5, row=0.04, bw=15e3, wake=0.3,
+           first=2.0, ldst=1.6, lbw=300e3)
+
+
+def build(g, T, rank, topo, cfg, NE):
+    ops = []
+    cur = [-1, -1]
+    Q = {"P": g.tensor, "V": g.vector, "A": g.scalar, "G": g, "S": g.sync}
+    V, PE, ACT = g.vector, g.tensor, g.scalar
+    top, jobs, sent = [0], [0], [0]
+
+    def add(eng, cyc, deps, fn, job=None, role=None, kind="c", n=1, after=(), info=None):
+        ops.append(dict(id=len(ops), eng=eng, cyc=cyc, deps=[d for d in deps if d is not None], fn=fn, job=job,
+                        role=role, kind=kind, n=n, after=list(after), info=info, tag=tuple(cur)))
+        return len(ops) - 1
+
+    def wa(n):
+        top[0] += (n + 7) // 8 * 8
+        return top[0] - (n + 7) // 8 * 8
+
+    def newjob():
+        jobs[0] += 1
+        return jobs[0]
+
+    def cb(name, a=0, n=1, p0=0, p1=128):
+        return T.cb[p0:p1, CB[name] + a:CB[name] + a + n]
+
+    def wf(a, n=1, step=1, p1=128):
+        return T.wf[0:p1, a:a + (n - 1) * step + 1:step] if step > 1 else T.wf[0:p1, a:a + n]
+
+    def wi(name, a=0, n=1, p0=0, p1=128):
+        return T.wi[p0:p1, WI[name] + a:WI[name] + a + n]
+
+    def vop(cyc, deps, fn, n=1, **kw):
+        return add("V", cyc, deps, lambda e, P, inc: fn(P, inc), n=n, **kw)
+
+    def ts(cyc, deps, *a):
+        return vop(cyc, deps, lambda P, inc: inc(V.tensor_scalar(*a)))
+
+    def tt(cyc, deps, *a):
+        return vop(cyc, deps, lambda P, inc: inc(V.tensor_tensor(*a)))
+
+    def cp(cyc, deps, *prs):
+        return vop(cyc, deps, lambda P, inc: [inc(V.tensor_copy(o, i)) for o, i in prs], n=len(prs))
+
+    def ms(cyc, o, c):
+        return vop(cyc, [], lambda P, inc: inc(V.memset(o, c)))
+
+    def scan(cyc, deps, o, a, b):
+        return vop(cyc, deps, lambda P, inc: inc(V.tensor_tensor_scan(o, a, b, 0.0, OP.mult, OP.add)))
+
+    def affine(deps, o, p1, n, scale, bias, job):
+        def fn(e, P, inc):
+            i = P[0:p1, 0:n]
+            if e == "V":
+                inc(V.tensor_scalar(o, i, scale, bias, OP.mult, OP.add) if bias else V.tensor_copy(o, i))
+            else:
+                inc(ACT.activation(o, i, AF.Identity, bias=bias, scale=scale) if bias else ACT.activation(o, i, AF.Copy))
+        return add("VA", max(n, 64), deps, fn, job=job, role="r")
+
+    def mm(cyc, deps, fn, n=1, **kw):
+        j = newjob()
+        return add("P", cyc, deps, lambda e, P, inc: fn(P, inc), job=j, role="w", n=n, **kw), j
+
+    def ldma(q, deps, sem, cnt, nbytes, prs, after=()):
+        d = add(q, 0, deps, lambda e, P, inc: [Q[e].dma_start(o, i).then_inc(T.sem[sem], 16) for o, i in prs],
+                kind="dma", n=len(prs), after=after)
+        return add("", 0, [d], None, kind="larr", info=(sem, cnt, nbytes))
+
+    def iota(n, deps, o, pat, b, cm, small=True):
+        if small:
+            return add("G", 160 + 2 * n, deps, lambda e, P, inc: inc(g.iota(o, pat, b, cm, allow_small_or_imprecise_dtypes=True)))
+        return add("G", 160 + 2 * n, deps, lambda e, P, inc: inc(g.iota(o, pat, b, cm)))
+
+    me = T.cores[rank]
+    base = 1024 * rank
+    peer = lambda d: T.cores[(rank + d) % N]
+    dstid = lambda c: DstId(rid=topo.addr(c)[0], pnc=topo.addr(c)[1])
+
+    l_cand = ldma("S", [], "dc", 16, 768, [(wi("CAND", 0, 192, 0, 1), T.cand[:])])
+
+    def ldpos(q, k, after):
+        c0 = 1024 * ((rank - 1 - k) % N)
+        return ldma(q, [], "dp%d" % k, 32, 262144, [(wi("POS", k * 512, 512, 64 * hf, 64 * hf + 64),
+                    T.pos0[:, c0 + hf * 512:c0 + hf * 512 + 512]) for hf in range(2)], after=after)
+    l_pos = {3: ldpos("A", 3, [])}
+    l_co = ldma("S", [], "dco", 48, 36864, [(wi("CO", 0, 128, 24 * a, 24 * a + 24), t[:, base:base + 1024])
+                                            for a, t in enumerate((T.fac, T.inc, T.th))], after=[l_cand - 1])
+    l_pos[0] = ldpos("A", 0, [l_pos[3] - 1])
+    l_pos[1] = ldpos("S", 1, [l_co - 1])
+    l_pos[2] = ldpos("A", 2, [l_pos[0] - 1])
+    tsp = cfg["tsplit"]
+    l_t0 = ldma("S", [], "dt", 0, 256 * tsp, [(T.tabs[:, 0:tsp], T.tab[:, 0:tsp])], after=[l_pos[2] - 1, l_pos[1] - 1])
+
+    PC = wa(4); TB = wa(1); IR = wa(192); SA = wa(192); SB = wa(192); CW = wa(16); I32 = wa(128); RST = wa(64)
+    c_pi = iota(1, [], wi("PI"), [[0, 1]], 0, 1, False)
+    c_gt = iota(192, [], cb("GT", 0, 192), [[1, 16], [0, 12]], 16 * rank, 0)
+    c_fr = iota(144, [], cb("FR", 0, 144), [[1, 144]], 0, 0)
+    c_z = ms(320, cb("CR", 0, 640, 0, 1), 0.0)
+    c_on = ms(64, cb("ON", 0, 128, 0, 1), 1.0)
+    c_ir = iota(192, [], wf(IR, 192, 1, 1), [[0, 16], [1, 12]], 0, 0)
+    c_cr = iota(192, [c_z], cb("CR", 64, 192, 0, 1), [[16, 8], [4, 2], [0, 12]], 11, 0)
+    c_rst = iota(64, [], wf(RST, 64), [[0, 4], [1, 16]], 0, 0)
+    c_rst = ts(64, [c_rst], wf(RST, 64), wf(RST, 64), 1.0, None, OP.min)
+    p1 = ts(64, [c_pi], wi("PI", 1), wi("PI"), 63, None, OP.bitwise_and)
+    p2 = ts(64, [c_pi], wi("PI", 2), wi("PI"), 15, None, OP.bitwise_and)
+    p3 = ts(64, [c_pi], wi("PI", 3), wi("PI"), 2, 1, OP.logical_shift_right, OP.bitwise_and)
+    c_pc = cp(64, [p1, p2, p3], (wf(PC, 4), wi("PI", 0, 4)))
+    c_tb = ts(64, [c_pc], wf(TB), wf(PC + 3), 4096.0, 2047.5, OP.mult, OP.add)
+    c_nh = ts(96, [c_pc, c_gt], cb("NH", 0, 192), cb("GT", 0, 192), wf(PC + 1), 0.5, OP.is_equal, OP.mult)
+    fr = cb("FR", 0, 128)
+    c_id = ts(64, [c_pc, c_fr], cb("ID", 0, 128), fr, wf(PC), None, OP.is_equal)
+    c_in = ts(64, [c_pc, c_fr], cb("IN", 0, 128), fr, wf(PC), -128.0, OP.is_equal, OP.mult)
+    c_i2 = ts(64, [c_pc, c_fr], T.i2[:, 0:128], fr, wf(PC), 2.0, OP.is_equal, OP.mult)
+    c_i32 = ts(128, [c_pc, c_fr], wf(I32, 128), fr, wf(PC), None, OP.is_equal)
+    c_sel = ts(64, [c_pc, c_fr], cb("SEL", 0, 16), cb("FR", 0, 16), wf(PC + 2), None, OP.is_equal)
+    w1 = ts(192, [c_ir], wf(SA, 192, 1, 1), wf(IR, 192, 1, 1), 0.0, 2.0, OP.not_equal, OP.mult)
+    w2 = ts(192, [c_ir], wf(SB, 192, 1, 1), wf(IR, 192, 1, 1), 0.0, 0.5, OP.is_equal, OP.mult)
+    w3 = scan(192, [w1, w2, c_z], cb("WR", 64, 192, 0, 1), wf(SA, 192, 1, 1), wf(SB, 192, 1, 1))
+    offs = (64, 192, 0, 128)
+    w4, j = mm(512, [c_cr, w3, c_on], lambda P, inc: [inc(PE.matmul(
+        P[:, 2 * v + a:2 * v + a + 1], cb(nm, offs[v], 128, 0, 1), cb("ON", 0, 1, 0, 1), True, True))
+        for v in range(4) for a, nm in enumerate(("CR", "WR"))], n=8)
+    w5 = affine([w4], wf(CW, 8), 128, 8, 1.0, 0.0, j)
+    c_w = [ts(72, [w5, c_fr], cb("W", 144 * v, 144), cb("FR", 0, 144), wf(CW + 2 * v), wf(CW + 2 * v + 1), OP.is_equal, OP.mult)
+           for v in range(4)]
+    w6 = ts(64, [w5, c_pc], wf(CW + 8), wf(PC), 64.0, wf(CW + 7), OP.is_ge, OP.mult)
+    c_w.append(ts(72, [w6, c_fr], cb("W", 576, 144), cb("FR", 0, 144), wf(CW + 6), wf(CW + 8), OP.is_equal, OP.mult))
+
+    s1 = cp(192, [l_cand], (cb("CAND", 0, 192, 0, 1), wi("CAND", 0, 192, 0, 1)))
+    s2, j = mm(192, [s1, c_on], lambda P, inc: inc(PE.matmul(P[:, 0:192], cb("ON", 0, 128, 0, 1), cb("CAND", 0, 192, 0, 1), True, True)))
+    s3 = vop(192, [s2, c_pc], lambda P, inc: inc(V.tensor_scalar(
+        cb("U", 0, 192), P[:, 0:192], wf(PC + 1), 0.5, OP.not_equal, OP.subtract)), job=j, role="r")
+    s_loc = tt(192, [s3, c_nh], T.sall[:, 576:768], cb("U", 0, 192), cb("NH", 0, 192), OP.min)
+
+    def fsend(e, P, inc):
+        g.remote_dma_fused([RemoteDMATransfer(
+            dst_ids=[dstid(peer(-1 - k)) for k in range(3)], dma_engine_mask=topo.mask(me, peer(1)), remote_sem=T.sem["sS"],
+            src=T.sall[:, 576:768], dsts=[T.sall[:, 192 * k:192 * k + 192] for k in range(3)])], local_sem=T.sem["sent"])
+        sent[0] += NE
+    d = add("G", 0, [s_loc], fsend, kind="rem")
+    s_arr = add("", 0, [d], None, kind="rarr", info=("sS", 3 * NE, 384 // NE, 384))
+    l_tab = ldma("S", [s_loc], "dt", 32, 256 * (8192 - tsp), [(T.tabs[:, tsp:8192], T.tab[:, tsp:8192])], after=[l_t0 - 1, d])
+
+    def exchange(w, grp, hf, deps, col, width, mode):
+        arr = {}
+        prev = []
+        so, dn = (T.mo, T.mi) if w == "m" else (T.so, T.si)
+        for call in MODES[mode]:
+            def fn(e, P, inc, call=call):
+                trs = []
+                e0 = 0
+                for k, sh in call:
+                    c = peer(1 + k) if w == "m" else peer(-1 - k)
+                    m = sum(1 << x for x in topo.engines(me, c)[e0:e0 + NE // sh])
+                    e0 += NE // sh
+                    a = col(k)
+                    trs.append((c, m, T.sem["%s%d%d%d" % (w, grp, hf, k)], so[:, a:a + width], dn[:, a:a + width]))
+                sent[0] += e0
+                if len(trs) == 1:
+                    c, m, sm, a, b = trs[0]
+                    g.remote_dma(b, a, sm, T.sem["sent"], topo.addr(c)[1], topo.addr(c)[0], m)
+                else:
+                    g.remote_dma_fused([RemoteDMATransfer(dst_ids=[dstid(c)], dma_engine_mask=m, remote_sem=sm, src=a, dst=b)
+                                        for c, m, sm, a, b in trs], local_sem=T.sem["sent"])
+            d = add("G", 0, [x for k, sh in call for x in deps[k]], fn, kind="rem", after=prev)
+            prev = [d]
+            for k, sh in call:
+                arr[k] = add("", 0, [d], None, kind="rarr",
+                             info=("%s%d%d%d" % (w, grp, hf, k), NE // sh, 128 * sh // NE, width * (2 if w == "m" else 4)))
+        return arr
+
+    cv, ptc = {}, []
+    for k in (3, 0, 1, 2):
+        cv[k] = ts(512, [l_pos[k]], T.pz[:, k * 512:k * 512 + 512], wi("POS", k * 512, 512), 2.0, 2.0, OP.mult, OP.add)
+    qc = lambda q: (q % 2) * 128 + (q // 2) * 64
+    for hf in range(2):
+        a, j = mm(256, [cv[3], c_id], lambda P, inc, hf=hf: [inc(PE.matmul(
+            P[:, qc(q):qc(q) + 64], T.pz[64 * hf:64 * hf + 64, 1536 + q * 128:1536 + q * 128 + 128],
+            cb("ID", 64 * hf, 64, 64 * hf, 64 * hf + 64), True, True)) for q in range(4)], n=4)
+        ptc.append(affine([a], T.pt[:, hf * 256:hf * 256 + 256], 128, 256, 0.5, -33.0, j))
+    k1 = cp(128, [l_co], (cb("CO", 0, 128, 0, 72), wi("CO", 0, 128, 0, 72)))
+    k2, j = mm(72, [k1, c_id], lambda P, inc: inc(PE.matmul(P[:, 0:72], cb("CO", 0, 128, 0, 72), cb("ID", 0, 72, 0, 72), True, True)))
+    CO = wa(72); R = wa(112); AD = wa(32); BI = wa(32); TM = wa(64); M = wa(64)
+    D0 = [wa(32), wa(32)]; D1 = [wa(32), wa(32)]; AB = [wa(32), wa(32)]
+    C1B = wa(16); C0D = wa(16); C1D = wa(16); TP = wa(16); T8 = wa(32)
+    co = affine([k2], wf(CO, 72), 128, 72, 1.0, 0.0, j)
+    zb = ms(64, wf(BI, 32), 0.0)
+    zd = ms(64, wf(D0[0], 64), 0.0)
+    k3 = cp(320, [co, zb], (wf(R, 24, 2), wf(CO, 24)), (wf(R + 1, 24, 2), wf(CO + 24, 24)), (wf(AD, 16, 2), wf(CO + 8, 16)),
+            (wf(AD + 1, 16, 2), wf(CO + 8, 16)), (wf(BI + 1, 16, 2), wf(CO + 32, 16)))
+
+    def comp(deps, i, kk, src):
+        a = tt(64, deps, wf(TM + 16 * (i - 3), 16), wf(AD + 16 * (kk - 1), 16), wf(R + 16 * src, 16), OP.mult)
+        return tt(64, [a], wf(R + 16 * i, 16), wf(TM + 16 * (i - 3), 16), wf(BI + 16 * (kk - 1), 16), OP.add)
+    r3 = comp([k3], 3, 1, 0); r4 = comp([k3], 4, 2, 0); r5 = comp([k3], 5, 2, 1); r6 = comp([r3], 6, 2, 3)
+    m1 = cp(64, [r3, r4, r5, r6], (wi("MOD", 0, 64), wf(R + 48, 64)))
+    m2 = ts(64, [m1], wi("MOD", 0, 64), wi("MOD", 0, 64), 63, None, OP.bitwise_and)
+    m3 = cp(64, [m2], (wf(M, 64), wi("MOD", 0, 64)))
+    e1 = tt(64, [m3, zd], wf(D0[0] + 1, 16, 2), wf(M, 16), wf(R + 16, 16), OP.subtract)
+    e2 = cp(64, [k3], (wf(D1[0] + 1, 16, 2), wf(R + 16, 16)))
+    e3 = tt(64, [m3], wf(C1B, 16), wf(M + 16, 16), wf(R + 32, 16), OP.subtract)
+    e4 = tt(64, [m3], wf(C0D, 16), wf(M + 32, 16), wf(R + 32, 16), OP.subtract)
+    e5 = tt(64, [m3], wf(TP, 16), wf(M + 48, 16), wf(M + 16, 16), OP.subtract)
+    e6 = tt(64, [e5, e4], wf(C1D, 16), wf(TP, 16), wf(C0D, 16), OP.subtract)
+
+    def mcol(o, hf, k):
+        return (hf * 4 + k) * 128 + o * 64 if o < 2 else 512 * o + (hf * 4 + k) * 64
+
+    def positions(o, hf, deps, acol, bcol):
+        ix = ((o - 1) * 2 + hf) * 256
+        a = vop(256, deps + [ptc[hf]], lambda P, inc: [inc(V.tensor_scalar(
+            T.yb[:, ix + qc(q):ix + qc(q) + 64], T.pt[:, hf * 256 + qc(q):hf * 256 + qc(q) + 64], acol(q), bcol(q), OP.mult, OP.add))
+            for q in range(4)], n=4)
+        b = ts(128, [a], T.flb[:, ix:ix + 256], T.yb[:, ix:ix + 256], 1.0 / 64, 192.0078125, OP.mult, OP.add)
+
+        def ftr(P, inc):
+            for c in (0, 128):
+                PE.matmul(P[:, c:c + 128], T.yb[:, ix + c:ix + c + 128], T.i2[:, 0:128], True, False)
+                inc(PE.matmul(P[:, c:c + 128], T.flb[:, ix + c:ix + c + 128], cb("IN", 0, 128), False, True))
+        c, j = mm(512, [b, c_i2, c_in], ftr, n=4)
+        return affine([c], T.pos2[:, o * 512 + hf * 256:o * 512 + hf * 256 + 256], 128, 256, 1.0, 24642.0, j)
+
+    def compare(dep, j, c):
+        def fc(e, P, inc):
+            if e == "V":
+                inc(V.tensor_scalar(T.bits[:, c:c + 512], P[:, 0:512], -1.0, 1.0, OP.max, OP.min))
+            else:
+                inc(ACT.activation(T.bits[:, c:c + 512], P[:, 0:512], AF.Sign))
+        return add("VA", 512, [dep], fc, job=j, role="r")
+
+    def maskmm(j, part, v, c0, deps, after):
+        def fm(e, P, inc):
+            for dl in range(8):
+                y, q = dl // 4, dl % 4
+                c = c0(q) + y
+                i = PE.matmul(P[:, 0:64], cb("W", 144 * v + 11 - (8 * y + q), 128), T.bits[:, c:c + 127:2],
+                              part == 0 and dl == 0, part == 1 and dl == 7)
+            if part:
+                inc(i)
+        return add("P", 512, deps + [c_w[v]], fm, job=j, role="w", n=8, after=after)
+
+    def offsets(dep, j, o, hf, k, away):
+        a = mcol(o, hf, k)
+        return vop(64, [dep, c_tb], lambda P, inc: inc(V.tensor_scalar(
+            (T.mo if away else T.mi)[:, a:a + 64], P[:, 0:64], wf(TB), None, OP.add)), job=j, role="r")
+
+    def masks(o, hf, pdep):
+        pc = o * 512 + hf * 256
+        dmm, cmpo, out = [], [], []
+        bc = lambda tl: ((o * 2 + hf) * 6 + tl) * 512
+        for tl in range(6):
+            a, j = mm(512, [pdep, s_loc, s_arr], lambda P, inc, pr=tl // 2, h=tl % 2: [inc(PE.matmul(
+                P[:, x * 256:x * 256 + 256], T.sall[64 * h:64 * h + 64, pr * 256 + x * 128:pr * 256 + x * 128 + 128],
+                T.pos2[64 * h:64 * h + 64, pc:pc + 256], True, True)) for x in range(2)], n=2, info="D")
+            dmm.append(a)
+            cmpo.append(compare(a, j, bc(tl)))
+        for k in range(4):
+            tl = 3 * (k // 2) + k % 2
+            j = newjob()
+            a = dmm[(tl + 1) // 2 * 2 + 1]
+            for part in range(2):
+                x = tl + part
+                a = maskmm(j, part, 2 * (k % 2) + part, lambda q, x=x: bc(x // 2 * 2 + q // 2) + (x % 2) * 256 + (q % 2) * 128,
+                           cmpo[x // 2 * 2:x // 2 * 2 + 2], [a, dmm[(tl + 1) // 2 * 2]])
+            out.append(offsets(a, j, o, hf, k, k < 3))
+        return out
+
+    def masks0():
+        z = ms(64, cb("SBD", 0, 128), 0.0)
+        z = cp(128, [z, s_loc], *[(cb("SBD", 64 * h, 64, 64 * h, 64 * h + 64), T.sall[64 * h:64 * h + 64, 704:768]) for h in range(2)])
+        out = [[None] * 4, [None] * 4]
+        for k in (3, 0, 1, 2):
+            cur[:] = [0, 0]
+            db, j = mm(512, [cv[k], z], lambda P, inc, k=k: inc(PE.matmul(
+                P[:, 0:512], cb("SBD", 0, 128), T.pz[:, k * 512:k * 512 + 512], True, True)), info="D")
+            cb_ = compare(db, j, (8 + k) * 512)
+            for hf in range(2):
+                cur[:] = [hf, 0]
+                da, j = mm(512, [cv[k], s_loc], lambda P, inc, k=k, hf=hf: inc(PE.matmul(
+                    P[:, 0:512], T.sall[64 * hf:64 * hf + 64, 576:704], T.pz[64 * hf:64 * hf + 64, k * 512:k * 512 + 512], True, True)),
+                    info="D")
+                ca = compare(da, j, (hf * 4 + k) * 512)
+                j = newjob()
+                a = maskmm(j, 0, 0, lambda q, c=(hf * 4 + k) * 512: c + q * 128, [ca], [db])
+                a = maskmm(j, 1, 4 if hf else 1, lambda q, c=(8 + k) * 512: c + q * 128, [cb_], [a])
+                out[hf][k] = offsets(a, j, 0, hf, k, False)
+        return out
+
+    def lookup(o, hf, k, dep):
+        a = mcol(o, hf, k)
+        gc0 = ((o * 2 + hf) * 4 + k) * 1024
+
+        def fg(e, P, inc):
+            src = T.tabs[:, 0:8192].indirect(T.mi[:, a:a + 64])
+            if e == "V":
+                inc(V.tensor_copy(T.gat[:, gc0:gc0 + 1024], src))
+            else:
+                inc(ACT.activation(T.gat[:, gc0:gc0 + 1024], src, AF.Copy))
+        ga = add("VA", 1024, [dep, l_tab], fg, kind="gat")
+
+        def fr_(P, inc):
+            for q in range(4):
+                for t in range(2):
+                    c = gc0 + t * 4 + q
+                    i = PE.matmul(P[:, q * 16:q * 16 + 16], T.gat[:, c:c + 1017:8], cb("SEL", 0, 16), t == 0, t == 1)
+                inc(i)
+        return mm(512, [ga, c_sel], fr_, n=8)
+
+    mk0 = masks0()
+    for hf in range(2):
+        OUT = wa(80); FP = wa(64); TPm = wa(64)
+        cur[:] = [hf, 1]
+        mk = masks(1, hf, positions(1, hf, [co], lambda q, hf=hf: wf(CO + 4 * hf + q), lambda q, hf=hf: wf(CO + 24 + 4 * hf + q)))
+        Fc = fdep = None
+        selprep = [e1, e2]
+        flags = []
+        for r in range(3):
+            os_ = (0, 1) if r == 0 else (r + 1,)
+            wd = 64 * len(os_)
+            th = wf(CO + 48 + 8 * r + 4 * hf, 4)
+            col = lambda k, o=os_[0], hf=hf: mcol(o, hf, k)
+            arr = exchange("m", r, hf, [[mk[k]] for k in range(3)], lambda k, r=r, hf=hf: mcol(r + 1, hf, k), 64, cfg["mm"])
+            cps = [[], [], [], []]
+            NN = wa(384 if r == 0 else 192); DF = wa(64); CM = wa(64); CN = wa(64); TQ = wa(64); FN = wa(64)
+            for k in range(4):
+                for o in os_:
+                    red, j = lookup(o, hf, k, mk0[hf][k] if o == 0 else arr[k] if k < 3 else mk[3])
+                    a = mcol(o, hf, k)
+                    if k == 3 and r > 0:
+                        cps[k].append(vop(64, [red, fdep], lambda P, inc, NN=NN, Fc=Fc: inc(V.tensor_tensor(
+                            wf(NN, 64), wf(Fc, 64), P[:, 0:64], OP.subtract)), job=j, role="r"))
+                    else:
+                        cps[k].append(affine([red], (T.so if k < 3 else T.si)[:, a:a + 64], 128, 64, 1.0, 0.0, j))
+            sar = exchange("s", r, hf, cps, col, wd, cfg["sm"])
+            sic = [T.si[:, col(k):col(k) + wd] for k in range(4)]
+            if r == 0:
+                a = tt(256, cps[3] + [sar[0]], wf(NN, 128), sic[3], sic[0], OP.add)
+                a = tt(256, [a, sar[1]], wf(NN + 128, 128), wf(NN, 128), sic[1], OP.add)
+                fdep = tt(256, [a, sar[2]], wf(NN + 256, 128), wf(NN + 128, 128), sic[2], OP.add)
+                Fc = NN + 256
+                x0, x1, dd = wf(Fc + 64, 64), wf(Fc, 64), [fdep]
+            else:
+                a = tt(128, cps[3] + [sar[0]], wf(NN + 64, 64), wf(NN, 64), sic[0], OP.subtract)
+                a = tt(128, [a, sar[1]], wf(NN + 128, 64), wf(NN + 64, 64), sic[1], OP.subtract)
+                x0, x1, dd = sic[2], wf(NN + 128, 64), [a, sar[2]]
+            cm = tt(128, dd, wf(CM, 64), x0, x1, OP.is_ge)
+            df = tt(128, dd, wf(DF, 64), x0, x1, OP.subtract)
+            cn = scan(64, [cm, c_rst], wf(CN, 64), wf(RST, 64), wf(CM, 64))
+            cnt = wf(CN + 15, 4, 16)
+            fl = tt(64, [cn, co], wf(OUT + 64 + 4 * r, 4), cnt, th, OP.is_ge)
+            flags.append(fl)
+            if r < 2:
+                d1 = D1[r] + 16 * hf
+                ab = AB[r] + 16 * hf
+                ac = vop(128, [cn, co], lambda P, inc, d1=d1, cnt=cnt, th=th: [inc(V.tensor_tensor(
+                    wf(d1 + x, 4, 4), cnt, th, OP.is_ge)) for x in (0, 2)], n=2)
+                sl = scan(64, [ac] + selprep, wf(ab, 16), wf(D0[r] + 16 * hf, 16), wf(d1, 16))
+                mk = masks(r + 2, hf, positions(r + 2, hf, [sl], lambda q, ab=ab: wf(ab + 4 * q + 1), lambda q, ab=ab: wf(ab + 4 * q + 3)))
+                tq = vop(256, [ac, df], lambda P, inc, TQ=TQ, DF=DF, d1=d1: [inc(V.tensor_scalar(
+                    wf(TQ + 16 * q, 16), wf(DF + 16 * q, 16), wf(d1 + 4 * q), None, OP.mult)) for q in range(4)], n=4)
+                fdep = tt(128, [tq, fdep], wf(FN, 64), wf(Fc, 64), wf(TQ, 64), OP.add)
+                Fc = FN
+                if r == 0:
+                    t8 = T8 + 16 * hf
+                    a1 = tt(64, [ac, e3], wf(t8, 8), wf(d1, 8, 2), wf(C1B + 8 * hf, 8), OP.mult)
+                    a2 = tt(64, [ac, e6], wf(t8 + 8, 8), wf(d1, 8, 2), wf(C1D + 8 * hf, 8), OP.mult)
+                    selprep = [tt(64, [a1], wf(D1[1] + 16 * hf + 1, 8, 2), wf(t8, 8), wf(R + 32 + 8 * hf, 8), OP.add),
+                               tt(64, [a2, zd], wf(D0[1] + 16 * hf + 1, 8, 2), wf(t8 + 8, 8), wf(C0D + 8 * hf, 8), OP.add)]
+                else:
+                    fp = cp(256, [fdep], *[(wf(FP + q, 16, 4), wf(Fc + 16 * q, 16)) for q in range(4)])
+            else:
+                tq = vop(256, [fl, df], lambda P, inc, TPm=TPm, DF=DF, OUT=OUT: [inc(V.tensor_scalar(
+                    wf(TPm + q, 16, 4), wf(DF + 16 * q, 16), wf(OUT + 72 + q), None, OP.mult)) for q in range(4)], n=4)
+                fo = tt(128, [tq, fp], wf(OUT, 64), wf(FP, 64), wf(TPm, 64), OP.add)
+                a, j = mm(512, [fo, c_i32] + flags, lambda P, inc, OUT=OUT: inc(PE.transpose(P[0:76, 0:128], wf(OUT, 76), wf(I32, 128))))
+                a = affine([a], T.ob[0:76, hf * 128:hf * 128 + 128], 76, 128, 1.0, 0.0, j)
+                ldma("S", [a], "do", 0, 32768, [(T.yf[:, hf * 512:hf * 512 + 512], T.ob[0:64, hf * 128:hf * 128 + 128])])
+                ldma("A" if hf else "S", [a], "do", 0, 6144, [(T.ya[:, hf * 512:hf * 512 + 512], T.ob[64:76, hf * 128:hf * 128 + 128])])
+    assert top[0] <= 7424
+    return ops, Q, sent
+
+
+def dur(op, e, p):
+    k = op["kind"]
+    if k == "dma":
+        return 0.1 * op["n"]
+    if k == "rem":
+        return p["iss"]
+    if e == "P":
+        return op["cyc"] * p["pc"] * 1e-3 + p["pf"] * op["n"]
+    c = op["cyc"] * (p["gr"] if k == "gat" else 1.0)
+    return c * 0.83e-3 * p["f"] + op["n"] * (p["fixa"] if e == "A" else p["fix"])
+
+
+def place(op, e, t0, p, st):
+    k = op["kind"]
+    if k == "larr":
+        st["dma"] = max(t0 + p["ldst"], st["dma"]) + op["info"][2] / p["lbw"]
+        return st["dma"]
+    if k == "rarr":
+        if st["rsrc"] != op["deps"][0]:
+            st["rs"] = max(t0 + p["st"] + (p["first"] if st["rsrc"] is None else 0.0), st["dma"])
+            st["rsrc"] = op["deps"][0]
+        f = st["rs"] + op["info"][2] * (p["row"] + op["info"][3] / p["bw"])
+        st["dma"] = max(st["dma"], f)
+        return f + p["wake"]
+    return t0 + dur(op, e, p)
+
+
+def schedule(ops, cfg, p):
+    n = len(ops)
+    succ = [[] for _ in range(n)]
+    for o in ops:
+        for d in o["deps"] + o["after"]:
+            succ[d].append(o["id"])
+    lev = [0.0] * n
+    for o in reversed(ops):
+        if o["kind"] == "rarr":
+            c = p["st"] + o["info"][2] * p["row"] + p["wake"]
+        elif o["kind"] == "larr":
+            c = p["ldst"] + o["info"][2] / p["lbw"]
+        else:
+            c = dur(o, o["eng"][0], p) + p["sem"]
+        lev[o["id"]] = c + max([lev[s] for s in succ[o["id"]]] + [0.0])
+    pri = [lev[i] + cfg["ba"] * (o["tag"][0] != 1) + cfg["bo"] * (o["tag"][1] != 1) + cfg["bd"] * (o["info"] == "D")
+           for i, o in enumerate(ops)]
+    fin = [None] * n
+    free = dict(P=0.0, V=0.0, A=0.0, G=0.0, S=0.0)
+    st = dict(dma=0.0, rsrc=None, rs=0.0)
+    bank_job, bank_rd, isd = [None] * 8, [None] * 8, [False] * 8
+    jb = {}
+    left = [len(o["deps"]) + len(o["after"]) for o in ops]
+    ready = [o["id"] for o in ops if left[o["id"]] == 0]
+    plan = []
+
+    def done(i):
+        for s in succ[i]:
+            left[s] -= 1
+            if left[s] == 0:
+                if ops[s]["eng"] == "":
+                    fin[s] = place(ops[s], "", fin[i], p, st)
+                    plan.append((s, "", None, None))
+                    done(s)
+                else:
+                    ready.append(s)
+    while ready:
+        cand = []
+        for i in ready:
+            o = ops[i]
+            t = max([fin[d] + p["sem"] for d in o["deps"]] + [0.0])
+            bk = None
+            if o["role"] == "w" and o["job"] not in jb:
+                fr = [b for b in range(8) if bank_job[b] is None]
+                if not fr or (o["info"] == "D" and sum(isd[b] for b in range(8) if bank_job[b] is not None) >= cfg["maxd"]):
+                    continue
+                bk = min(fr, key=lambda b: -1.0 if bank_rd[b] is None else fin[bank_rd[b]])
+                if bank_rd[bk] is not None:
+                    t = max(t, fin[bank_rd[bk]] + p["sem"])
+            e = min(o["eng"], key=lambda x: (max(t, free[x]), x == "V"))
+            cand.append((max(t, free[e]), i, e, bk))
+        t0, _, e0, _b = min(cand)
+        t, i, e, bk = max([c for c in cand if c[0] <= t0 + cfg["slack"] and c[2] == e0], key=lambda c: pri[c[1]])
+        o = ops[i]
+        war = None
+        if bk is not None:
+            jb[o["job"]] = bk
+            bank_job[bk] = o["job"]
+            isd[bk] = o["info"] == "D"
+            war = bank_rd[bk]
+        if o["role"] == "r":
+            bank_job[jb[o["job"]]] = None
+            bank_rd[jb[o["job"]]] = i
+        fin[i] = place(o, e, t, p, st)
+        free[e] = fin[i]
+        plan.append((i, e, jb.get(o["job"]), war))
+        ready.remove(i)
+        done(i)
+    assert len(plan) == n
+    return plan, max(fin)
+
+
+def rank_program(g, core, T, topo):
+    rank = T.rank_of(core)
+    if rank is None:
+        return
+    ops, Q, sent = build(g, T, rank, topo, CFG, len(topo.engines(core, T.cores[(rank + 1) % N])))
+    cnt = dict(P=0, V=0, A=0, G=0)
+    know = {e: {} for e in Q}
+    tag, clock = {}, {}
+    for i, e, bank, war in schedule(ops, CFG, NOM)[0]:
+        o = ops[i]
+        if e == "":
+            tag[i] = (o["info"][0], o["info"][1])
+            clock[i] = dict(clock[o["deps"][0]]) if o["kind"] == "larr" else {}
+            continue
+        kn = know[e]
+        need = {}
+        for d in o["deps"] + ([war] if war is not None else []):
+            s, c = tag[d]
+            if need.get(s, (0, 0))[0] < c:
+                need[s] = (c, d)
+        for s, (c, d) in sorted(need.items(), key=lambda x: -x[1][1]):
+            if kn.get(s, 0) < c:
+                Q[e].wait_ge(T.sem[s], c)
+                kn[s] = c
+                for s2, c2 in clock[d].items():
+                    kn[s2] = max(kn.get(s2, 0), c2)
+
+        def inc(ins, e=e):
+            ins.then_inc(T.sem["e" + e], 1)
+            cnt[e] += 1
+        o["fn"](e, T["ps%d" % bank] if bank is not None else None, inc)
+        clock[i] = dict(kn)
+        if o["kind"] in ("c", "gat"):
+            tag[i] = ("e" + e, cnt[e])
+    for e in "PVAG":
+        g.sync.wait_ge(T.sem["e" + e], cnt[e])
+    g.sync.wait_ge(T.sem["sent"], sent[0])
+    g.sync.wait_ge(T.sem["do"], 64)

@@ -1,38 +1,51 @@
+import math
+import numpy as np
 from concourse.bass import DstId, RemoteDMATransfer
 from concourse.mybir import AluOpType as OP, ActivationFunctionType as AF
 
 N = 4
-CB = dict(FR=0, GT=144, CR=336, WR=656, ON=976, NH=1104, ID=1296, IN=1424, SEL=1552, U=1568, W=1760, CAND=2480, CO=2672, SBD=2800)
-WI = dict(PI=0, MOD=16, CAND=96, CO=288, POS=416)
+CB = dict(FR=0, F63=192, ID=384, NI=512, SEL=640, NSEL=672, ON=704, NR=832, IR=976, WR=1120, VR=1264, SA=1408, SB=1552,
+          CR=1696, CO=1840, LA=1968, X=2096, SALL=2320, PR=2704)
+CH = dict(ID=0, NI=128, W0=256, W1=288, W2=352, WB=384, NW=416, V1=448, V2=624, H=800)
+WI = dict(PI=0, CAND=8, MOD=24, CO=96, POS=224)
 SCRATCH = {
     "tabs": ("sbuf", [128, 8192], "bfloat16"),
-    "cb": ("sbuf", [128, 2928], "bfloat16"),
-    "wi": ("sbuf", [128, 2464], "int32"),
-    "wf": ("sbuf", [128, 7424], "float32"),
-    "i2": ("sbuf", [128, 128], "float16"),
-    "yb": ("sbuf", [128, 1536], "float16"),
-    "flb": ("sbuf", [128, 1536], "bfloat16"),
-    "pos2": ("sbuf", [128, 2048], "bfloat16"),
+    "cb": ("sbuf", [128, 2736], "bfloat16"),
+    "ch": ("sbuf", [128, 1824], "float16"),
+    "wi": ("sbuf", [128, 2272], "int32"),
+    "wf": ("sbuf", [128, 4096], "float32"),
+    "d1": ("sbuf", [128, 864], "float32"),
+    "tq": ("sbuf", [128, 704], "float32"),
+    "fl": ("sbuf", [128, 1536], "bfloat16"),
+    "dg": ("sbuf", [128, 3072], "bfloat16"),
+    "pos2": ("sbuf", [128, 1536], "bfloat16"),
     "pz": ("sbuf", [128, 2048], "bfloat16"),
     "pt": ("sbuf", [128, 512], "bfloat16"),
-    "sall": ("sbuf", [128, 768], "bfloat16"),
-    "bits": ("sbuf", [128, 48 * 512], "bfloat16"),
+    "zz": ("sbuf", [128, 8 * 1536], "float16"),
+    "bb": ("sbuf", [128, 8 * 1536], "float16"),
+    "zi": ("sbuf", [128, 3 * 264], "float16"),
     "gat": ("sbuf", [128, 32 * 1024], "bfloat16"),
-    "mo": ("sbuf", [128, 2048], "uint16"),
-    "mi": ("sbuf", [128, 2048], "uint16"),
-    "so": ("sbuf", [128, 2048], "float32"),
-    "si": ("sbuf", [128, 2048], "float32"),
-    "ob": ("sbuf", [128, 256], "float32"),
+    "mk": ("sbuf", [128, 3200], "uint16"),
+    "dup": ("sbuf", [128, 1152], "uint16"),
+    "of": ("sbuf", [128, 8], "uint16"),
+    "so": ("sbuf", [128, 1728], "float16"),
+    "si": ("sbuf", [128, 1728], "float16"),
+    "ob": ("sbuf", [128, 512], "float32"),
 }
 for _b in range(8):
     SCRATCH["ps%d" % _b] = ("psum", [128, 512], "float32")
-SEMAPHORES = (["eP", "eV", "eA", "eG", "sent", "dc", "dp0", "dp1", "dp2", "dp3", "dco", "dt", "do", "sS"]
+SEMAPHORES = (["eP", "eV", "eA", "eG", "sent", "dc", "dp0", "dp1", "dp2", "dp3", "dco", "dt", "do", "sS", "dup"]
               + ["%s%d%d%d" % (w, a, h, k) for w in "ms" for a in range(3) for h in range(2) for k in range(3)])
 
-MODES = {"per": [[(0, 1)], [(1, 1)], [(2, 1)]], "two": [[(0, 2), (1, 2)], [(2, 1)]], "one": [[(0, 4), (1, 4), (2, 2)]]}
-CFG = dict(mm="per", sm="per", tsplit=4096, slack=0.15, maxd=3, ba=3.5, bo=5.0, bd=1.0)
-NOM = dict(f=1.25, gr=1.56, pc=0.5, pf=0.02, fix=0.03, fixa=0.06, sem=0.1, iss=0.5, st=1.5, row=0.04, bw=15e3, wake=0.3,
-           first=2.0, ldst=1.6, lbw=300e3)
+CFG = dict(tsplit=1024, slack=0.05, maxd=3, ba=1.0, bo=-2.0, bd=0.0, gs=(1, 1, 2, 2), vb=0.3, tw=1, late=(), bg=6.0, bc=1.0,
+           look=0.35, alpha=0.0, tc=False, seed=1, iters=12000, heat=0.001,
+           mean=1.0, focus=0.7, dup=False)
+NOM = dict(f=1.05, gr=1.5, pc=0.44, pf=0.003, fix=0.052, fixa=0.068, sem=0.1, iss=0.1, st=0.9, row=0.015, bw=12e3, wake=0.3,
+           first=2.8, ldst=1.5, lbw=300e3)
+VARY = [dict(), dict(f=1.0, gr=1.2, st=1.3, iss=0.2), dict(f=1.3, gr=1.9, st=0.6, lbw=400e3, first=1.8, fix=0.065, fixa=0.085),
+        dict(f=1.3, gr=1.3, st=1.4, wake=0.5, first=4.0, lbw=230e3, sem=0.14, fix=0.065, fixa=0.085)]
+LIMIT = dict(L=2, M=2, S=8)
+KEPT = {}
 
 
 def build(g, T, rank, topo, cfg, NE):
@@ -42,9 +55,9 @@ def build(g, T, rank, topo, cfg, NE):
     V, PE, ACT = g.vector, g.tensor, g.scalar
     top, jobs, sent = [0], [0], [0]
 
-    def add(eng, cyc, deps, fn, job=None, role=None, kind="c", n=1, after=(), info=None):
-        ops.append(dict(id=len(ops), eng=eng, cyc=cyc, deps=[d for d in deps if d is not None], fn=fn, job=job,
-                        role=role, kind=kind, n=n, after=list(after), info=info, tag=tuple(cur)))
+    def add(eng, cyc, deps, fn, job=None, cls="S", zj=None, kind="c", n=1, after=(), info=None, cya=None):
+        ops.append(dict(id=len(ops), eng=eng, cyc=cyc, cya=cyc if cya is None else cya, deps=[d for d in deps if d is not None],
+                        fn=fn, job=job, cls=cls, zj=zj, kind=kind, n=n, after=list(after), info=info, tag=tuple(cur)))
         return len(ops) - 1
 
     def wa(n):
@@ -55,375 +68,402 @@ def build(g, T, rank, topo, cfg, NE):
         jobs[0] += 1
         return jobs[0]
 
-    def cb(name, a=0, n=1, p0=0, p1=128):
-        return T.cb[p0:p1, CB[name] + a:CB[name] + a + n]
+    def cols(t, a, n, step=1, p0=0, p1=128):
+        return t[p0:p1, a:a + (n - 1) * step + 1:step] if step > 1 else t[p0:p1, a:a + n]
 
-    def wf(a, n=1, step=1, p1=128):
-        return T.wf[0:p1, a:a + (n - 1) * step + 1:step] if step > 1 else T.wf[0:p1, a:a + n]
+    cb = lambda name, a=0, n=1, p0=0, p1=128: cols(T.cb, CB[name] + a, n, 1, p0, p1)
+    ch = lambda name, a=0, n=1, p0=0, p1=128: cols(T.ch, CH[name] + a, n, 1, p0, p1)
+    wi = lambda name, a=0, n=1, p0=0, p1=128: cols(T.wi, WI[name] + a, n, 1, p0, p1)
+    wf = lambda a, n=1, step=1, p1=128: cols(T.wf, a, n, step, 0, p1)
 
-    def wi(name, a=0, n=1, p0=0, p1=128):
-        return T.wi[p0:p1, WI[name] + a:WI[name] + a + n]
+    def vop(cyc, deps, fn, **kw):
+        return add("V", max(cyc, 64), deps, lambda e, P, inc, Z: inc(fn(P)), **kw)
 
-    def vop(cyc, deps, fn, n=1, **kw):
-        return add("V", cyc, deps, lambda e, P, inc: fn(P, inc), n=n, **kw)
+    ts = lambda cyc, deps, *a: vop(cyc, deps, lambda P: V.tensor_scalar(*a))
+    tt = lambda cyc, deps, *a: vop(cyc, deps, lambda P: V.tensor_tensor(*a))
+    cp = lambda cyc, deps, o, i: vop(cyc, deps, lambda P: V.tensor_copy(o, i))
+    ms = lambda cyc, o, c, deps=(): vop(cyc, list(deps), lambda P: V.memset(o, c))
 
-    def ts(cyc, deps, *a):
-        return vop(cyc, deps, lambda P, inc: inc(V.tensor_scalar(*a)))
-
-    def tt(cyc, deps, *a):
-        return vop(cyc, deps, lambda P, inc: inc(V.tensor_tensor(*a)))
-
-    def cp(cyc, deps, *prs):
-        return vop(cyc, deps, lambda P, inc: [inc(V.tensor_copy(o, i)) for o, i in prs], n=len(prs))
-
-    def ms(cyc, o, c):
-        return vop(cyc, [], lambda P, inc: inc(V.memset(o, c)))
-
-    def scan(cyc, deps, o, a, b):
-        return vop(cyc, deps, lambda P, inc: inc(V.tensor_tensor_scan(o, a, b, 0.0, OP.mult, OP.add)))
-
-    def affine(deps, o, p1, n, scale, bias, job):
-        def fn(e, P, inc):
-            i = P[0:p1, 0:n]
+    def aff(n, deps, o, i, scale, bias, eng="VA", cyv=None, **kw):
+        def fn(e, P, inc, Z):
+            x = i(P) if "job" in kw else i
+            y = o(Z) if "zj" in kw else o
             if e == "V":
-                inc(V.tensor_scalar(o, i, scale, bias, OP.mult, OP.add) if bias else V.tensor_copy(o, i))
+                inc(V.tensor_scalar(y, x, scale, bias, OP.mult, OP.add))
             else:
-                inc(ACT.activation(o, i, AF.Identity, bias=bias, scale=scale) if bias else ACT.activation(o, i, AF.Copy))
-        return add("VA", max(n, 64), deps, fn, job=job, role="r")
+                inc(ACT.activation(y, x, AF.Identity, bias=bias, scale=scale))
+        return add(eng, max(cyv or n, 64), deps, fn, cya=n, **kw)
 
-    def mm(cyc, deps, fn, n=1, **kw):
-        j = newjob()
-        return add("P", cyc, deps, lambda e, P, inc: fn(P, inc), job=j, role="w", n=n, **kw), j
+    def mm(deps, lst, job=None, f32=0, **kw):
+        j = job or newjob()
+
+        def fn(e, P, inc, Z):
+            for a in lst(P, Z):
+                i = PE.matmul(*a)
+            inc(i)
+        l = lst(T.ps0, 0)
+        return add("P", sum(max(64, a[2].shape[1]) for a in l) + 3 * f32, deps, fn, job=j, n=len(l), **kw), j
+
+    def group(l):
+        return [(o, a, b, x == 0, x == len(l) - 1) for x, (o, a, b) in enumerate(l)]
 
     def ldma(q, deps, sem, cnt, nbytes, prs, after=()):
-        d = add(q, 0, deps, lambda e, P, inc: [Q[e].dma_start(o, i).then_inc(T.sem[sem], 16) for o, i in prs],
+        d = add(q, 0, deps, lambda e, P, inc, Z: [Q[e].dma_start(o, i).then_inc(T.sem[sem], 16) for o, i in prs],
                 kind="dma", n=len(prs), after=after)
         return add("", 0, [d], None, kind="larr", info=(sem, cnt, nbytes))
 
-    def iota(n, deps, o, pat, b, cm, small=True):
-        if small:
-            return add("G", 160 + 2 * n, deps, lambda e, P, inc: inc(g.iota(o, pat, b, cm, allow_small_or_imprecise_dtypes=True)))
-        return add("G", 160 + 2 * n, deps, lambda e, P, inc: inc(g.iota(o, pat, b, cm)))
+    def iota(n, deps, o, pat, b, cm, after=()):
+        return add("G", 160 + 2 * n, deps, lambda e, P, inc, Z: inc(g.iota(o, pat, b, cm, allow_small_or_imprecise_dtypes=True)),
+                   after=after)
 
     me = T.cores[rank]
     base = 1024 * rank
     peer = lambda d: T.cores[(rank + d) % N]
     dstid = lambda c: DstId(rid=topo.addr(c)[0], pnc=topo.addr(c)[1])
 
-    l_cand = ldma("S", [], "dc", 16, 768, [(wi("CAND", 0, 192, 0, 1), T.cand[:])])
+    for a in range(2):
+        l_cand = ldma("AS"[a], [], "dc", 64, 60000, [(wi("CAND", 8 + a, 1, 48 * t, 48 * t + 48), T.cand[:, 12 * t + 6 * a:12 * t + 6 * a + 6])
+                                                     for t in range(2)], after=[0] if a else [])
 
     def ldpos(q, k, after):
         c0 = 1024 * ((rank - 1 - k) % N)
         return ldma(q, [], "dp%d" % k, 32, 262144, [(wi("POS", k * 512, 512, 64 * hf, 64 * hf + 64),
                     T.pos0[:, c0 + hf * 512:c0 + hf * 512 + 512]) for hf in range(2)], after=after)
-    l_pos = {3: ldpos("A", 3, [])}
+    l_pos = {3: ldpos("A", 3, [l_cand - 1])}
     l_co = ldma("S", [], "dco", 48, 36864, [(wi("CO", 0, 128, 24 * a, 24 * a + 24), t[:, base:base + 1024])
                                             for a, t in enumerate((T.fac, T.inc, T.th))], after=[l_cand - 1])
-    l_pos[0] = ldpos("A", 0, [l_pos[3] - 1])
-    l_pos[1] = ldpos("S", 1, [l_co - 1])
-    l_pos[2] = ldpos("A", 2, [l_pos[0] - 1])
+    last = [l_co - 1, l_pos[3] - 1]
+    for k in range(3):
+        if k not in cfg["late"]:
+            l_pos[k] = ldpos("AS"[k % 2], k, last)
+            last = last + [l_pos[k] - 1]
     tsp = cfg["tsplit"]
-    l_t0 = ldma("S", [], "dt", 0, 256 * tsp, [(T.tabs[:, 0:tsp], T.tab[:, 0:tsp])], after=[l_pos[2] - 1, l_pos[1] - 1])
+    l_t0 = ldma("S", [], "dt", 0, 256 * tsp, [(T.tabs[:, 0:tsp], T.tab[:, 0:tsp])], after=last)
 
-    PC = wa(4); TB = wa(1); IR = wa(192); SA = wa(192); SB = wa(192); CW = wa(16); I32 = wa(128); RST = wa(64)
-    c_pi = iota(1, [], wi("PI"), [[0, 1]], 0, 1, False)
-    c_gt = iota(192, [], cb("GT", 0, 192), [[1, 16], [0, 12]], 16 * rank, 0)
-    c_fr = iota(144, [], cb("FR", 0, 144), [[1, 144]], 0, 0)
-    c_z = ms(320, cb("CR", 0, 640, 0, 1), 0.0)
-    c_on = ms(64, cb("ON", 0, 128, 0, 1), 1.0)
-    c_ir = iota(192, [], wf(IR, 192, 1, 1), [[0, 16], [1, 12]], 0, 0)
-    c_cr = iota(192, [c_z], cb("CR", 64, 192, 0, 1), [[16, 8], [4, 2], [0, 12]], 11, 0)
-    c_rst = iota(64, [], wf(RST, 64), [[0, 4], [1, 16]], 0, 0)
-    c_rst = ts(64, [c_rst], wf(RST, 64), wf(RST, 64), 1.0, None, OP.min)
-    p1 = ts(64, [c_pi], wi("PI", 1), wi("PI"), 63, None, OP.bitwise_and)
-    p2 = ts(64, [c_pi], wi("PI", 2), wi("PI"), 15, None, OP.bitwise_and)
-    p3 = ts(64, [c_pi], wi("PI", 3), wi("PI"), 2, 1, OP.logical_shift_right, OP.bitwise_and)
-    c_pc = cp(64, [p1, p2, p3], (wf(PC, 4), wi("PI", 0, 4)))
-    c_tb = ts(64, [c_pc], wf(TB), wf(PC + 3), 4096.0, 2047.5, OP.mult, OP.add)
-    c_nh = ts(96, [c_pc, c_gt], cb("NH", 0, 192), cb("GT", 0, 192), wf(PC + 1), 0.5, OP.is_equal, OP.mult)
-    fr = cb("FR", 0, 128)
-    c_id = ts(64, [c_pc, c_fr], cb("ID", 0, 128), fr, wf(PC), None, OP.is_equal)
-    c_in = ts(64, [c_pc, c_fr], cb("IN", 0, 128), fr, wf(PC), -128.0, OP.is_equal, OP.mult)
-    c_i2 = ts(64, [c_pc, c_fr], T.i2[:, 0:128], fr, wf(PC), 2.0, OP.is_equal, OP.mult)
-    c_i32 = ts(128, [c_pc, c_fr], wf(I32, 128), fr, wf(PC), None, OP.is_equal)
-    c_sel = ts(64, [c_pc, c_fr], cb("SEL", 0, 16), cb("FR", 0, 16), wf(PC + 2), None, OP.is_equal)
-    w1 = ts(192, [c_ir], wf(SA, 192, 1, 1), wf(IR, 192, 1, 1), 0.0, 2.0, OP.not_equal, OP.mult)
-    w2 = ts(192, [c_ir], wf(SB, 192, 1, 1), wf(IR, 192, 1, 1), 0.0, 0.5, OP.is_equal, OP.mult)
-    w3 = scan(192, [w1, w2, c_z], cb("WR", 64, 192, 0, 1), wf(SA, 192, 1, 1), wf(SB, 192, 1, 1))
-    offs = (64, 192, 0, 128)
-    w4, j = mm(512, [c_cr, w3, c_on], lambda P, inc: [inc(PE.matmul(
-        P[:, 2 * v + a:2 * v + a + 1], cb(nm, offs[v], 128, 0, 1), cb("ON", 0, 1, 0, 1), True, True))
-        for v in range(4) for a, nm in enumerate(("CR", "WR"))], n=8)
-    w5 = affine([w4], wf(CW, 8), 128, 8, 1.0, 0.0, j)
-    c_w = [ts(72, [w5, c_fr], cb("W", 144 * v, 144), cb("FR", 0, 144), wf(CW + 2 * v), wf(CW + 2 * v + 1), OP.is_equal, OP.mult)
-           for v in range(4)]
-    w6 = ts(64, [w5, c_pc], wf(CW + 8), wf(PC), 64.0, wf(CW + 7), OP.is_ge, OP.mult)
-    c_w.append(ts(72, [w6, c_fr], cb("W", 576, 144), cb("FR", 0, 144), wf(CW + 6), wf(CW + 8), OP.is_equal, OP.mult))
+    c_c0 = ms(64, wi("CAND", 8, 2, 96, 128), 0)
 
-    s1 = cp(192, [l_cand], (cb("CAND", 0, 192, 0, 1), wi("CAND", 0, 192, 0, 1)))
-    s2, j = mm(192, [s1, c_on], lambda P, inc: inc(PE.matmul(P[:, 0:192], cb("ON", 0, 128, 0, 1), cb("CAND", 0, 192, 0, 1), True, True)))
-    s3 = vop(192, [s2, c_pc], lambda P, inc: inc(V.tensor_scalar(
-        cb("U", 0, 192), P[:, 0:192], wf(PC + 1), 0.5, OP.not_equal, OP.subtract)), job=j, role="r")
-    s_loc = tt(192, [s3, c_nh], T.sall[:, 576:768], cb("U", 0, 192), cb("NH", 0, 192), OP.min)
-
-    def fsend(e, P, inc):
+    def fsend(e, P, inc, Z):
         g.remote_dma_fused([RemoteDMATransfer(
             dst_ids=[dstid(peer(-1 - k)) for k in range(3)], dma_engine_mask=topo.mask(me, peer(1)), remote_sem=T.sem["sS"],
-            src=T.sall[:, 576:768], dsts=[T.sall[:, 192 * k:192 * k + 192] for k in range(3)])], local_sem=T.sem["sent"])
+            src=wi("CAND", 8, 2), dsts=[wi("CAND", 2 * k, 2) for k in range(3)])], local_sem=T.sem["sent"])
         sent[0] += NE
-    d = add("G", 0, [s_loc], fsend, kind="rem")
-    s_arr = add("", 0, [d], None, kind="rarr", info=("sS", 3 * NE, 384 // NE, 384))
-    l_tab = ldma("S", [s_loc], "dt", 32, 256 * (8192 - tsp), [(T.tabs[:, tsp:8192], T.tab[:, tsp:8192])], after=[l_t0 - 1, d])
+    d = add("G", 0, [l_cand, c_c0], fsend, kind="rem")
+    s_arr = add("", 0, [d], None, kind="rarr", info=("sS", 3 * NE, 384 // NE, 8))
+    conv = lambda k: cp(512, [l_pos[k]], T.pz[:, k * 512:k * 512 + 512], wi("POS", k * 512, 512))
+    cv = {k: conv(k) for k in (3, 0, 1, 2) if k in l_pos}
+    l_tab = ldma("S", [(cv if cfg["tc"] else l_pos)[cfg["tw"]]], "dt", 32, 256 * (8192 - tsp), [(T.tabs[:, tsp:8192], T.tab[:, tsp:8192])], after=[l_t0 - 1, d])
+    last = [l_tab - 1]
+    for k in cfg["late"]:
+        l_pos[k] = ldpos("S", k, last)
+        last = [l_pos[k] - 1]
+        cv[k] = conv(k)
 
-    def exchange(w, grp, hf, deps, col, width, mode):
-        arr = {}
-        prev = []
-        so, dn = (T.mo, T.mi) if w == "m" else (T.so, T.si)
-        for call in MODES[mode]:
-            def fn(e, P, inc, call=call):
-                trs = []
-                e0 = 0
-                for k, sh in call:
-                    c = peer(1 + k) if w == "m" else peer(-1 - k)
-                    m = sum(1 << x for x in topo.engines(me, c)[e0:e0 + NE // sh])
-                    e0 += NE // sh
-                    a = col(k)
-                    trs.append((c, m, T.sem["%s%d%d%d" % (w, grp, hf, k)], so[:, a:a + width], dn[:, a:a + width]))
-                sent[0] += e0
-                if len(trs) == 1:
-                    c, m, sm, a, b = trs[0]
-                    g.remote_dma(b, a, sm, T.sem["sent"], topo.addr(c)[1], topo.addr(c)[0], m)
-                else:
-                    g.remote_dma_fused([RemoteDMATransfer(dst_ids=[dstid(c)], dma_engine_mask=m, remote_sem=sm, src=a, dst=b)
-                                        for c, m, sm, a, b in trs], local_sem=T.sem["sent"])
-            d = add("G", 0, [x for k, sh in call for x in deps[k]], fn, kind="rem", after=prev)
-            prev = [d]
-            for k, sh in call:
-                arr[k] = add("", 0, [d], None, kind="rarr",
-                             info=("%s%d%d%d" % (w, grp, hf, k), NE // sh, 128 * sh // NE, width * (2 if w == "m" else 4)))
-        return arr
+    PC = wa(8); CW = wa(16); CF = wa(8); I32 = wa(128)
+    c_pi = add("G", 162, [], lambda e, P, inc, Z: inc(g.iota(wi("PI"), [[0, 1]], 0, 1)))
+    c_ir = iota(132, [], cb("IR", 0, 132, 0, 1), [[0, 22], [1, 6]], 0, 0)
+    c_f63 = iota(192, [], cb("F63", 0, 192), [[0, 3], [1, 64]], 0, 0)
+    c_fr = iota(192, [], cb("FR", 0, 192), [[1, 192]], -64, 0)
+    c_nr = iota(132, [], cb("NR", 0, 132, 0, 1), [[1, 22], [0, 6]], 0, 0)
+    c_vr = iota(144, [], cb("VR", 0, 144, 0, 1), [[1, 3], [2, 8], [0, 6]], 48, 0)
+    c_pr = iota(32, [], cb("PR", 0, 32), [[8, 2], [16, 2], [1, 8]], 0, 0)
+    c_d1 = iota(864, [], T.d1[:, :], [[0, 864]], -8192, 0, after=[d, c_ir, c_f63, c_fr, c_nr, c_vr, c_pr])
+    c_tq = iota(704, [], T.tq[:, :], [[0, 704]], 0, 0, after=[c_d1])
+    c_cr = iota(144, [], cb("CR", 0, 144, 0, 1), [[0, 72], [1, 2]], -1, 0, after=[c_d1])
+    c_cr = [ms(64, cols(T.cb, CB["CR"] + 33, 4, 36, 0, 1), -1.0, [c_cr])]
+    c_on = ms(64, cb("ON", 0, 128, 0, 1), 1.0)
+    c_x0 = ms(160, cb("LA", 0, 320), 0.0)
+    c_zi = ms(396, T.zi[:, :], 0.0)
+    bit = lambda c, s, m: ts(64, [c_pi], wi("PI", c), wi("PI"), s, m, OP.logical_shift_right, OP.bitwise_and)
+    pbits = [bit(1, 0, 15), bit(2, 1, 1), bit(3, 2, 3), bit(4, 0, 3)]
+    c_pc = cp(64, pbits, wf(PC, 5), wi("PI", 0, 5))
+    c_tb = aff(1, [c_pc], wf(PC + 5), wf(PC + 2), 4096.0, 2048.0)
+    c_fb = ts(64, [c_pc], wf(PC + 6), wf(PC), 72.0, 6120.0, OP.is_lt, OP.mult)
+    c_o1 = aff(1, [c_pc], wf(PC + 7), wf(PC + 3), 36.0, 32.0)
+    c_of = [cp(64, pbits, T.of[:, 0:1], wi("PI", 3)), ts(64, [c_o1], T.of[:, 2:3], wf(PC + 7), wf(PC + 4), None, OP.add)]
+    c_i16 = ts(64, [c_pc, c_fr], ch("ID", 0, 128), cb("FR", 64, 128), wf(PC), None, OP.is_equal)
+    eye = lambda o, s: aff(128, [c_i16], o, ch("ID", 0, 128), s, 0.0, cyv=64)
+    c_id, c_ni, c_n16, c_i32 = eye(cb("ID", 0, 128), 1.0), eye(cb("NI", 0, 128), -1.0), eye(ch("NI", 0, 128), -1.0), eye(wf(I32, 128), 1.0)
+    c_sel = [ts(64, [c_pc, c_fr], cb(nm, 0, 18), cb("FR", 64, 18), wf(PC + 1), s, OP.is_equal, OP.mult) for nm, s in (("SEL", 1.0), ("NSEL", -1.0))]
+    w1 = ts(66, [c_ir], cb("SA", 0, 132, 0, 1), cb("IR", 0, 132, 0, 1), 2.0, 2.0, OP.mult, OP.min)
+    w2 = ts(66, [c_ir], cb("SB", 0, 132, 0, 1), cb("IR", 0, 132, 0, 1), 0.0, None, OP.is_equal)
+    w3 = vop(66, [w1, w2], lambda P: V.tensor_tensor_scan(cb("WR", 0, 132, 0, 1), cb("SA", 0, 132, 0, 1), cb("SB", 0, 132, 0, 1),
+                                                          0.0, OP.mult, OP.add))
+    rows = [(nm, sh) for sh in (0, 2, 4) for nm in ("NR", "WR")] + [("VR", 0)]
+    w4, j = mm([c_nr, c_vr, w3, c_on], lambda P, Z: [(P[:, x:x + 1], cb(nm, sh, 128, 0, 1), cb("ON", 0, 1, 0, 1), True, True)
+                                                     for x, (nm, sh) in enumerate(rows)])
+    w5 = aff(7, [w4], wf(CW, 7), lambda P: P[:, 0:7], 1.0, 0.0, job=j)
+    w6 = ts(64, [w5, c_pc], wf(CW + 7), wf(PC), 64.0, wf(CW + 5), OP.is_ge, OP.mult)
+    w7 = [aff(1, [w5], wf(CW + 8 + x), wf(CW + c), 1.0, b) for x, (c, b) in enumerate(((2, 21.0), (2, -11.0), (4, 10.0)))]
+    wt = lambda nm, c, a, b, d: ts(64, d + [c_pr], ch(nm, c, 32), cb("PR", 0, 32), wf(CW + a), wf(CW + b), OP.is_equal, OP.mult)
+    c_w0, c_w2, c_wb = wt("W0", 0, 0, 1, [w5]), wt("W2", 0, 10, 5, w7), wt("WB", 0, 10, 7, w7 + [w6])
+    c_w1 = [wt("W1", 32 * x, 8 + x, 3, w7) for x in range(2)]
+    c_nw = aff(32, [c_w0], ch("NW", 0, 32), ch("W0", 0, 32), -1.0, 0.0)
+    c_v = [ts(88, [w5, c_f63], ch(nm, 0, 176, 0, 96), cb("F63", 0, 176, 0, 96), wf(CW + 6, 1, 1, 96), s, OP.is_equal, OP.mult)
+           for nm, s in (("V1", 129.0 / 64), ("V2", 2.0))]
 
-    cv, ptc = {}, []
-    for k in (3, 0, 1, 2):
-        cv[k] = ts(512, [l_pos[k]], T.pz[:, k * 512:k * 512 + 512], wi("POS", k * 512, 512), 2.0, 2.0, OP.mult, OP.add)
+    h96 = lambda nm, a=0, n=128: ch(nm, a, n, 0, 96)
+
+    def onehot(k, dep):
+        return [ts(64, [dep, c_f63], h96("H", 256 * k + 128 * a), cb("F63", 0, 128, 0, 96), wf(CF + 2 * k + a, 1, 1, 96), s,
+                   OP.is_equal, OP.mult) for a, s in ((0, -1.0 / 64), (1, -2.0))]
+
+    def smat(k, o):
+        w = 48 - 16 * ((rank + 1 + k) % N)
+        return group([(o, x, h96("ID", 0, 96)) for x in (h96("V1", w), h96("H", 256 * k), h96("H", 256 * k + 128))])
+
+    def lmat(k, t, o, p0=0, n=128):
+        w = 48 - 16 * ((rank + 1 + k) % N)
+        return [(o, x, h96("NW", 16 * t, 8)) for x in (h96("V2", w + p0, n), h96("H", 256 * k + 128 + p0, n))]
+    s0 = onehot(3, cp(64, [l_cand], wf(CF + 6, 2, 1, 96), wi("CAND", 8, 2, 0, 96)))
+    s3, j = mm(s0 + c_v + [c_i16], lambda P, Z: smat(3, P[:, 0:96]))
+    s_x = [aff(96, [s3, c_x0], cb("X", 96 * h, 96, 64 * h, 64 * h + 64), lambda P, h=h: P[64 * h:64 * h + 64, 0:96],
+               1.0, 0.0, job=j) for h in range(2)]
+    s_all = [aff(96, [s3], cb("SALL", 288, 96), lambda P: P[:, 0:96], 1.0, 0.0, job=j, after=s_x)]
+    s3, j = mm(s0 + c_v + [c_i16, c_nw], lambda P, Z: [(P[:, 0:32], h96("V2"), h96("ID", 96, 32), True, False)] + [
+        x + (False, i == 3) for h in range(2) for i, x in enumerate(
+            [y for t in range(2) for y in lmat(3, t, cols(P, 16 * t + 8 * h, 8, 1, 64 * h, 64 * h + 64), 64 * h, 64)])])
+    s_l0 = aff(32, [s3], cb("X", 192, 32), lambda P: P[:, 0:32], 1.0, 0.0, job=j)
+    s1 = cp(64, [s_arr], wf(CF, 6, 1, 96), wi("CAND", 0, 6, 0, 96))
+    s1 = [x for k in range(3) for x in onehot(k, s1)] + s0 + c_v + [c_i16, c_nw]
+    s3, j = mm(s1, lambda P, Z: [x for k in range(3) for x in smat(k, P[:, 96 * k:96 * k + 96])])
+    s_all.append(aff(288, [s3], cb("SALL", 0, 288), lambda P: P[:, 0:288], 1.0, 0.0, job=j))
+    s3, j = mm(s1, lambda P, Z: [x for k in range(4) for t in range(2) for x in group(
+        lmat(k, t, cols(P, 32 * (k // 2) + 16 * t + 8 * (k % 2), 8)))])
+    s_l = [aff(64, [s3, c_x0], cb("LA", 64 * h, 64, 64 * h, 64 * h + 64), lambda P, h=h: P[64 * h:64 * h + 64, 0:64],
+               1.0, 0.0, job=j) for h in range(2)]
+
+    def send(w, grp, hf, k, deps, a, b, nb, after):
+        def fn(e, P, inc, Z):
+            c = peer(1 + k) if w == "m" else peer(-1 - k)
+            g.remote_dma(b, a, T.sem["%s%d%d%d" % (w, grp, hf, k)], T.sem["sent"], topo.addr(c)[1], topo.addr(c)[0], topo.mask(me, c))
+            sent[0] += NE
+            if w == "m" and cfg["dup"]:
+                x = ((grp * 2 + hf) * 3 + k) * 64
+                g.remote_dma(T.dup[:, x:x + 64], a, T.sem["dup"], T.sem["sent"], topo.addr(c)[1], topo.addr(c)[0], topo.mask(me, c))
+                sent[0] += NE
+        d = add("G", 0, deps, fn, kind="rem", after=after + [c_tq])
+        return add("", 0, [d], None, kind="rarr", info=("%s%d%d%d" % (w, grp, hf, k), NE, 128 // NE, nb))
+
+    ptc = []
     qc = lambda q: (q % 2) * 128 + (q // 2) * 64
     for hf in range(2):
-        a, j = mm(256, [cv[3], c_id], lambda P, inc, hf=hf: [inc(PE.matmul(
+        a, j = mm([cv[3], c_id], lambda P, Z, hf=hf: [(
             P[:, qc(q):qc(q) + 64], T.pz[64 * hf:64 * hf + 64, 1536 + q * 128:1536 + q * 128 + 128],
-            cb("ID", 64 * hf, 64, 64 * hf, 64 * hf + 64), True, True)) for q in range(4)], n=4)
-        ptc.append(affine([a], T.pt[:, hf * 256:hf * 256 + 256], 128, 256, 0.5, -33.0, j))
-    k1 = cp(128, [l_co], (cb("CO", 0, 128, 0, 72), wi("CO", 0, 128, 0, 72)))
-    k2, j = mm(72, [k1, c_id], lambda P, inc: inc(PE.matmul(P[:, 0:72], cb("CO", 0, 128, 0, 72), cb("ID", 0, 72, 0, 72), True, True)))
-    CO = wa(72); R = wa(112); AD = wa(32); BI = wa(32); TM = wa(64); M = wa(64)
-    D0 = [wa(32), wa(32)]; D1 = [wa(32), wa(32)]; AB = [wa(32), wa(32)]
-    C1B = wa(16); C0D = wa(16); C1D = wa(16); TP = wa(16); T8 = wa(32)
-    co = affine([k2], wf(CO, 72), 128, 72, 1.0, 0.0, j)
-    zb = ms(64, wf(BI, 32), 0.0)
-    zd = ms(64, wf(D0[0], 64), 0.0)
-    k3 = cp(320, [co, zb], (wf(R, 24, 2), wf(CO, 24)), (wf(R + 1, 24, 2), wf(CO + 24, 24)), (wf(AD, 16, 2), wf(CO + 8, 16)),
-            (wf(AD + 1, 16, 2), wf(CO + 8, 16)), (wf(BI + 1, 16, 2), wf(CO + 32, 16)))
+            cb("ID", 64 * hf, 64, 64 * hf, 64 * hf + 64), True, True) for q in range(4)])
+        ptc.append(aff(256, [a], T.pt[:, hf * 256:hf * 256 + 256], lambda P: P[:, 0:256], 1.0 / 64, -0.5, job=j))
+    k1 = cp(128, [l_co], cb("CO", 0, 128, 0, 72), wi("CO", 0, 128, 0, 72))
+    a0, a1, a2, b0, b1, b2, zr = 0, 8, 16, 24, 32, 40, 80
+    lay = [a0, b0, a0, b0, a1, b1, a1, a1, a2, a2, a2, a2, zr, b1, zr, b2, zr, b2, 48, 56, 64]
+    CO = wa(168); TM = wa(64); R = wa(64); M = wa(64); B0 = wa(8); BS = wa(32); AL = wa(32); DL = wa(32)
 
-    def comp(deps, i, kk, src):
-        a = tt(64, deps, wf(TM + 16 * (i - 3), 16), wf(AD + 16 * (kk - 1), 16), wf(R + 16 * src, 16), OP.mult)
-        return tt(64, [a], wf(R + 16 * i, 16), wf(TM + 16 * (i - 3), 16), wf(BI + 16 * (kk - 1), 16), OP.add)
-    r3 = comp([k3], 3, 1, 0); r4 = comp([k3], 4, 2, 0); r5 = comp([k3], 5, 2, 1); r6 = comp([r3], 6, 2, 3)
-    m1 = cp(64, [r3, r4, r5, r6], (wi("MOD", 0, 64), wf(R + 48, 64)))
+    def moves(x0, x1):
+        k2, j = mm([k1, c_id], lambda P, Z: [(P[:, 8 * x:8 * x + 8], cb("CO", 0, 128, 0, 72), cb("ID", lay[x], 8, 0, 72), True, True)
+                                             for x in range(x0, x1)])
+        return aff(8 * (x1 - x0), [k2], wf(CO + 8 * x0, 8 * (x1 - x0)), lambda P: P[:, 8 * x0:8 * x1], 1.0, 0.0, job=j)
+    co0 = moves(0, 2)
+    co = moves(2, 21)
+    r1 = tt(96, [co0, co], wf(TM, 48), wf(CO, 48), wf(CO + 48, 48), OP.mult)
+    r1 = tt(96, [r1], wf(R, 48), wf(TM, 48), wf(CO + 96, 48), OP.add)
+    r2 = tt(64, [r1], wf(TM + 48, 16), wf(R, 16), wf(CO + 64, 16), OP.mult)
+    r2 = tt(64, [r2], wf(R + 48, 16), wf(TM + 48, 16), wf(CO + 112, 16), OP.add)
+    m1 = cp(64, [r2], wi("MOD", 0, 64), wf(R, 64))
     m2 = ts(64, [m1], wi("MOD", 0, 64), wi("MOD", 0, 64), 63, None, OP.bitwise_and)
-    m3 = cp(64, [m2], (wf(M, 64), wi("MOD", 0, 64)))
-    e1 = tt(64, [m3, zd], wf(D0[0] + 1, 16, 2), wf(M, 16), wf(R + 16, 16), OP.subtract)
-    e2 = cp(64, [k3], (wf(D1[0] + 1, 16, 2), wf(R + 16, 16)))
-    e3 = tt(64, [m3], wf(C1B, 16), wf(M + 16, 16), wf(R + 32, 16), OP.subtract)
-    e4 = tt(64, [m3], wf(C0D, 16), wf(M + 32, 16), wf(R + 32, 16), OP.subtract)
-    e5 = tt(64, [m3], wf(TP, 16), wf(M + 48, 16), wf(M + 16, 16), OP.subtract)
-    e6 = tt(64, [e5, e4], wf(C1D, 16), wf(TP, 16), wf(C0D, 16), OP.subtract)
+    m3 = cp(64, [m2], wf(M, 64), wi("MOD", 0, 64))
+    c_b0 = aff(8, [co0], wf(B0, 8), wf(CO + 8, 8), 1.0 / 64, 192.0078125)
 
-    def mcol(o, hf, k):
-        return (hf * 4 + k) * 128 + o * 64 if o < 2 else 512 * o + (hf * 4 + k) * 64
+    def choice(deps, out, xa, xb, ya, yb):
+        return [aff(8, deps, out(v), wf(c, 8), s, b) for v, (c, s, b) in enumerate(
+            ((xa, -1.0, -64.0), (ya, 1.0, 0.0), (xb, -1.0 / 64, -64.0078125), (yb, 1.0 / 64, 192.0078125)))]
+    c_t = aff(24, [co, c_d1], cols(T.d1, 0, 24, 36), wf(CO + 144, 24), 129.0, -128.0)
+    lim0 = choice([m3, c_d1], lambda v: cols(T.d1, 32 + v, 8, 36), M, M + 8, CO + 32, CO + 40)
+    bs = choice([m3], lambda v: wf(BS + v, 8, 4), M + 32, M + 40, CO + 64, CO + 120)
+    al = choice([m3], lambda v: wf(AL + v, 8, 4), M + 48, M + 56, M + 16, M + 24)
+    dl = tt(64, bs + al, wf(DL, 32), wf(BS, 32), wf(AL, 32), OP.subtract)
+    lim2 = [ms(64, cols(T.d1, 576 + 32 + v, 8, 36), v - 1.0, [c_d1]) for v in range(2)]
 
     def positions(o, hf, deps, acol, bcol):
-        ix = ((o - 1) * 2 + hf) * 256
-        a = vop(256, deps + [ptc[hf]], lambda P, inc: [inc(V.tensor_scalar(
-            T.yb[:, ix + qc(q):ix + qc(q) + 64], T.pt[:, hf * 256 + qc(q):hf * 256 + qc(q) + 64], acol(q), bcol(q), OP.mult, OP.add))
-            for q in range(4)], n=4)
-        b = ts(128, [a], T.flb[:, ix:ix + 256], T.yb[:, ix:ix + 256], 1.0 / 64, 192.0078125, OP.mult, OP.add)
+        ix = (o - 1) * 2 + hf
+        dg = [aff(128, deps + [c_id], T.dg[:, ix * 512 + q * 128:ix * 512 + q * 128 + 128], cb("ID", 0, 128), acol(q), 0.0, cyv=64)
+              for q in range(4)]
+        fl = [aff(64, deps + [ptc[hf]], T.fl[:, ix * 256 + qc(q):ix * 256 + qc(q) + 64], T.pt[:, hf * 256 + qc(q):hf * 256 + qc(q) + 64],
+                  acol(q), bcol(q)) for q in range(4)]
+        c, j = mm(dg + fl + [c_ni], lambda P, Z: [x for y in range(2) for x in (
+            [(P[:, 128 * y:128 * y + 128], T.fl[:, ix * 256 + 128 * y:ix * 256 + 128 * y + 128], cb("NI", 0, 128), True, False)]
+            + [(P[64 * h:64 * h + 64, 128 * y:128 * y + 128], T.pt[:, hf * 256 + qc(2 * h + y):hf * 256 + qc(2 * h + y) + 64],
+                T.dg[:, ix * 512 + (2 * h + y) * 128:ix * 512 + (2 * h + y) * 128 + 128], False, True) for h in range(2)])])
+        return aff(256, [c], T.pos2[:, ix * 256:ix * 256 + 256], lambda P: P[:, 0:256], 64.0, 193.0 * 64, job=j)
 
-        def ftr(P, inc):
-            for c in (0, 128):
-                PE.matmul(P[:, c:c + 128], T.yb[:, ix + c:ix + c + 128], T.i2[:, 0:128], True, False)
-                inc(PE.matmul(P[:, c:c + 128], T.flb[:, ix + c:ix + c + 128], cb("IN", 0, 128), False, True))
-        c, j = mm(512, [b, c_i2, c_in], ftr, n=4)
-        return affine([c], T.pos2[:, o * 512 + hf * 256:o * 512 + hf * 256 + 256], 128, 256, 1.0, 24642.0, j)
+    def zpass(dep, j, c, n):
+        return aff(n, [dep], T.zz[:, c:c + n], lambda P: P[:, 0:n], 1.0, 1536.4921875, job=j, cls="D")
 
-    def compare(dep, j, c):
-        def fc(e, P, inc):
-            if e == "V":
-                inc(V.tensor_scalar(T.bits[:, c:c + 512], P[:, 0:512], -1.0, 1.0, OP.max, OP.min))
-            else:
-                inc(ACT.activation(T.bits[:, c:c + 512], P[:, 0:512], AF.Sign))
-        return add("VA", 512, [dep], fc, job=j, role="r")
+    def bpass(deps, c, n):
+        return ts(n // 2, deps, T.bb[:, c:c + n], T.zz[:, c:c + n], 1538.0, 64.0, OP.is_ge, OP.mult)
 
-    def maskmm(j, part, v, c0, deps, after):
-        def fm(e, P, inc):
-            for dl in range(8):
-                y, q = dl // 4, dl % 4
-                c = c0(q) + y
-                i = PE.matmul(P[:, 0:64], cb("W", 144 * v + 11 - (8 * y + q), 128), T.bits[:, c:c + 127:2],
-                              part == 0 and dl == 0, part == 1 and dl == 7)
-            if part:
-                inc(i)
-        return add("P", 512, deps + [c_w[v]], fm, job=j, role="w", n=8, after=after)
+    def offsets(dep, j, a):
+        zj = newjob()
+        z = [aff(64, [dep, c_zi], lambda Z, t=t: cols(T.zi, Z + 1 + 2 * t, 64, 4), lambda P, t=t: cols(P, 64 * t, 64), 1.0, -98816.0,
+                 job=j, cls="M", zj=zj) for t in range(2)]
+        s, j2 = mm(z + [c_i16], lambda P, Z: [x for k in range(2) for x in group(
+            [(P[:, 64 * k:64 * k + 64], cols(T.zi, Z + 1 + 128 * k - y, 128), ch("ID", 64 * y, 64)) for y in range(2)])], zj=zj)
+        return vop(128, [s, c_tb], lambda P: V.tensor_scalar(T.mk[:, a:a + 128], P[:, 0:128], wf(PC + 5), None, OP.add), job=j2)
 
-    def offsets(dep, j, o, hf, k, away):
-        a = mcol(o, hf, k)
-        return vop(64, [dep, c_tb], lambda P, inc: inc(V.tensor_scalar(
-            (T.mo if away else T.mi)[:, a:a + 64], P[:, 0:64], wf(TB), None, OP.add)), job=j, role="r")
+    mo = lambda o, hf, k: ((o - 1) * 2 + hf) * 256 + 64 * k
+    mi = lambda o, hf, k: 1536 + 128 * k + 64 * hf if o == 0 else mo(o, hf, 3) if k == 3 else 2048 + ((o - 1) * 2 + hf) * 192 + 64 * k
 
     def masks(o, hf, pdep):
-        pc = o * 512 + hf * 256
-        dmm, cmpo, out = [], [], []
-        bc = lambda tl: ((o * 2 + hf) * 6 + tl) * 512
-        for tl in range(6):
-            a, j = mm(512, [pdep, s_loc, s_arr], lambda P, inc, pr=tl // 2, h=tl % 2: [inc(PE.matmul(
-                P[:, x * 256:x * 256 + 256], T.sall[64 * h:64 * h + 64, pr * 256 + x * 128:pr * 256 + x * 128 + 128],
-                T.pos2[64 * h:64 * h + 64, pc:pc + 256], True, True)) for x in range(2)], n=2, info="D")
-            dmm.append(a)
-            cmpo.append(compare(a, j, bc(tl)))
-        for k in range(4):
-            tl = 3 * (k // 2) + k % 2
+        ix = (o - 1) * 2 + hf
+        pc, zc = ix * 256, (2 + ix) * 1536
+        zat = lambda tl, h: zc + (512 * h + 256 * tl if tl < 2 else 1024 + 256 * h)
+        zs, bs_ = {}, {}
+        for tls in ((0, 1), (2,)):
+            for h in range(2):
+                a, j = mm([pdep] + s_all, lambda P, Z, tls=tls, h=h: [(
+                    P[:, x * 256:x * 256 + 256], cb("SALL", 128 * tl, 128, 64 * h, 64 * h + 64), T.pos2[64 * h:64 * h + 64, pc:pc + 256],
+                    True, True) for x, tl in enumerate(tls)], cls="D", info="D")
+                z = zpass(a, j, zat(tls[0], h), 256 * len(tls))
+                zs[tls[0], h] = z
+                if len(tls) == 2:
+                    bs_[0, h] = bpass([z], zat(0, h), 512)
+        bs_[2, 0] = bs_[2, 1] = bpass([zs[2, 0], zs[2, 1]], zat(2, 0), 512)
+        out = []
+        for gp in range(2):
             j = newjob()
-            a = dmm[(tl + 1) // 2 * 2 + 1]
-            for part in range(2):
-                x = tl + part
-                a = maskmm(j, part, 2 * (k % 2) + part, lambda q, x=x: bc(x // 2 * 2 + q // 2) + (x % 2) * 256 + (q % 2) * 128,
-                           cmpo[x // 2 * 2:x // 2 * 2 + 2], [a, dmm[(tl + 1) // 2 * 2]])
-            out.append(offsets(a, j, o, hf, k, k < 3))
-        return out
+            a = None
+            ws = [(0, ch("W0", 0, 32)), (1, ch("W1", 0, 32))] if gp == 0 else [(1, ch("W1", 32, 32)), (2, ch("W2", 0, 32))]
+            parts = [(T.zz, zs, h) for h in range(2)] + [(T.bb, bs_, h) for h in range(2)]
+            for x, (t, dep, h) in enumerate(parts):
+                a, _ = mm([dep[0, h], dep[2 * gp, h], c_w0, c_w2] + c_w1 + s_l, lambda P, Z, x=x, t=t, h=h, ws=ws, gp=gp: [
+                    (cols(P, 2 * q0 + h, 32, 4), u, w, x + q0 + i == 0, x + q0 + i == 5) for q0 in range(2) for i, (u, w) in enumerate(
+                        [(cols(t, zat(tl, h) + q0, 128, 2), w) for tl, w in ws]
+                        + [(cols(T.pos2, pc + q0, 128, 2), cb("LA", 64 * h + 32 * gp, 32))][:x < 2])],
+                    job=j, cls="M", after=[a] if a else [])
+            out.append(offsets(a, j, mo(o, hf, 2 * gp)))
+        return [out[0], out[0], out[1], out[1]]
 
     def masks0():
-        z = ms(64, cb("SBD", 0, 128), 0.0)
-        z = cp(128, [z, s_loc], *[(cb("SBD", 64 * h, 64, 64 * h, 64 * h + 64), T.sall[64 * h:64 * h + 64, 704:768]) for h in range(2)])
-        out = [[None] * 4, [None] * 4]
+        out = {}
         for k in (3, 0, 1, 2):
             cur[:] = [0, 0]
-            db, j = mm(512, [cv[k], z], lambda P, inc, k=k: inc(PE.matmul(
-                P[:, 0:512], cb("SBD", 0, 128), T.pz[:, k * 512:k * 512 + 512], True, True)), info="D")
-            cb_ = compare(db, j, (8 + k) * 512)
-            for hf in range(2):
-                cur[:] = [hf, 0]
-                da, j = mm(512, [cv[k], s_loc], lambda P, inc, k=k, hf=hf: inc(PE.matmul(
-                    P[:, 0:512], T.sall[64 * hf:64 * hf + 64, 576:704], T.pz[64 * hf:64 * hf + 64, k * 512:k * 512 + 512], True, True)),
-                    info="D")
-                ca = compare(da, j, (hf * 4 + k) * 512)
-                j = newjob()
-                a = maskmm(j, 0, 0, lambda q, c=(hf * 4 + k) * 512: c + q * 128, [ca], [db])
-                a = maskmm(j, 1, 4 if hf else 1, lambda q, c=(8 + k) * 512: c + q * 128, [cb_], [a])
-                out[hf][k] = offsets(a, j, 0, hf, k, False)
+            zc, pc = k * 768, k * 512
+            da, j = mm([cv[k]] + s_x, lambda P, Z, pc=pc: [(P[:, 0:512], cb("X", 0, 128), T.pz[:, pc:pc + 512], True, True)],
+                       cls="D", info="D")
+            za = zpass(da, j, zc, 512)
+            db, j = mm([cv[k]] + s_x, lambda P, Z, pc=pc: [(P[64 * h:64 * h + 64, 0:256], cb("X", 128, 64),
+                       T.pz[:, pc + 256 * h:pc + 256 * h + 256], True, True) for h in range(2)], cls="D", info="D")
+            zb = zpass(db, j, zc + 512, 256)
+            b = bpass([za, zb], zc, 768)
+            a, j = mm([b, c_w0, c_wb, s_l0] + c_w1, lambda P, Z, zc=zc, pc=pc: [x for h in range(2) for q0 in range(2) for x in group(
+                [(cols(P, 2 * q0 + h, 32, 4), cols(t, zc + c + q0, 128, 2), w) for t in (T.zz, T.bb)
+                 for c, w in ((256 * h, ch("W0", 0, 32)), (512, ch("WB" if h else "W1", 0, 32)))]
+                + [(cols(P, 2 * q0 + h, 32, 4), cols(T.pz, pc + 256 * h + q0, 128, 2), cb("X", 192, 32))])], cls="M")
+            out[k] = offsets(a, j, mi(0, 0, k))
         return out
 
     def lookup(o, hf, k, dep):
-        a = mcol(o, hf, k)
+        a = mi(o, hf, k)
         gc0 = ((o * 2 + hf) * 4 + k) * 1024
+        n = cfg["gs"][o]
+        w = 64 // n
 
-        def fg(e, P, inc):
-            src = T.tabs[:, 0:8192].indirect(T.mi[:, a:a + 64])
-            if e == "V":
-                inc(V.tensor_copy(T.gat[:, gc0:gc0 + 1024], src))
-            else:
-                inc(ACT.activation(T.gat[:, gc0:gc0 + 1024], src, AF.Copy))
-        ga = add("VA", 1024, [dep, l_tab], fg, kind="gat")
+        def fg(e, x):
+            src = T.tabs[:, 0:8192].indirect(T.mk[:, a + x * w:a + x * w + w])
+            dst = T.gat[:, gc0 + 16 * x * w:gc0 + 16 * (x + 1) * w]
+            return V.tensor_copy(dst, src) if e == "V" else ACT.activation(dst, src, AF.Copy)
+        return [add("VA", 16 * w, [dep, l_tab], lambda e, P, inc, Z, x=x: inc(fg(e, x)), kind="gat") for x in range(n)]
 
-        def fr_(P, inc):
-            for q in range(4):
-                for t in range(2):
-                    c = gc0 + t * 4 + q
-                    i = PE.matmul(P[:, q * 16:q * 16 + 16], T.gat[:, c:c + 1017:8], cb("SEL", 0, 16), t == 0, t == 1)
-                inc(i)
-        return mm(512, [ga, c_sel], fr_, n=8)
+    def sums(o, hf, k, out, sel="SEL"):
+        gc0 = ((o * 2 + hf) * 4 + k) * 1024
+        return [[(out(q), cols(T.gat, gc0 + 4 * (q // 2) + 2 * t + q % 2, 128, 8), cb(sel, 0, 18)) for t in range(2)] for q in range(4)]
 
     mk0 = masks0()
+    i32 = wf(I32, 128)
     for hf in range(2):
-        OUT = wa(80); FP = wa(64); TPm = wa(64)
         cur[:] = [hf, 1]
-        mk = masks(1, hf, positions(1, hf, [co], lambda q, hf=hf: wf(CO + 4 * hf + q), lambda q, hf=hf: wf(CO + 24 + 4 * hf + q)))
-        Fc = fdep = None
-        selprep = [e1, e2]
-        flags = []
+        mk = masks(1, hf, positions(1, hf, [c_b0], lambda q, hf=hf: wf(CO + 4 * hf + q), lambda q, hf=hf: wf(B0 + 4 * hf + q)))
+        tqa = lambda x, hf=hf: (hf * 4 + x) * 88
+        terms, lim = [], lim0 + [c_t]
         for r in range(3):
             os_ = (0, 1) if r == 0 else (r + 1,)
-            wd = 64 * len(os_)
-            th = wf(CO + 48 + 8 * r + 4 * hf, 4)
-            col = lambda k, o=os_[0], hf=hf: mcol(o, hf, k)
-            arr = exchange("m", r, hf, [[mk[k]] for k in range(3)], lambda k, r=r, hf=hf: mcol(r + 1, hf, k), 64, cfg["mm"])
-            cps = [[], [], [], []]
-            NN = wa(384 if r == 0 else 192); DF = wa(64); CM = wa(64); CN = wa(64); TQ = wa(64); FN = wa(64)
-            for k in range(4):
-                for o in os_:
-                    red, j = lookup(o, hf, k, mk0[hf][k] if o == 0 else arr[k] if k < 3 else mk[3])
-                    a = mcol(o, hf, k)
-                    if k == 3 and r > 0:
-                        cps[k].append(vop(64, [red, fdep], lambda P, inc, NN=NN, Fc=Fc: inc(V.tensor_tensor(
-                            wf(NN, 64), wf(Fc, 64), P[:, 0:64], OP.subtract)), job=j, role="r"))
-                    else:
-                        cps[k].append(affine([red], (T.so if k < 3 else T.si)[:, a:a + 64], 128, 64, 1.0, 0.0, j))
-            sar = exchange("s", r, hf, cps, col, wd, cfg["sm"])
-            sic = [T.si[:, col(k):col(k) + wd] for k in range(4)]
+            wd = 72 * len(os_)
+            sc = lambda k, r=r, hf=hf, wd=wd: (0, 864, 1296)[r] + (hf * 3 + k) * wd
+            arr, sar, prev = {}, {}, []
+            for k in range(3):
+                a, b = mo(r + 1, hf, k), mi(r + 1, hf, k)
+                arr[k] = send("m", r, hf, k, [mk[k]], T.mk[:, a:a + 64], T.mk[:, b:b + 64], 128, prev)
+                prev = [arr[k] - 1]
+            ga = {k: [x for o in os_ for x in lookup(o, hf, k, mk0[k] if o == 0 else arr[k] if k < 3 else mk[3])] for k in range(4)}
+            prev = []
+            for k in range(3):
+                a, j = mm(ga[k] + c_sel, lambda P, Z, k=k, os_=os_, hf=hf: [x for i, o in enumerate(os_) for l in sums(
+                    o, hf, k, lambda q: cols(P, 72 * i + 18 * q, 18)) for x in group(l)])
+                a = aff(wd, [a], cols(T.so, sc(k), wd), lambda P, wd=wd: P[:, 0:wd], 1.0, -2040.0, job=j)
+                sar[k] = send("s", r, hf, k, [a], cols(T.so, sc(k), wd), cols(T.si, sc(k), wd), 2 * wd, prev)
+                prev = [sar[k] - 1]
+            j = newjob()
+
+            def head(P, Z, r=r, hf=hf, tqa=tqa):
+                l = [(P[:, 0:144], cb("ON", 0, 128, 0, 1), cb("CR", 0, 144, 0, 1))]
+                l += [(cols(P, 1, 72, 2), i32, cols(T.tq, tqa(x), 72)) for x in range(r + 1 if r else 0)]
+                for o, sel in ((1, "SEL"), (0, "NSEL")) if r == 0 else ((r + 1, "SEL"),):
+                    l += [x for y in sums(o, hf, 3, lambda q: cols(P, 36 * q + 1, 18, 2), sel) for x in y]
+                return [(o, a, b, x == 0, False) for x, (o, a, b) in enumerate(l)]
+            a, _ = mm(ga[3] + c_sel + c_cr + [c_on, c_i32] + terms, head, job=j, cls="L", f32=72 * (r + 1) if r else 0)
+            for k in range(3):
+                a, _ = mm([sar[k], c_n16], lambda P, Z, k=k, r=r, sc=sc, wd=wd: [
+                    (cols(P, 1, 72, 2), ch("NI" if x < wd - 72 else "ID", 0, 128), cols(T.si, sc(k) + x, 72), False, k == 2 and x == wd - 72)
+                    for x in range(0, wd, 72)], job=j, cls="L", after=[a])
+            CM = wa(144); SC = wa(144)
+            cm = vop(144, [a], lambda P, CM=CM: V.tensor_scalar(wf(CM, 144), P[:, 0:144], 0.0, 129.0, OP.is_ge, OP.mult), job=j, cls="L")
+            d1 = cols(T.d1, 288 * r + 144 * hf, 144)
+            sl = vop(144, [cm] + lim, lambda P, CM=CM, SC=SC, d1=d1: V.tensor_tensor_scan(
+                wf(SC, 144), wf(CM, 144), d1, 200.0, OP.subtract, OP.max))
+            tq = tqa(r + 1)
             if r == 0:
-                a = tt(256, cps[3] + [sar[0]], wf(NN, 128), sic[3], sic[0], OP.add)
-                a = tt(256, [a, sar[1]], wf(NN + 128, 128), wf(NN, 128), sic[1], OP.add)
-                fdep = tt(256, [a, sar[2]], wf(NN + 256, 128), wf(NN + 128, 128), sic[2], OP.add)
-                Fc = NN + 256
-                x0, x1, dd = wf(Fc + 64, 64), wf(Fc, 64), [fdep]
-            else:
-                a = tt(128, cps[3] + [sar[0]], wf(NN + 64, 64), wf(NN, 64), sic[0], OP.subtract)
-                a = tt(128, [a, sar[1]], wf(NN + 128, 64), wf(NN + 64, 64), sic[1], OP.subtract)
-                x0, x1, dd = sic[2], wf(NN + 128, 64), [a, sar[2]]
-            cm = tt(128, dd, wf(CM, 64), x0, x1, OP.is_ge)
-            df = tt(128, dd, wf(DF, 64), x0, x1, OP.subtract)
-            cn = scan(64, [cm, c_rst], wf(CN, 64), wf(RST, 64), wf(CM, 64))
-            cnt = wf(CN + 15, 4, 16)
-            fl = tt(64, [cn, co], wf(OUT + 64 + 4 * r, 4), cnt, th, OP.is_ge)
-            flags.append(fl)
+                f0, j0 = mm(ga[3] + list(sar.values()), lambda P, Z, hf=hf, sc=sc: group(
+                    [(P[:, 0:72], ch("ID", 0, 128), cols(T.si, sc(k), 72)) for k in range(3)]
+                    + [x for y in sums(0, hf, 3, lambda q: cols(P, 18 * q, 18)) for x in y]))
+                terms = [aff(72, [f0, c_tq], cols(T.tq, tqa(0), 72), lambda P: P[:, 0:72], -1.0, 0.0, job=j0)]
             if r < 2:
-                d1 = D1[r] + 16 * hf
-                ab = AB[r] + 16 * hf
-                ac = vop(128, [cn, co], lambda P, inc, d1=d1, cnt=cnt, th=th: [inc(V.tensor_tensor(
-                    wf(d1 + x, 4, 4), cnt, th, OP.is_ge)) for x in (0, 2)], n=2)
-                sl = scan(64, [ac] + selprep, wf(ab, 16), wf(D0[r] + 16 * hf, 16), wf(d1, 16))
-                mk = masks(r + 2, hf, positions(r + 2, hf, [sl], lambda q, ab=ab: wf(ab + 4 * q + 1), lambda q, ab=ab: wf(ab + 4 * q + 3)))
-                tq = vop(256, [ac, df], lambda P, inc, TQ=TQ, DF=DF, d1=d1: [inc(V.tensor_scalar(
-                    wf(TQ + 16 * q, 16), wf(DF + 16 * q, 16), wf(d1 + 4 * q), None, OP.mult)) for q in range(4)], n=4)
-                fdep = tt(128, [tq, fdep], wf(FN, 64), wf(Fc, 64), wf(TQ, 64), OP.add)
-                Fc = FN
-                if r == 0:
-                    t8 = T8 + 16 * hf
-                    a1 = tt(64, [ac, e3], wf(t8, 8), wf(d1, 8, 2), wf(C1B + 8 * hf, 8), OP.mult)
-                    a2 = tt(64, [ac, e6], wf(t8 + 8, 8), wf(d1, 8, 2), wf(C1D + 8 * hf, 8), OP.mult)
-                    selprep = [tt(64, [a1], wf(D1[1] + 16 * hf + 1, 8, 2), wf(t8, 8), wf(R + 32 + 8 * hf, 8), OP.add),
-                               tt(64, [a2, zd], wf(D0[1] + 16 * hf + 1, 8, 2), wf(t8 + 8, 8), wf(C0D + 8 * hf, 8), OP.add)]
-                else:
-                    fp = cp(256, [fdep], *[(wf(FP + q, 16, 4), wf(Fc + 16 * q, 16)) for q in range(4)])
+                fg = ts(64, [sl, c_tq], cols(T.tq, tq + 72 + 4 * r, 4), wf(SC + 33, 4, 36), 64.0, -1.0, OP.is_ge, OP.mult)
+                nf = lambda q, tq=tq, r=r: cols(T.tq, tq + 72 + 4 * r + q, 1)
+                mk = masks(r + 2, hf, positions(r + 2, hf, [sl], lambda q, SC=SC: wf(SC + 36 * q + 33), lambda q, SC=SC: wf(SC + 36 * q + 35)))
             else:
-                tq = vop(256, [fl, df], lambda P, inc, TPm=TPm, DF=DF, OUT=OUT: [inc(V.tensor_scalar(
-                    wf(TPm + q, 16, 4), wf(DF + 16 * q, 16), wf(OUT + 72 + q), None, OP.mult)) for q in range(4)], n=4)
-                fo = tt(128, [tq, fp], wf(OUT, 64), wf(FP, 64), wf(TPm, 64), OP.add)
-                a, j = mm(512, [fo, c_i32] + flags, lambda P, inc, OUT=OUT: inc(PE.transpose(P[0:76, 0:128], wf(OUT, 76), wf(I32, 128))))
-                a = affine([a], T.ob[0:76, hf * 128:hf * 128 + 128], 76, 128, 1.0, 0.0, j)
-                ldma("S", [a], "do", 0, 32768, [(T.yf[:, hf * 512:hf * 512 + 512], T.ob[0:64, hf * 128:hf * 128 + 128])])
-                ldma("A" if hf else "S", [a], "do", 0, 6144, [(T.ya[:, hf * 512:hf * 512 + 512], T.ob[64:76, hf * 128:hf * 128 + 128])])
-    assert top[0] <= 7424
+                fg = aff(4, [sl, c_tq], cols(T.tq, tq + 80, 4), wf(SC + 34, 4, 36), 1.0, 0.0)
+                nf = lambda q, SC=SC: wf(SC + 36 * q + 34)
+            terms = terms + [fg] + [aff(16, [fg if r < 2 else sl, c_tq], cols(T.tq, tq + 18 * q, 16), lambda P, q=q: cols(P, 36 * q + 1, 16, 2),
+                                        nf(q), 0.0, job=j, cls="L", after=[cm]) for q in range(4)]
+            if r == 0:
+                TP = wa(16)
+                a = tt(64, [fg, dl] + c_of, wf(TP, 16), cols(T.tq, tq + 72, 8).indirect(T.of[:, 0:1]), wf(DL + 16 * hf, 16), OP.mult)
+                lim = [tt(64, [a, c_t], cols(T.d1, 288 + 144 * hf, 144).indirect(T.of[:, 2:3]), wf(TP, 16), wf(BS + 16 * hf, 16), OP.add)]
+            elif r == 1:
+                lim = lim2
+                a, j = mm(terms, lambda P, Z, tqa=tqa: group([(P[0:84, 0:128], cols(T.tq, tqa(x), 84), i32) for x in range(3)]), f32=384)
+                early = aff(128, [a, c_fb], T.ob[0:84, 256 + hf * 128:384 + hf * 128], lambda P: P[0:84, 0:128], -1.0,
+                            wf(PC + 6, 1, 1, 84), job=j)
+            else:
+                a, j = mm(terms[-5:], lambda P, Z, tq=tq: [(P[0:84, 0:128], cols(T.tq, tq, 84), i32, True, True)], f32=128)
+                a = vop(128, [a, early], lambda P, hf=hf: V.tensor_tensor(
+                    T.ob[0:84, hf * 128:hf * 128 + 128], T.ob[0:84, 256 + hf * 128:384 + hf * 128], P[0:84, 0:128], OP.subtract), job=j)
+                prs = [(T.yf[:, hf * 512 + 128 * q:hf * 512 + 128 * q + 128], T.ob[18 * q:18 * q + 16, hf * 128:hf * 128 + 128])
+                       for q in range(4)] + [(T.ya[:, hf * 512:hf * 512 + 512], T.ob[72:84, hf * 128:hf * 128 + 128])]
+                ldma("S", [a], "do", 0, 24576, prs[:3] if hf else prs)
+                if hf:
+                    ldma("A", [a], "do", 0, 14336, prs[3:])
+    assert top[0] <= 4096
     return ops, Q, sent
 
 
 def dur(op, e, p):
     k = op["kind"]
     if k == "dma":
-        return 0.1 * op["n"]
+        return 0.06 * op["n"]
     if k == "rem":
         return p["iss"]
     if e == "P":
         return op["cyc"] * p["pc"] * 1e-3 + p["pf"] * op["n"]
-    c = op["cyc"] * (p["gr"] if k == "gat" else 1.0)
-    return c * 0.83e-3 * p["f"] + op["n"] * (p["fixa"] if e == "A" else p["fix"])
+    c = (op["cya"] if e == "A" else op["cyc"]) * (p["gr"] if k == "gat" else 1.0)
+    return c * 0.83e-3 * p["f"] + (p["fixa"] if e == "A" else p["fix"])
 
 
 def place(op, e, t0, p, st):
@@ -432,37 +472,40 @@ def place(op, e, t0, p, st):
         st["dma"] = max(t0 + p["ldst"], st["dma"]) + op["info"][2] / p["lbw"]
         return st["dma"]
     if k == "rarr":
-        if st["rsrc"] != op["deps"][0]:
-            st["rs"] = max(t0 + p["st"] + (p["first"] if st["rsrc"] is None else 0.0), st["dma"])
-            st["rsrc"] = op["deps"][0]
-        f = st["rs"] + op["info"][2] * (p["row"] + op["info"][3] / p["bw"])
-        st["dma"] = max(st["dma"], f)
-        return f + p["wake"]
+        t = max(t0 + p["st"] + (0.0 if st["used"] else p["first"]), st["dma"])
+        st["used"] = True
+        st["dma"] = t + op["info"][2] * (p["row"] + op["info"][3] / p["bw"])
+        return st["dma"] + p["wake"]
     return t0 + dur(op, e, p)
 
 
 def schedule(ops, cfg, p):
     n = len(ops)
     succ = [[] for _ in range(n)]
+    uses = {}
     for o in ops:
         for d in o["deps"] + o["after"]:
             succ[d].append(o["id"])
+        for j in (o["job"], o["zj"]):
+            uses[j] = uses.get(j, 0) + 1
     lev = [0.0] * n
     for o in reversed(ops):
         if o["kind"] == "rarr":
-            c = p["st"] + o["info"][2] * p["row"] + p["wake"]
+            c = p["st"] + o["info"][2] * p["row"] + p["wake"] + cfg["bc"]
         elif o["kind"] == "larr":
             c = p["ldst"] + o["info"][2] / p["lbw"]
         else:
             c = dur(o, o["eng"][0], p) + p["sem"]
         lev[o["id"]] = c + max([lev[s] for s in succ[o["id"]]] + [0.0])
     pri = [lev[i] + cfg["ba"] * (o["tag"][0] != 1) + cfg["bo"] * (o["tag"][1] != 1) + cfg["bd"] * (o["info"] == "D")
-           for i, o in enumerate(ops)]
+           - cfg["bg"] * (o["kind"] == "gat") + cfg.get("dp", {}).get(i, 0.0) for i, o in enumerate(ops)]
     fin = [None] * n
     free = dict(P=0.0, V=0.0, A=0.0, G=0.0, S=0.0)
-    st = dict(dma=0.0, rsrc=None, rs=0.0)
-    bank_job, bank_rd, isd = [None] * 8, [None] * 8, [False] * 8
-    jb = {}
+    st = dict(dma=0.0, used=False)
+    limit = dict(LIMIT, D=cfg["maxd"])
+    held = [None] * 11
+    touch = [{} for _ in range(11)]
+    at = {None: None}
     left = [len(o["deps"]) + len(o["after"]) for o in ops]
     ready = [o["id"] for o in ops if left[o["id"]] == 0]
     plan = []
@@ -473,7 +516,7 @@ def schedule(ops, cfg, p):
             if left[s] == 0:
                 if ops[s]["eng"] == "":
                     fin[s] = place(ops[s], "", fin[i], p, st)
-                    plan.append((s, "", None, None))
+                    plan.append((s, "", None, None, []))
                     done(s)
                 else:
                     ready.append(s)
@@ -482,35 +525,165 @@ def schedule(ops, cfg, p):
         for i in ready:
             o = ops[i]
             t = max([fin[d] + p["sem"] for d in o["deps"]] + [0.0])
-            bk = None
-            if o["role"] == "w" and o["job"] not in jb:
-                fr = [b for b in range(8) if bank_job[b] is None]
-                if not fr or (o["info"] == "D" and sum(isd[b] for b in range(8) if bank_job[b] is not None) >= cfg["maxd"]):
-                    continue
-                bk = min(fr, key=lambda b: -1.0 if bank_rd[b] is None else fin[bank_rd[b]])
-                if bank_rd[bk] is not None:
-                    t = max(t, fin[bank_rd[bk]] + p["sem"])
-            e = min(o["eng"], key=lambda x: (max(t, free[x]), x == "V"))
-            cand.append((max(t, free[e]), i, e, bk))
-        t0, _, e0, _b = min(cand)
-        t, i, e, bk = max([c for c in cand if c[0] <= t0 + cfg["slack"] and c[2] == e0], key=lambda c: pri[c[1]])
+            res = []
+            for j, rng, lim in ((o["job"], range(8), limit[o["cls"]]), (o["zj"], range(8, 11), 3)):
+                if j not in at:
+                    fr = [b for b in rng if held[b] is None]
+                    if not fr or sum(held[b] == o["cls"] for b in rng) >= lim:
+                        break
+                    res.append(min(fr, key=lambda b: max([fin[x] for x in touch[b].values()] + [-1.0])))
+                else:
+                    res.append(at[j])
+            if len(res) < 2:
+                continue
+            best = None
+            for e in o["eng"]:
+                war = [x for b in res if b is not None for e2, x in touch[b].items() if e2 != e]
+                t1 = max([t, free[e]] + [fin[x] + p["sem"] for x in war])
+                key = (t1 + (dur(o, e, p) if len(o["eng"]) > 1 else 0.0) + (cfg["vb"] if e == "V" and o["kind"] == "gat" else 0.0) + (cfg.get("de", {}).get(i, 0.0) if e == "V" else 0.0), e == "V")
+                if best is None or key < best[0]:
+                    best = (key, t1, e, war)
+            cand.append((best[1], i, best[2], res, best[3]))
+        t0, _, e0 = min(cand, key=lambda c: (c[0] - cfg["look"] * (c[2] in "PG"), c[1]))[:3]
+        mine = [c for c in cand if c[2] == e0]
+        pick = max([c for c in mine if c[0] <= t0 + cfg["slack"]], key=lambda c: pri[c[1]])
+        t1 = pick[0] + cfg["alpha"] * dur(ops[pick[1]], e0, p)
+        t, i, e, res, war = max([c for c in mine if c[0] <= t1], key=lambda c: pri[c[1]])
         o = ops[i]
-        war = None
-        if bk is not None:
-            jb[o["job"]] = bk
-            bank_job[bk] = o["job"]
-            isd[bk] = o["info"] == "D"
-            war = bank_rd[bk]
-        if o["role"] == "r":
-            bank_job[jb[o["job"]]] = None
-            bank_rd[jb[o["job"]]] = i
+        for j, b in zip((o["job"], o["zj"]), res):
+            if j is not None:
+                at[j] = b
+                uses[j] -= 1
+                held[b] = (held[b] or o["cls"]) if uses[j] else None
+                touch[b][e] = i
         fin[i] = place(o, e, t, p, st)
         free[e] = fin[i]
-        plan.append((i, e, jb.get(o["job"]), war))
+        plan.append((i, e, res[0], res[1], war))
         ready.remove(i)
         done(i)
     assert len(plan) == n
     return plan, max(fin)
+
+
+def improve(ops, plan, cfg):
+    n = len(ops)
+    ps = [dict(NOM, pc=0.417 * v.get("f", NOM["f"]), **v) for v in VARY]
+    du = [[{e: dur(o, e, p) for e in o["eng"]} for o in ops] for p in ps]
+    pre = [o["deps"] + o["after"] for o in ops]
+    succ = [[] for _ in ops]
+    land = [[] for _ in ops]
+    uses = {}
+    for o in ops:
+        for d in pre[o["id"]]:
+            succ[d].append(o["id"])
+        if o["eng"] == "":
+            land[o["deps"][0]].append(o["id"])
+        for j in (o["job"], o["zj"]):
+            uses[j] = uses.get(j, 0) + 1
+    real = lambda i: i if ops[i]["eng"] else ops[i]["deps"][0]
+    before = [{real(d) for d in pre[i]} for i in range(n)]
+    behind = [{x for s in succ[i] for x in ([s] if ops[s]["eng"] else succ[s])} for i in range(n)]
+    limit = dict(LIMIT, D=3)
+
+    def allot(order, eng):
+        at, left, out = {}, dict(uses), []
+        idle = [list(range(8)), [8, 9, 10]]
+        num = dict(L=0, M=0, S=0, D=0)
+        touch = [{} for _ in range(11)]
+        for i in order:
+            o, e = ops[i], eng[i]
+            res, war = [None, None], []
+            for x, j in enumerate((o["job"], o["zj"])):
+                if j is not None:
+                    if j not in at:
+                        if not idle[x] or (x == 0 and num[o["cls"]] >= limit[o["cls"]]):
+                            return None
+                        at[j] = idle[x].pop(0)
+                        num[o["cls"]] += 1 - x
+                    b = res[x] = at[j]
+                    war += [y for e2, y in touch[b].items() if e2 != e]
+                    touch[b][e] = i
+                    left[j] -= 1
+                    if not left[j]:
+                        idle[x].append(b)
+                        num[o["cls"]] -= 1 - x
+            out.append((i, e, res[0], res[1], war))
+            out += [(s, "", None, None, []) for s in land[i]]
+        return out
+
+    def cost(pl, bound):
+        tot = 0.0
+        for x, p in enumerate(ps):
+            fin = [0.0] * n
+            free = dict(P=0.0, V=0.0, A=0.0, G=0.0, S=0.0)
+            st = dict(dma=0.0, used=False)
+            sem, d = p["sem"], du[x]
+            last, why = {}, [None] * n
+            for i, e, _, _, war in pl:
+                if e:
+                    t = free[e] - sem
+                    w = last.get(e)
+                    for y in deps[i]:
+                        if fin[y] > t:
+                            t, w = fin[y], y
+                    for y in war:
+                        if fin[y] > t:
+                            t, w = fin[y], y
+                    fin[i] = free[e] = t + sem + d[i][e]
+                    why[i], last[e] = w, i
+                else:
+                    why[i] = deps[i][0]
+                    fin[i] = place(ops[i], "", fin[why[i]], p, st)
+            end = max(fin)
+            tot += (end + cfg["mean"] * sum(fin) / n) / ref[x]
+            if tot > bound[x]:
+                return None, None
+            part[x] = tot
+            i = fin.index(end)
+            chain[x] = []
+            while i is not None:
+                chain[x].append(real(i))
+                i = why[i]
+        return tot, (list(part), [i for c in chain for i in c])
+    deps = [o["deps"] for o in ops]
+    chain = [[] for _ in ps]
+    order = [x[0] for x in plan if x[1]]
+    eng = {x[0]: x[1] for x in plan}
+    ref, part = [1.0] * len(ps), [0.0] * len(ps)
+    best = allot(order, eng)
+    now, (parts, crit) = cost(best, [1e9] * len(ps))
+    ref = [parts[x] - (parts[x - 1] if x else 0.0) for x in range(len(ps))]
+    now, (parts, crit) = cost(best, [1e9] * len(ps))
+    low = now
+    rng = np.random.RandomState(cfg["seed"])
+    for it in range(cfg["iters"]):
+        a = order.index(crit[rng.randint(len(crit))]) if rng.rand() < cfg["focus"] else int(rng.randint(len(order)))
+        i = order[a]
+        new, old = order, eng[i]
+        u = rng.rand()
+        if len(ops[i]["eng"]) > 1 and u < 0.3:
+            eng[i] = "V" if old == "A" else "A"
+        if u > 0.15 or eng[i] == old:
+            step, b, far = (1 if rng.rand() < 0.5 else -1), a, int(rng.choice([1, 1, 2, 3, 6]))
+            stop = behind[i] if step > 0 else before[i]
+            while far and 0 <= b + step < len(order) and order[b + step] not in stop:
+                b += step
+                far -= eng[order[b]] == eng[i]
+            new = order[:a] + order[a + 1:]
+            new.insert(b, i)
+        heat = cfg["heat"] * (1.0 - it / cfg["iters"]) * -math.log(rng.rand() + 1e-12)
+        pl = allot(new, eng)
+        c = None
+        if pl:
+            c, pt = cost(pl, [x + heat + 0.003 * (len(ps) - 1 - y) for y, x in enumerate(parts)])
+        if c is None:
+            eng[i] = old
+        else:
+            order, now, (parts, crit) = new, c, pt
+            if c < low:
+                low, best = c, pl
+    KEPT["low"] = low
+    return best
 
 
 def rank_program(g, core, T, topo):
@@ -521,7 +694,9 @@ def rank_program(g, core, T, topo):
     cnt = dict(P=0, V=0, A=0, G=0)
     know = {e: {} for e in Q}
     tag, clock = {}, {}
-    for i, e, bank, war in schedule(ops, CFG, NOM)[0]:
+    if "plan" not in KEPT:
+        KEPT["plan"] = improve(ops, schedule(ops, CFG, NOM)[0], CFG)
+    for i, e, bank, zb, war in KEPT["plan"]:
         o = ops[i]
         if e == "":
             tag[i] = (o["info"][0], o["info"][1])
@@ -529,7 +704,7 @@ def rank_program(g, core, T, topo):
             continue
         kn = know[e]
         need = {}
-        for d in o["deps"] + ([war] if war is not None else []):
+        for d in o["deps"] + war:
             s, c = tag[d]
             if need.get(s, (0, 0))[0] < c:
                 need[s] = (c, d)
@@ -543,11 +718,13 @@ def rank_program(g, core, T, topo):
         def inc(ins, e=e):
             ins.then_inc(T.sem["e" + e], 1)
             cnt[e] += 1
-        o["fn"](e, T["ps%d" % bank] if bank is not None else None, inc)
+        o["fn"](e, T["ps%d" % bank] if bank is not None else None, inc, 264 * (zb - 8) if zb else 0)
         clock[i] = dict(kn)
         if o["kind"] in ("c", "gat"):
             tag[i] = ("e" + e, cnt[e])
     for e in "PVAG":
         g.sync.wait_ge(T.sem["e" + e], cnt[e])
     g.sync.wait_ge(T.sem["sent"], sent[0])
-    g.sync.wait_ge(T.sem["do"], 64)
+    g.sync.wait_ge(T.sem["do"], 160)
+    if CFG["dup"]:
+        g.sync.wait_ge(T.sem["dup"], 18 * 8)

@@ -4,60 +4,62 @@ from concourse.bass import DstId, RemoteDMATransfer
 from concourse.mybir import AluOpType as OP, ActivationFunctionType as AF
 
 N = 4
-CB = dict(FR=0, F63=192, ID=384, NI=512, SEL=640, NSEL=672, ON=704, NR=832, IR=976, WR=1120, VR=1264, SA=1408, SB=1552,
-          CR=1696, CO=1840, LA=1968, X=2096, SALL=2320, PR=2704)
-CH = dict(ID=0, NI=128, W0=256, W1=288, W2=352, WB=384, NW=416, V1=448, V2=624, H=800)
-WI = dict(PI=0, CAND=8, MOD=24, CO=96, POS=224)
+CB = dict(F63=0, FR=64, ID=256, NI=384, I64=512, SEL=640, NSEL=712, X=784, ON=1024, NR=1152, IR=1296, WR=1440, VR=1584,
+          SA=1728, SB=1872, CR=2016, CR2=2088, CO=2152, PR=2280, QR=2344, BL=2688, CM=3032)
+CH = dict(ID=0, NI=128, W=256, LA=576, NW=704, V1=752, V2=928, H=1104, SALL=2128)
+WI = dict(PI=0, CAND=8, MOD=24, CO=104, POS=232)
 SCRATCH = {
     "tabs": ("sbuf", [128, 8192], "bfloat16"),
-    "cb": ("sbuf", [128, 2736], "bfloat16"),
-    "ch": ("sbuf", [128, 1824], "float16"),
-    "wi": ("sbuf", [128, 2272], "int32"),
-    "wf": ("sbuf", [128, 4096], "float32"),
-    "d1": ("sbuf", [128, 864], "float32"),
-    "tq": ("sbuf", [128, 704], "float32"),
-    "fl": ("sbuf", [128, 1536], "bfloat16"),
-    "dg": ("sbuf", [128, 3072], "bfloat16"),
-    "pos2": ("sbuf", [128, 1536], "bfloat16"),
+    "cb": ("sbuf", [128, 3800], "bfloat16"),
+    "ch": ("sbuf", [128, 2512], "float16"),
+    "wi": ("sbuf", [128, 2280], "int32"),
+    "wf": ("sbuf", [128, 4608], "float32"),
+    "fl": ("sbuf", [128, 3072], "bfloat16"),
+    "pos2": ("sbuf", [128, 4608], "float16"),
     "pz": ("sbuf", [128, 2048], "bfloat16"),
     "pt": ("sbuf", [128, 512], "bfloat16"),
     "zz": ("sbuf", [128, 8 * 1536], "float16"),
     "bb": ("sbuf", [128, 8 * 1536], "float16"),
-    "zi": ("sbuf", [128, 3 * 264], "float16"),
+    "zi": ("sbuf", [128, 3 * 520], "float16"),
     "gat": ("sbuf", [128, 32 * 1024], "bfloat16"),
     "mk": ("sbuf", [128, 3200], "uint16"),
-    "dup": ("sbuf", [128, 1152], "uint16"),
-    "of": ("sbuf", [128, 8], "uint16"),
-    "so": ("sbuf", [128, 1728], "float16"),
-    "si": ("sbuf", [128, 1728], "float16"),
-    "ob": ("sbuf", [128, 512], "float32"),
+    "yy": ("sbuf", [128, 3072], "float16"),
+    "so": ("sbuf", [128, 1536], "float16"),
+    "si": ("sbuf", [128, 1536], "float16"),
 }
 for _b in range(8):
     SCRATCH["ps%d" % _b] = ("psum", [128, 512], "float32")
-SEMAPHORES = (["eP", "eV", "eA", "eG", "sent", "dc", "dp0", "dp1", "dp2", "dp3", "dco", "dt", "do", "sS", "dup"]
+SEMAPHORES = (["eP", "eV", "eA", "eG", "sent", "dc", "dp0", "dp1", "dp2", "dp3", "dco", "dt", "dth", "do", "sS", "left"]
               + ["%s%d%d%d" % (w, a, h, k) for w in "ms" for a in range(3) for h in range(2) for k in range(3)])
 
-CFG = dict(tsplit=1024, slack=0.05, maxd=3, ba=1.0, bo=-2.0, bd=0.0, gs=(1, 1, 2, 2), vb=0.3, tw=1, late=(), bg=6.0, bc=1.0,
-           look=0.35, alpha=0.0, tc=False, seed=1, iters=12000, heat=0.001,
-           mean=1.0, focus=0.7, dup=False)
-NOM = dict(f=1.05, gr=1.5, pc=0.44, pf=0.003, fix=0.052, fixa=0.068, sem=0.1, iss=0.1, st=0.9, row=0.015, bw=12e3, wake=0.3,
-           first=2.8, ldst=1.5, lbw=300e3)
-VARY = [dict(), dict(f=1.0, gr=1.2, st=1.3, iss=0.2), dict(f=1.3, gr=1.9, st=0.6, lbw=400e3, first=1.8, fix=0.065, fixa=0.085),
-        dict(f=1.3, gr=1.3, st=1.4, wake=0.5, first=4.0, lbw=230e3, sem=0.14, fix=0.065, fixa=0.085)]
-LIMIT = dict(L=2, M=2, S=8)
+CFG = dict(tsplit=1024, tsplit2=3328, tw=1, tc=False, late=(), gc=(1, 2), g0=2, gf=(3, 6, 6), go=(1, 2, 2), bm=(0, 0, 0), ab=(0, 1, 1),
+           ug=[[(0,), (1,), (2,)]] * 3, pair=((3,), (0,), (1,), (2,)), pre=1, fill=False, fe=("VA", "VA", "VA"), oe="VA", ce="VA",
+           slack=0.05, maxd=3, ba=3.0, bo=-2.0, bd=0.0, vb=0.0, bg=6.0, bc=2.0, look=0.0, alpha=0.0,
+           pr=dict(own=5, start3=4, start0=4, conv3=1, conv0=4, conv2=3, moves=-5, pairs=-2, pos30=-3, keep00=-5, keep01=-4, keep10=-5,
+                   keep11=-5, keep20=-5, keep21=-4, look10o=4, look11o=4, look20o=4, look21o=9, look30o=4, look31o=7, look21f=-2,
+                   look31f=-2, look30f=2, sum11=2),
+           eb=dict(start2=-1.6, mask11=1.3, keep00=-1.1, sum20=-1.0, turn=0.8, pos21=0.7, mask30=0.6),
+           seed=1, iters=70000, heat=0.001, mean=0.5, focus=0.7)
+NOM = dict(f=1.05, gr=1.5, pc=0.44, pf=0.003, fix=0.033, fixa=0.048, sem=0.19, iss=0.1, st=0.9, row=0.015, bw=12e3, wake=0.3,
+           first=2.8, hold=0.0, ldst=1.5, lbw=300e3)
+VARY = [dict(), dict(f=1.25, gr=1.85, st=0.6, lbw=400e3, first=1.8, fix=0.05, fixa=0.065, sem=0.15),
+        dict(f=1.2, gr=1.25, st=1.4, iss=0.2, wake=0.5, first=3.5, lbw=240e3, sem=0.25, fix=0.04, fixa=0.06),
+        dict(f=1.0, gr=1.3, pc=0.55, st=1.1, iss=0.3, row=0.02, sem=0.28, first=0.5, hold=2.0)]
+LIMIT = dict(L=2, M=2, U=2, S=8)
 KEPT = {}
 
 
 def build(g, T, rank, topo, cfg, NE):
     ops = []
     cur = [-1, -1]
+    name = ["load"]
     Q = {"P": g.tensor, "V": g.vector, "A": g.scalar, "G": g, "S": g.sync}
     V, PE, ACT = g.vector, g.tensor, g.scalar
     top, jobs, sent = [0], [0], [0]
 
     def add(eng, cyc, deps, fn, job=None, cls="S", zj=None, kind="c", n=1, after=(), info=None, cya=None):
         ops.append(dict(id=len(ops), eng=eng, cyc=cyc, cya=cyc if cya is None else cya, deps=[d for d in deps if d is not None],
-                        fn=fn, job=job, cls=cls, zj=zj, kind=kind, n=n, after=list(after), info=info, tag=tuple(cur)))
+                        fn=fn, job=job, cls=cls, zj=zj, kind=kind, n=n, after=list(after), info=info, tag=tuple(cur), name=name[0]))
         return len(ops) - 1
 
     def wa(n):
@@ -90,6 +92,8 @@ def build(g, T, rank, topo, cfg, NE):
             y = o(Z) if "zj" in kw else o
             if e == "V":
                 inc(V.tensor_scalar(y, x, scale, bias, OP.mult, OP.add))
+            elif e == "G":
+                inc(g.affine_select(y, x, [[0, n]], OP.is_ge, 0.0, 0, 0))
             else:
                 inc(ACT.activation(y, x, AF.Identity, bias=bias, scale=scale))
         return add(eng, max(cyv or n, 64), deps, fn, cya=n, **kw)
@@ -114,7 +118,7 @@ def build(g, T, rank, topo, cfg, NE):
 
     def iota(n, deps, o, pat, b, cm, after=()):
         return add("G", 160 + 2 * n, deps, lambda e, P, inc, Z: inc(g.iota(o, pat, b, cm, allow_small_or_imprecise_dtypes=True)),
-                   after=after)
+                   after=after, info="g")
 
     me = T.cores[rank]
     base = 1024 * rank
@@ -145,60 +149,76 @@ def build(g, T, rank, topo, cfg, NE):
     def fsend(e, P, inc, Z):
         g.remote_dma_fused([RemoteDMATransfer(
             dst_ids=[dstid(peer(-1 - k)) for k in range(3)], dma_engine_mask=topo.mask(me, peer(1)), remote_sem=T.sem["sS"],
-            src=wi("CAND", 8, 2), dsts=[wi("CAND", 2 * k, 2) for k in range(3)])], local_sem=T.sem["sent"])
-        sent[0] += NE
-    d = add("G", 0, [l_cand, c_c0], fsend, kind="rem")
+            src=wi("CAND", 8, 2), dsts=[wi("CAND", 2 * k, 2) for k in range(3)])], local_sem=T.sem["left"])
+    name[0] = "const"
+    c_pi = add("G", 162, [], lambda e, P, inc, Z: inc(g.iota(wi("PI"), [[0, 1]], 0, 1)), info="g")
+    c_ir = iota(132, [], cb("IR", 0, 132, 0, 1), [[0, 22], [1, 6]], 0, 0)
+    c_f63 = iota(192, [], cb("F63", 0, 192), [[0, 3], [1, 64]], 0, 0)
+    c_nr = iota(132, [], cb("NR", 0, 132, 0, 1), [[1, 22], [0, 6]], 0, 0)
+    c_vr = iota(144, [], cb("VR", 0, 144, 0, 1), [[1, 3], [2, 8], [0, 6]], 48, 0)
+    c_pr = iota(64, [], cb("PR", 0, 64), [[8, 2], [16, 4], [1, 8]], 0, 0)
+    name[0] = "load"
+    d = add("G", 0, [l_cand, c_c0], fsend, kind="rem", info="first", after=[c_pi, c_ir, c_f63, c_nr, c_vr, c_pr])
     s_arr = add("", 0, [d], None, kind="rarr", info=("sS", 3 * NE, 384 // NE, 8))
-    conv = lambda k: cp(512, [l_pos[k]], T.pz[:, k * 512:k * 512 + 512], wi("POS", k * 512, 512))
+    s_left = add("", 0, [d], None, kind="rarr", info=("left", NE, 0, 0))
+
+    def conv(k):
+        name[0] = "conv%d" % k
+        return aff(512, [l_pos[k]], T.pz[:, k * 512:k * 512 + 512], wi("POS", k * 512, 512), 1.0, 0.0, eng="VAG" if k in cfg["gc"] else "VA")
     cv = {k: conv(k) for k in (3, 0, 1, 2) if k in l_pos}
-    l_tab = ldma("S", [(cv if cfg["tc"] else l_pos)[cfg["tw"]]], "dt", 32, 256 * (8192 - tsp), [(T.tabs[:, tsp:8192], T.tab[:, tsp:8192])], after=[l_t0 - 1, d])
+    ts2 = cfg["tsplit2"]
+    l_t1 = ldma("S", [l_pos[cfg["tw"]]], "dt", 0, 256 * (ts2 - tsp), [(T.tabs[:, tsp:ts2], T.tab[:, tsp:ts2])], after=[l_t0 - 1, d])
+    l_tab = ldma("S", [s_left], "dt", 48, 256 * (8192 - ts2), [(T.tabs[:, ts2:8192], T.tab[:, ts2:8192])], after=[l_t1 - 1])
     last = [l_tab - 1]
     for k in cfg["late"]:
         l_pos[k] = ldpos("S", k, last)
         last = [l_pos[k] - 1]
         cv[k] = conv(k)
 
+    name[0] = "const"
     PC = wa(8); CW = wa(16); CF = wa(8); I32 = wa(128)
-    c_pi = add("G", 162, [], lambda e, P, inc, Z: inc(g.iota(wi("PI"), [[0, 1]], 0, 1)))
-    c_ir = iota(132, [], cb("IR", 0, 132, 0, 1), [[0, 22], [1, 6]], 0, 0)
-    c_f63 = iota(192, [], cb("F63", 0, 192), [[0, 3], [1, 64]], 0, 0)
-    c_fr = iota(192, [], cb("FR", 0, 192), [[1, 192]], -64, 0)
-    c_nr = iota(132, [], cb("NR", 0, 132, 0, 1), [[1, 22], [0, 6]], 0, 0)
-    c_vr = iota(144, [], cb("VR", 0, 144, 0, 1), [[1, 3], [2, 8], [0, 6]], 48, 0)
-    c_pr = iota(32, [], cb("PR", 0, 32), [[8, 2], [16, 2], [1, 8]], 0, 0)
-    c_d1 = iota(864, [], T.d1[:, :], [[0, 864]], -8192, 0, after=[d, c_ir, c_f63, c_fr, c_nr, c_vr, c_pr])
-    c_tq = iota(704, [], T.tq[:, :], [[0, 704]], 0, 0, after=[c_d1])
-    c_cr = iota(144, [], cb("CR", 0, 144, 0, 1), [[0, 72], [1, 2]], -1, 0, after=[c_d1])
-    c_cr = [ms(64, cols(T.cb, CB["CR"] + 33, 4, 36, 0, 1), -1.0, [c_cr])]
+    c_fr = aff(64, [c_f63], cb("FR", 128, 64), cb("F63", 0, 64), 1.0, 64.0, cyv=64)
+    c_qr = [iota(n, [], cb("QR", c, n), pat, 0, 0, after=[d])
+            for c, n, pat in ((0, 256, [[1, 2], [2, 2], [0, 64]]), (256, 68, [[0, 17], [1, 4]]), (324, 16, [[1, 4], [0, 4]]))]
+    c_cr = ms(64, cb("CR", 0, 64, 0, 1), 6144.0)
+    c_cm = ms(384, cb("CM", 0, 768, 64, 96), 1.0)
     c_on = ms(64, cb("ON", 0, 128, 0, 1), 1.0)
-    c_x0 = ms(160, cb("LA", 0, 320), 0.0)
-    c_zi = ms(396, T.zi[:, :], 0.0)
+    c_x0 = ms(168, cb("SEL", 0, 336), 0.0)
+    c_zi = ms(780, T.zi[:, :], 0.0)
+    c_wz = ms(128, ch("W", 192, 256), 0.0)
     bit = lambda c, s, m: ts(64, [c_pi], wi("PI", c), wi("PI"), s, m, OP.logical_shift_right, OP.bitwise_and)
-    pbits = [bit(1, 0, 15), bit(2, 1, 1), bit(3, 2, 3), bit(4, 0, 3)]
-    c_pc = cp(64, pbits, wf(PC, 5), wi("PI", 0, 5))
+    pbits = [bit(1, 0, 15), bit(2, 1, 1), bit(3, 0, 3)]
+    c_p0 = cp(64, [c_pi], wf(PC), wi("PI"))
+    c_pc = cp(64, pbits + [c_p0], wf(PC + 1, 3), wi("PI", 1, 3))
     c_tb = aff(1, [c_pc], wf(PC + 5), wf(PC + 2), 4096.0, 2048.0)
-    c_fb = ts(64, [c_pc], wf(PC + 6), wf(PC), 72.0, 6120.0, OP.is_lt, OP.mult)
-    c_o1 = aff(1, [c_pc], wf(PC + 7), wf(PC + 3), 36.0, 32.0)
-    c_of = [cp(64, pbits, T.of[:, 0:1], wi("PI", 3)), ts(64, [c_o1], T.of[:, 2:3], wf(PC + 7), wf(PC + 4), None, OP.add)]
-    c_i16 = ts(64, [c_pc, c_fr], ch("ID", 0, 128), cb("FR", 64, 128), wf(PC), None, OP.is_equal)
-    eye = lambda o, s: aff(128, [c_i16], o, ch("ID", 0, 128), s, 0.0, cyv=64)
-    c_id, c_ni, c_n16, c_i32 = eye(cb("ID", 0, 128), 1.0), eye(cb("NI", 0, 128), -1.0), eye(ch("NI", 0, 128), -1.0), eye(wf(I32, 128), 1.0)
-    c_sel = [ts(64, [c_pc, c_fr], cb(nm, 0, 18), cb("FR", 64, 18), wf(PC + 1), s, OP.is_equal, OP.mult) for nm, s in (("SEL", 1.0), ("NSEL", -1.0))]
+    up = lambda c: cols(T.wf, c, 1, 1, 64, 128)
+    c_k = ts(64, [c_p0], up(PC + 7), up(PC), 68.0, 9.5 * 128, OP.is_ge, OP.mult)
+    c_k = [ms(64, wf(PC + 6, 1, 1, 64), 128.0), aff(1, [c_k], up(PC + 6), up(PC + 7), 1.0, -128.0)]
+    c_bl = ts(170, c_qr + c_k + [c_pc], cb("BL", 0, 340), cb("QR", 0, 340), wf(PC + 3), wf(PC + 6), OP.is_equal, OP.mult)
+    c_bc = aff(16, [c_bl], cb("QR", 0, 16), cb("BL", 324, 16), 8.0, 0.0)
+    c_i16 = ts(64, [c_p0, c_fr], ch("ID", 0, 128), cb("FR", 64, 128), wf(PC), None, OP.is_equal)
+    eye = lambda o, s, n=128: aff(n, [c_i16], o, ch("ID", 0, n), s, 0.0, cyv=64)
+    c_id, c_n16 = eye(cb("ID", 0, 128), 1.0), eye(ch("NI", 0, 128), -1.0)
+    c_i32 = eye(wf(I32, 64), -1.0, 64)
+    c_sel = [ts(64, [c_pc, c_fr, c_x0], cols(T.cb, CB[nm] + 3, 16, 4), cb("FR", 64, 16), wf(PC + 1), s, OP.is_equal, OP.mult)
+             for nm, s in (("SEL", 1.0), ("NSEL", -1.0))]
     w1 = ts(66, [c_ir], cb("SA", 0, 132, 0, 1), cb("IR", 0, 132, 0, 1), 2.0, 2.0, OP.mult, OP.min)
     w2 = ts(66, [c_ir], cb("SB", 0, 132, 0, 1), cb("IR", 0, 132, 0, 1), 0.0, None, OP.is_equal)
     w3 = vop(66, [w1, w2], lambda P: V.tensor_tensor_scan(cb("WR", 0, 132, 0, 1), cb("SA", 0, 132, 0, 1), cb("SB", 0, 132, 0, 1),
                                                           0.0, OP.mult, OP.add))
-    rows = [(nm, sh) for sh in (0, 2, 4) for nm in ("NR", "WR")] + [("VR", 0)]
-    w4, j = mm([c_nr, c_vr, w3, c_on], lambda P, Z: [(P[:, x:x + 1], cb(nm, sh, 128, 0, 1), cb("ON", 0, 1, 0, 1), True, True)
-                                                     for x, (nm, sh) in enumerate(rows)])
-    w5 = aff(7, [w4], wf(CW, 7), lambda P: P[:, 0:7], 1.0, 0.0, job=j)
-    w6 = ts(64, [w5, c_pc], wf(CW + 7), wf(PC), 64.0, wf(CW + 5), OP.is_ge, OP.mult)
-    w7 = [aff(1, [w5], wf(CW + 8 + x), wf(CW + c), 1.0, b) for x, (c, b) in enumerate(((2, 21.0), (2, -11.0), (4, 10.0)))]
-    wt = lambda nm, c, a, b, d: ts(64, d + [c_pr], ch(nm, c, 32), cb("PR", 0, 32), wf(CW + a), wf(CW + b), OP.is_equal, OP.mult)
-    c_w0, c_w2, c_wb = wt("W0", 0, 0, 1, [w5]), wt("W2", 0, 10, 5, w7), wt("WB", 0, 10, 7, w7 + [w6])
-    c_w1 = [wt("W1", 32 * x, 8 + x, 3, w7) for x in range(2)]
-    c_nw = aff(32, [c_w0], ch("NW", 0, 32), ch("W0", 0, 32), -1.0, 0.0)
-    c_v = [ts(88, [w5, c_f63], ch(nm, 0, 176, 0, 96), cb("F63", 0, 176, 0, 96), wf(CW + 6, 1, 1, 96), s, OP.is_equal, OP.mult)
+
+    def column(deps, rows, c):
+        a, j = mm(deps + [c_on], lambda P, Z: [(P[:, x:x + 1], cb(nm, sh, 128, 0, 1), cb("ON", 0, 1, 0, 1), True, True)
+                                               for x, (nm, sh) in enumerate(rows)])
+        return aff(len(rows), [a], wf(c, len(rows)), lambda P: P[:, 0:len(rows)], 1.0, 0.0, job=j)
+    w5 = column([c_nr, w3], [(nm, sh) for sh in (0, 2, 4) for nm in ("NR", "WR")], CW)
+    w6 = column([c_vr], [("VR", 0)], CW + 6)
+    w7 = [aff(1, [w5], wf(CW + 8 + x), wf(CW + c), 1.0, b) for x, (c, b) in enumerate(((2, 21.0), (4, 42.0), (4, 10.0)))]
+    wt = lambda c, a, b, d, p0=0, p1=128: ts(64, d + [c_pr], ch("W", c, 64, p0, p1), cb("PR", 0, 64, p0, p1), cols(T.wf, CW + a, 1, 1, p0, p1),
+                                             cols(T.wf, CW + b, 1, 1, p0, p1), OP.is_equal, OP.mult)
+    c_w = [wt(0, 0, 1, [w5]), wt(64, 8, 3, w7), wt(128, 9, 5, w7), wt(192, 8, 3, w7 + [c_wz], 0, 64), wt(256, 10, 5, w7 + [c_wz], 64, 128)]
+    c_nw = aff(48, [c_w[0]], ch("NW", 0, 48), ch("W", 0, 48), -1.0, 0.0)
+    c_v = [ts(88, [w6, c_f63], ch(nm, 0, 176, 0, 96), cb("F63", 0, 176, 0, 96), wf(CW + 6, 1, 1, 96), s, OP.is_equal, OP.mult)
            for nm, s in (("V1", 129.0 / 64), ("V2", 2.0))]
 
     h96 = lambda nm, a=0, n=128: ch(nm, a, n, 0, 96)
@@ -213,23 +233,25 @@ def build(g, T, rank, topo, cfg, NE):
 
     def lmat(k, t, o, p0=0, n=128):
         w = 48 - 16 * ((rank + 1 + k) % N)
-        return [(o, x, h96("NW", 16 * t, 8)) for x in (h96("V2", w + p0, n), h96("H", 256 * k + 128 + p0, n))]
+        return [(o, x, h96("NW", 32 * t, 8)) for x in (h96("V2", w + p0, n), h96("H", 256 * k + 128 + p0, n))]
+    name[0] = "own"
     s0 = onehot(3, cp(64, [l_cand], wf(CF + 6, 2, 1, 96), wi("CAND", 8, 2, 0, 96)))
-    s3, j = mm(s0 + c_v + [c_i16], lambda P, Z: smat(3, P[:, 0:96]))
+    s3, j = mm(s0 + c_v[:1] + [c_i16], lambda P, Z: smat(3, P[:, 0:96]))
     s_x = [aff(96, [s3, c_x0], cb("X", 96 * h, 96, 64 * h, 64 * h + 64), lambda P, h=h: P[64 * h:64 * h + 64, 0:96],
                1.0, 0.0, job=j) for h in range(2)]
-    s_all = [aff(96, [s3], cb("SALL", 288, 96), lambda P: P[:, 0:96], 1.0, 0.0, job=j, after=s_x)]
-    s3, j = mm(s0 + c_v + [c_i16, c_nw], lambda P, Z: [(P[:, 0:32], h96("V2"), h96("ID", 96, 32), True, False)] + [
+    s_all = [aff(96, [s3], ch("SALL", 288, 96), lambda P: P[:, 0:96], 1.0, 0.0, job=j, after=s_x)]
+    s3, j = mm(s0 + c_v + [c_i16, c_nw], lambda P, Z: [(cols(P, c, 24), h96("V2"), h96("ID", 96, 24), c == 0, False) for c in (0, 24)] + [
         x + (False, i == 3) for h in range(2) for i, x in enumerate(
-            [y for t in range(2) for y in lmat(3, t, cols(P, 16 * t + 8 * h, 8, 1, 64 * h, 64 * h + 64), 64 * h, 64)])])
-    s_l0 = aff(32, [s3], cb("X", 192, 32), lambda P: P[:, 0:32], 1.0, 0.0, job=j)
+            [y for t in range(2) for y in lmat(3, t, cols(P, 32 * t + 8 * h, 8, 1, 64 * h, 64 * h + 64), 64 * h, 64)])])
+    s_l0 = aff(48, [s3], cb("X", 192, 48), lambda P: P[:, 0:48], 1.0, 0.0, job=j)
+    name[0] = "pairs"
     s1 = cp(64, [s_arr], wf(CF, 6, 1, 96), wi("CAND", 0, 6, 0, 96))
     s1 = [x for k in range(3) for x in onehot(k, s1)] + s0 + c_v + [c_i16, c_nw]
     s3, j = mm(s1, lambda P, Z: [x for k in range(3) for x in smat(k, P[:, 96 * k:96 * k + 96])])
-    s_all.append(aff(288, [s3], cb("SALL", 0, 288), lambda P: P[:, 0:288], 1.0, 0.0, job=j))
-    s3, j = mm(s1, lambda P, Z: [x for k in range(4) for t in range(2) for x in group(
-        lmat(k, t, cols(P, 32 * (k // 2) + 16 * t + 8 * (k % 2), 8)))])
-    s_l = [aff(64, [s3, c_x0], cb("LA", 64 * h, 64, 64 * h, 64 * h + 64), lambda P, h=h: P[64 * h:64 * h + 64, 0:64],
+    s_all.append(aff(288, [s3], ch("SALL", 0, 288), lambda P: P[:, 0:288], 1.0, 0.0, job=j))
+    s3, j = mm(s1, lambda P, Z: group([(cols(P, c, 32), h96("V2"), h96("ID", 96, 32)) for c in (0, 32)] + [
+        (cols(P, 8 * k, 40), x, h96("NW", 0, 40)) for k in range(4) for _, x, _ in lmat(k, 0, None)]))
+    s_l = [aff(64, [s3, c_wz], ch("LA", 64 * h, 64, 64 * h, 64 * h + 64), lambda P, h=h: P[64 * h:64 * h + 64, 0:64],
                1.0, 0.0, job=j) for h in range(2)]
 
     def send(w, grp, hf, k, deps, a, b, nb, after):
@@ -237,14 +259,11 @@ def build(g, T, rank, topo, cfg, NE):
             c = peer(1 + k) if w == "m" else peer(-1 - k)
             g.remote_dma(b, a, T.sem["%s%d%d%d" % (w, grp, hf, k)], T.sem["sent"], topo.addr(c)[1], topo.addr(c)[0], topo.mask(me, c))
             sent[0] += NE
-            if w == "m" and cfg["dup"]:
-                x = ((grp * 2 + hf) * 3 + k) * 64
-                g.remote_dma(T.dup[:, x:x + 64], a, T.sem["dup"], T.sem["sent"], topo.addr(c)[1], topo.addr(c)[0], topo.mask(me, c))
-                sent[0] += NE
-        d = add("G", 0, deps, fn, kind="rem", after=after + [c_tq])
+        d = add("G", 0, deps, fn, kind="rem", after=after + c_qr)
         return add("", 0, [d], None, kind="rarr", info=("%s%d%d%d" % (w, grp, hf, k), NE, 128 // NE, nb))
 
     ptc = []
+    name[0] = "turn"
     qc = lambda q: (q % 2) * 128 + (q // 2) * 64
     for hf in range(2):
         a, j = mm([cv[3], c_id], lambda P, Z, hf=hf: [(
@@ -252,46 +271,53 @@ def build(g, T, rank, topo, cfg, NE):
             cb("ID", 64 * hf, 64, 64 * hf, 64 * hf + 64), True, True) for q in range(4)])
         ptc.append(aff(256, [a], T.pt[:, hf * 256:hf * 256 + 256], lambda P: P[:, 0:256], 1.0 / 64, -0.5, job=j))
     k1 = cp(128, [l_co], cb("CO", 0, 128, 0, 72), wi("CO", 0, 128, 0, 72))
+    l_th = ldma("S", [k1, c_cm], "dth", 96, 6144, [(cb("CM", 128 * x, 128, 64, 68), cb("CO", 0, 128, 48 + 4 * x, 52 + 4 * x)) for x in range(6)],
+                after=[l_tab - 1])
     a0, a1, a2, b0, b1, b2, zr = 0, 8, 16, 24, 32, 40, 80
-    lay = [a0, b0, a0, b0, a1, b1, a1, a1, a2, a2, a2, a2, zr, b1, zr, b2, zr, b2, 48, 56, 64]
-    CO = wa(168); TM = wa(64); R = wa(64); M = wa(64); B0 = wa(8); BS = wa(32); AL = wa(32); DL = wa(32)
+    lay = [a0, b0, a0, b0, a1, b1, a1, a1, a2, a2, a2, a2, zr, b1, zr, b2, zr, b2]
+    CO = wa(144); TM = wa(64); R = wa(64); M = wa(80); B0 = wa(8); B1 = wa(32); XS = wa(32); YS = wa(32)
 
     def moves(x0, x1):
         k2, j = mm([k1, c_id], lambda P, Z: [(P[:, 8 * x:8 * x + 8], cb("CO", 0, 128, 0, 72), cb("ID", lay[x], 8, 0, 72), True, True)
                                              for x in range(x0, x1)])
         return aff(8 * (x1 - x0), [k2], wf(CO + 8 * x0, 8 * (x1 - x0)), lambda P: P[:, 8 * x0:8 * x1], 1.0, 0.0, job=j)
     co0 = moves(0, 2)
-    co = moves(2, 21)
+    name[0] = "moves"
+    co = moves(2, 18)
     r1 = tt(96, [co0, co], wf(TM, 48), wf(CO, 48), wf(CO + 48, 48), OP.mult)
     r1 = tt(96, [r1], wf(R, 48), wf(TM, 48), wf(CO + 96, 48), OP.add)
     r2 = tt(64, [r1], wf(TM + 48, 16), wf(R, 16), wf(CO + 64, 16), OP.mult)
     r2 = tt(64, [r2], wf(R + 48, 16), wf(TM + 48, 16), wf(CO + 112, 16), OP.add)
-    m1 = cp(64, [r2], wi("MOD", 0, 64), wf(R, 64))
-    m2 = ts(64, [m1], wi("MOD", 0, 64), wi("MOD", 0, 64), 63, None, OP.bitwise_and)
-    m3 = cp(64, [m2], wf(M, 64), wi("MOD", 0, 64))
-    c_b0 = aff(8, [co0], wf(B0, 8), wf(CO + 8, 8), 1.0 / 64, 192.0078125)
+    m1 = [aff(64, [r2], wi("MOD", 0, 64), wf(R, 64), 1.0, 32.0, eng="V"),
+          aff(16, [co], wi("MOD", 64, 16), wf(CO + 56, 16), 1.0, 32.0, eng="V")]
+    m2 = ts(80, m1, wi("MOD", 0, 80), wi("MOD", 0, 80), 63, None, OP.bitwise_and)
+    m3 = aff(80, [m2], wf(M, 80), wi("MOD", 0, 80), 1.0, -32.0)
 
-    def choice(deps, out, xa, xb, ya, yb):
-        return [aff(8, deps, out(v), wf(c, 8), s, b) for v, (c, s, b) in enumerate(
-            ((xa, -1.0, -64.0), (ya, 1.0, 0.0), (xb, -1.0 / 64, -64.0078125), (yb, 1.0 / 64, 192.0078125)))]
-    c_t = aff(24, [co, c_d1], cols(T.d1, 0, 24, 36), wf(CO + 144, 24), 129.0, -128.0)
-    lim0 = choice([m3, c_d1], lambda v: cols(T.d1, 32 + v, 8, 36), M, M + 8, CO + 32, CO + 40)
-    bs = choice([m3], lambda v: wf(BS + v, 8, 4), M + 32, M + 40, CO + 64, CO + 120)
-    al = choice([m3], lambda v: wf(AL + v, 8, 4), M + 48, M + 56, M + 16, M + 24)
-    dl = tt(64, bs + al, wf(DL, 32), wf(BS, 32), wf(AL, 32), OP.subtract)
-    lim2 = [ms(64, cols(T.d1, 576 + 32 + v, 8, 36), v - 1.0, [c_d1]) for v in range(2)]
+    def signed(deps, o, c, t, n, step=1):
+        a = ts(64, deps, wf(t, n), wf(c, n, step), 32.0, -64.0, OP.is_gt, OP.mult)
+        return tt(64, [a], wf(o, n, step), wf(c, n, step), wf(t, n), OP.add)
+    quo = lambda deps, o, c, up=0.0: aff(8, deps, o, wf(c, 8), 1.0 / 64, up)
+    name[0] = "turn"
+    c_b0 = [quo([co0], wf(B0, 8), CO + 8), signed([co0], B1 + 16, CO, B1 + 24, 8)]
+    name[0] = "moves"
+    c_b1 = [quo([co], wf(B1, 8), CO + 40), quo([m3], wf(B1 + 8, 8), M + 8)]
+    c_xy = [aff(8, [m3], wf(XS, 8, 4), wf(M + 16, 8), 1.0, 64.0), quo([m3], wf(XS + 1, 8, 4), M + 24, 2.0),
+            aff(8, [m3], wf(XS + 2, 8, 4), wf(M + 48, 8), 1.0, 64.0), quo([m3], wf(XS + 3, 8, 4), M + 56, 2.0),
+            aff(8, [m3], wf(YS, 8, 4), wf(M + 72, 8), 1.0, 0.0), quo([co], wf(YS + 1, 8, 4), CO + 120),
+            aff(8, [m3], wf(YS + 2, 8, 4), wf(M + 32, 8), 1.0, 0.0), quo([m3], wf(YS + 3, 8, 4), M + 40)]
 
-    def positions(o, hf, deps, acol, bcol):
-        ix = (o - 1) * 2 + hf
-        dg = [aff(128, deps + [c_id], T.dg[:, ix * 512 + q * 128:ix * 512 + q * 128 + 128], cb("ID", 0, 128), acol(q), 0.0, cyv=64)
-              for q in range(4)]
-        fl = [aff(64, deps + [ptc[hf]], T.fl[:, ix * 256 + qc(q):ix * 256 + qc(q) + 64], T.pt[:, hf * 256 + qc(q):hf * 256 + qc(q) + 64],
-                  acol(q), bcol(q)) for q in range(4)]
-        c, j = mm(dg + fl + [c_ni], lambda P, Z: [x for y in range(2) for x in (
-            [(P[:, 128 * y:128 * y + 128], T.fl[:, ix * 256 + 128 * y:ix * 256 + 128 * y + 128], cb("NI", 0, 128), True, False)]
-            + [(P[64 * h:64 * h + 64, 128 * y:128 * y + 128], T.pt[:, hf * 256 + qc(2 * h + y):hf * 256 + qc(2 * h + y) + 64],
-                T.dg[:, ix * 512 + (2 * h + y) * 128:ix * 512 + (2 * h + y) * 128 + 128], False, True) for h in range(2)])])
-        return aff(256, [c], T.pos2[:, ix * 256:ix * 256 + 256], lambda P: P[:, 0:256], 64.0, 193.0 * 64, job=j)
+    def positions(o, hf, x, deps, acol, bcol):
+        ix = ((o - 1) * 2 + hf) * 256 + 1536 * x
+        iy = ix % 3072
+        name[0] = "pos%d%d" % (o, hf)
+        ys = [aff(64, deps + [ptc[hf]], cols(T.yy, iy + qc(q), 64), cols(T.pt, hf * 256 + qc(q), 64), acol(q), bcol(q)) for q in range(4)]
+        fl = aff(256, ys, cols(T.fl, iy, 256), cols(T.yy, iy, 256), 1.0, 192.0078125, cyv=128)
+        c, j = mm([fl, c_id, c_n16], lambda P, Z: [x for y in (0, 128) for x in group(
+            [(cols(P, y, 128), cols(T.yy, iy + y, 128), ch("NI", 0, 128)), (cols(P, y, 128), cols(T.fl, iy + y, 128), cb("ID", 0, 128))])])
+        return aff(256, [c], cols(T.pos2, ix, 256), lambda P: P[:, 0:256], -64.0, 192.0 * 64 + 1000, job=j)
+
+    def both(o, hf, deps, aa, ba, ab, bb):
+        return positions(o, hf, 0, deps, aa, ba), positions(o, hf, 1, deps, ab, bb)
 
     def zpass(dep, j, c, n):
         return aff(n, [dep], T.zz[:, c:c + n], lambda P: P[:, 0:n], 1.0, 1536.4921875, job=j, cls="D")
@@ -299,158 +325,187 @@ def build(g, T, rank, topo, cfg, NE):
     def bpass(deps, c, n):
         return ts(n // 2, deps, T.bb[:, c:c + n], T.zz[:, c:c + n], 1538.0, 64.0, OP.is_ge, OP.mult)
 
-    def offsets(dep, j, a):
+    def offsets(dep, j, a, nk):
         zj = newjob()
-        z = [aff(64, [dep, c_zi], lambda Z, t=t: cols(T.zi, Z + 1 + 2 * t, 64, 4), lambda P, t=t: cols(P, 64 * t, 64), 1.0, -98816.0,
-                 job=j, cls="M", zj=zj) for t in range(2)]
-        s, j2 = mm(z + [c_i16], lambda P, Z: [x for k in range(2) for x in group(
+        z = [aff(32 * nk, [dep, c_zi], lambda Z, t=t: cols(T.zi, Z + 1 + 2 * t, 32 * nk, 4), lambda P, t=t: cols(P, 128 * t, 32 * nk),
+                 1.0, -98816.0, job=j, cls="M", zj=zj) for t in range(2)]
+        s, j2 = mm(z + [c_i16], lambda P, Z: [x for k in range(nk) for x in group(
             [(P[:, 64 * k:64 * k + 64], cols(T.zi, Z + 1 + 128 * k - y, 128), ch("ID", 64 * y, 64)) for y in range(2)])], zj=zj)
-        return vop(128, [s, c_tb], lambda P: V.tensor_scalar(T.mk[:, a:a + 128], P[:, 0:128], wf(PC + 5), None, OP.add), job=j2)
+        return aff(64 * nk, [s, c_tb], cols(T.mk, a, 64 * nk), lambda P: cols(P, 0, 64 * nk), 1.0, wf(PC + 5), eng=cfg["oe"], job=j2)
 
     mo = lambda o, hf, k: ((o - 1) * 2 + hf) * 256 + 64 * k
-    mi = lambda o, hf, k: 1536 + 128 * k + 64 * hf if o == 0 else mo(o, hf, 3) if k == 3 else 2048 + ((o - 1) * 2 + hf) * 192 + 64 * k
+    mi = lambda o, hf, k: (1536 + 128 * ((k + 1) % 4) + 64 * hf if o == 0 else mo(o, hf, 3) if k == 3
+                           else 2048 + ((o - 1) * 2 + hf) * 192 + 64 * k)
+    gi = lambda o, hf, k: 16 * (mi(o, hf, k) - 1536) if o == 0 else ((o * 2 + hf) * 4 + k) * 1024
 
     def masks(o, hf, pdep):
         ix = (o - 1) * 2 + hf
-        pc, zc = ix * 256, (2 + ix) * 1536
+        pc, zc = 3072 + ix * 256, (2 + ix) * 1536
+        name[0] = "mask%d%d" % (o, hf)
         zat = lambda tl, h: zc + (512 * h + 256 * tl if tl < 2 else 1024 + 256 * h)
-        zs, bs_ = {}, {}
-        for tls in ((0, 1), (2,)):
-            for h in range(2):
-                a, j = mm([pdep] + s_all, lambda P, Z, tls=tls, h=h: [(
-                    P[:, x * 256:x * 256 + 256], cb("SALL", 128 * tl, 128, 64 * h, 64 * h + 64), T.pos2[64 * h:64 * h + 64, pc:pc + 256],
-                    True, True) for x, tl in enumerate(tls)], cls="D", info="D")
-                z = zpass(a, j, zat(tls[0], h), 256 * len(tls))
-                zs[tls[0], h] = z
-                if len(tls) == 2:
-                    bs_[0, h] = bpass([z], zat(0, h), 512)
-        bs_[2, 0] = bs_[2, 1] = bpass([zs[2, 0], zs[2, 1]], zat(2, 0), 512)
+
+        def differ(tls, h):
+            a, j = mm([pdep] + s_all, lambda P, Z: [(cols(P, 256 * x, 256), ch("SALL", 128 * tl, 128, 64 * h, 64 * h + 64), cols(
+                T.pos2, pc, 256, 1, 64 * h, 64 * h + 64), True, True) for x, tl in enumerate(tls)], cls="D", info="D")
+            return zpass(a, j, zat(tls[0], h), 256 * len(tls))
+        zs = [[differ((0, 1), h)] for h in range(2)]
+        zs.append([differ((2,), h) for h in range(2)])
+        bs_ = [[bpass(zs[0] + zs[1], zc, 1024)]] * 2 if cfg["bm"][o - 1] else [[bpass(zs[h], zat(0, h), 512)] for h in range(2)]
+        bs_.append([bpass(zs[2], zat(2, 0), 512)])
         out = []
-        for gp in range(2):
-            j = newjob()
-            a = None
-            ws = [(0, ch("W0", 0, 32)), (1, ch("W1", 0, 32))] if gp == 0 else [(1, ch("W1", 32, 32)), (2, ch("W2", 0, 32))]
-            parts = [(T.zz, zs, h) for h in range(2)] + [(T.bb, bs_, h) for h in range(2)]
-            for x, (t, dep, h) in enumerate(parts):
-                a, _ = mm([dep[0, h], dep[2 * gp, h], c_w0, c_w2] + c_w1 + s_l, lambda P, Z, x=x, t=t, h=h, ws=ws, gp=gp: [
-                    (cols(P, 2 * q0 + h, 32, 4), u, w, x + q0 + i == 0, x + q0 + i == 5) for q0 in range(2) for i, (u, w) in enumerate(
-                        [(cols(t, zat(tl, h) + q0, 128, 2), w) for tl, w in ws]
-                        + [(cols(T.pos2, pc + q0, 128, 2), cb("LA", 64 * h + 32 * gp, 32))][:x < 2])],
-                    job=j, cls="M", after=[a] if a else [])
-            out.append(offsets(a, j, mo(o, hf, 2 * gp)))
-        return [out[0], out[0], out[1], out[1]]
+        for k0, nk, tls in ((0, 2, (0, 1)), (2, 2, (1, 2))) if cfg["ab"][o - 1] else ((0, 4, (0, 1, 2)),):
+            n = 32 + 8 * nk
+            a, j = mm([pdep, zs[0][0]] + s_l, lambda P, Z, k0=k0, n=n: [
+                (cols(P, 2 * q0 + h, n, 4), cols(T.pos2, pc + q0, 128, 2), ch("LA", 64 * h + 8 * k0, n), h + q0 == 0, False)
+                for h in range(2) for q0 in range(2)], cls="M")
+            parts = [(x, [(tl, x) for tl in tls if tl < 2]) for x in range(2)] + [(2, [(2, 0), (2, 1)])] * (2 in tls)
+            for t, dep in ((T.zz, zs), (T.bb, bs_)):
+                for x, bl in parts:
+                    a, _ = mm(dep[x] + c_w[:3], lambda P, Z, t=t, bl=bl, k0=k0, n=n, end=t is T.bb and x == parts[-1][0]: [
+                        (cols(P, 2 * q0 + h, n, 4), cols(t, zat(tl, h) + q0, 128, 2), ch("W", 64 * tl + 8 * k0, n), False,
+                         end and (tl, h) == bl[-1] and q0 == 1) for tl, h in bl for q0 in range(2)], job=j, cls="M", after=[a])
+            out += [offsets(a, j, mo(o, hf, k0), nk)] * nk
+        return out
 
     def masks0():
         out = {}
-        for k in (3, 0, 1, 2):
-            cur[:] = [0, 0]
-            zc, pc = k * 768, k * 512
-            da, j = mm([cv[k]] + s_x, lambda P, Z, pc=pc: [(P[:, 0:512], cb("X", 0, 128), T.pz[:, pc:pc + 512], True, True)],
-                       cls="D", info="D")
-            za = zpass(da, j, zc, 512)
-            db, j = mm([cv[k]] + s_x, lambda P, Z, pc=pc: [(P[64 * h:64 * h + 64, 0:256], cb("X", 128, 64),
-                       T.pz[:, pc + 256 * h:pc + 256 * h + 256], True, True) for h in range(2)], cls="D", info="D")
-            zb = zpass(db, j, zc + 512, 256)
-            b = bpass([za, zb], zc, 768)
-            a, j = mm([b, c_w0, c_wb, s_l0] + c_w1, lambda P, Z, zc=zc, pc=pc: [x for h in range(2) for q0 in range(2) for x in group(
-                [(cols(P, 2 * q0 + h, 32, 4), cols(t, zc + c + q0, 128, 2), w) for t in (T.zz, T.bb)
-                 for c, w in ((256 * h, ch("W0", 0, 32)), (512, ch("WB" if h else "W1", 0, 32)))]
-                + [(cols(P, 2 * q0 + h, 32, 4), cols(T.pz, pc + 256 * h + q0, 128, 2), cb("X", 192, 32))])], cls="M")
-            out[k] = offsets(a, j, mi(0, 0, k))
+        cur[:] = [0, 0]
+        for pair in cfg["pair"]:
+            jm, a = newjob(), None
+            for x, k in enumerate(pair):
+                zc, pc = k * 768, k * 512
+                name[0] = "start%d" % k
+                da, j = mm([cv[k]] + s_x, lambda P, Z, pc=pc: [(P[:, 0:512], cb("X", 0, 128), T.pz[:, pc:pc + 512], True, True)],
+                           cls="D", info="D")
+                za = zpass(da, j, zc, 512)
+                db, j = mm([cv[k]] + s_x, lambda P, Z, pc=pc: [(P[64 * h:64 * h + 64, 0:256], cb("X", 128, 64),
+                           T.pz[:, pc + 256 * h:pc + 256 * h + 256], True, True) for h in range(2)], cls="D", info="D")
+                zb = zpass(db, j, zc + 512, 256)
+                b = bpass([za, zb], zc, 768)
+
+                def f(P, Z, x=x, zc=zc, pc=pc, end=18 + len(pair) if x + 1 == len(pair) else -1):
+                    l = [(cols(P, 64 * x + 2 * q0 + h, w.shape[1], 4), u, w) for h in range(2) for q0 in range(2) for u, w in (
+                        [(cols(t, zc + c + q0, 128, 2), ch("W", w, 64 - 16 * x)) for t in (T.zz, T.bb) for c, w in ((256 * h, 0), (512, 192 + 64 * h))]
+                        + [(cols(T.pz, pc + 256 * h + q0, 128, 2), cb("X", 192, 48))])]
+                    return [y + (x + i == 0, x + i == end) for i, y in enumerate(l)]
+                a, _ = mm([b, s_l0] + c_w, f, job=jm, cls="M", after=[a] if a else [])
+            out[pair[0]] = out[pair[-1]] = offsets(a, jm, mi(0, 0, pair[0]), 2 * len(pair))
         return out
 
-    def lookup(o, hf, k, dep):
-        a = mi(o, hf, k)
-        gc0 = ((o * 2 + hf) * 4 + k) * 1024
-        n = cfg["gs"][o]
-        w = 64 // n
+    def lookup(o, hf, k, deps, n):
+        a, gc0, w = mi(o, hf, k), gi(o, hf, k), 64 * len(deps) // n
 
         def fg(e, x):
             src = T.tabs[:, 0:8192].indirect(T.mk[:, a + x * w:a + x * w + w])
             dst = T.gat[:, gc0 + 16 * x * w:gc0 + 16 * (x + 1) * w]
             return V.tensor_copy(dst, src) if e == "V" else ACT.activation(dst, src, AF.Copy)
-        return [add("VA", 16 * w, [dep, l_tab], lambda e, P, inc, Z, x=x: inc(fg(e, x)), kind="gat") for x in range(n)]
+        out = [[] for _ in deps]
+        for x in range(n):
+            part = range(x * w // 64, ((x + 1) * w - 1) // 64 + 1)
+            if o == 0:
+                cur[0] = part[0]
+            name[0] = "look%d%d%s" % (o, cur[0], "o" if k == 3 else "f")
+            i = add("VA", 16 * w, [deps[y] for y in part] + [l_tab], lambda e, P, inc, Z, x=x: inc(fg(e, x)), kind="gat")
+            for y in part:
+                out[y].append(i)
+        return out
 
-    def sums(o, hf, k, out, sel="SEL"):
-        gc0 = ((o * 2 + hf) * 4 + k) * 1024
-        return [[(out(q), cols(T.gat, gc0 + 4 * (q // 2) + 2 * t + q % 2, 128, 8), cb(sel, 0, 18)) for t in range(2)] for q in range(4)]
+    scores = lambda o, hf, k, q, t: cols(T.gat, gi(o, hf, k) + 4 * (q // 2) + 2 * t + q % 2, 128, 8)
+
+    def sums(o, hf, k, P, c):
+        return [x for q in range(4) for x in group(
+            [(cols(P, c + q, 16, 4), scores(o, hf, k, q, t), cols(T.cb, CB["SEL"] + 3, 16, 4)) for t in range(2)])]
+
+    def turned(o, hf, P, sel):
+        return [(P[0:64, 0:128], cb(sel, 3 - q, 64), scores(o, hf, 3, q, t)) for q in range(4) for t in range(2)]
 
     mk0 = masks0()
-    i32 = wf(I32, 128)
+    ga0 = {k: lookup(0, 0, k, [mk0[k]] * 2, cfg["g0"]) for k in (3, 0, 1, 2)}
+    open_ = lambda l: [x + (False, False) for x in l]
     for hf in range(2):
         cur[:] = [hf, 1]
-        mk = masks(1, hf, positions(1, hf, [c_b0], lambda q, hf=hf: wf(CO + 4 * hf + q), lambda q, hf=hf: wf(B0 + 4 * hf + q)))
-        tqa = lambda x, hf=hf: (hf * 4 + x) * 88
-        terms, lim = [], lim0 + [c_t]
+        col = lambda c, step=1, hf=hf: (lambda q: wf(c + step * (4 * hf + q)))
+        mk = masks(1, hf, positions(1, hf, 2, c_b0, col(B1 + 16), col(B0)))
+        nxt = both(2, hf, c_b1, col(M + 64), col(B1), col(M), col(B1 + 8))
+        F = fdep = None
+        flags, acs = [], []
         for r in range(3):
             os_ = (0, 1) if r == 0 else (r + 1,)
-            wd = 72 * len(os_)
-            sc = lambda k, r=r, hf=hf, wd=wd: (0, 864, 1296)[r] + (hf * 3 + k) * wd
+            wd = 64 * len(os_)
+            sc = lambda k, r=r, hf=hf, wd=wd: (0, 768, 1152)[r] + (hf * 3 + k) * wd
             arr, sar, prev = {}, {}, []
+            name[0] = "mask%d%d" % (r + 1, hf)
             for k in range(3):
                 a, b = mo(r + 1, hf, k), mi(r + 1, hf, k)
                 arr[k] = send("m", r, hf, k, [mk[k]], T.mk[:, a:a + 64], T.mk[:, b:b + 64], 128, prev)
                 prev = [arr[k] - 1]
-            ga = {k: [x for o in os_ for x in lookup(o, hf, k, mk0[k] if o == 0 else arr[k] if k < 3 else mk[3])] for k in range(4)}
+            ga = lookup(r + 1, hf, 0, [arr[k] for k in range(3)], cfg["gf"][r]) + lookup(r + 1, hf, 3, mk[3:], cfg["go"][r])
+            g0 = [ga0[k][hf] if r == 0 else [] for k in range(4)]
             prev = []
-            for k in range(3):
-                a, j = mm(ga[k] + c_sel, lambda P, Z, k=k, os_=os_, hf=hf: [x for i, o in enumerate(os_) for l in sums(
-                    o, hf, k, lambda q: cols(P, 72 * i + 18 * q, 18)) for x in group(l)])
-                a = aff(wd, [a], cols(T.so, sc(k), wd), lambda P, wd=wd: P[:, 0:wd], 1.0, -2040.0, job=j)
-                sar[k] = send("s", r, hf, k, [a], cols(T.so, sc(k), wd), cols(T.si, sc(k), wd), 2 * wd, prev)
-                prev = [sar[k] - 1]
+            name[0] = "sum%d%d" % (r, hf)
+            for ks in cfg["ug"][r]:
+                j, us = newjob(), []
+                for k in ks:
+                    for i, o in enumerate(os_):
+                        us.append(mm((ga[k] if o else g0[k] + ga[ks[0]]) + c_sel, lambda P, Z, k=k, o=o, hf=hf, c=wd * (k - ks[0]) + 64 * i:
+                                     sums(o, hf, k, P, c), job=j, cls="U")[0])
+                n = wd * len(ks)
+                a = aff(n, us, cols(T.so, sc(ks[0]), n), lambda P, n=n: P[:, 0:n], 1.0, -2048.0, job=j, cls="U")
+                for k in ks:
+                    sar[k] = send("s", r, hf, k, [a], cols(T.so, sc(k), wd), cols(T.si, sc(k), wd), 2 * wd, prev)
+                    prev = [sar[k] - 1]
+            ga[3] = ga[3] + g0[3]
             j = newjob()
-
-            def head(P, Z, r=r, hf=hf, tqa=tqa):
-                l = [(P[:, 0:144], cb("ON", 0, 128, 0, 1), cb("CR", 0, 144, 0, 1))]
-                l += [(cols(P, 1, 72, 2), i32, cols(T.tq, tqa(x), 72)) for x in range(r + 1 if r else 0)]
-                for o, sel in ((1, "SEL"), (0, "NSEL")) if r == 0 else ((r + 1, "SEL"),):
-                    l += [x for y in sums(o, hf, 3, lambda q: cols(P, 36 * q + 1, 18, 2), sel) for x in y]
-                return [(o, a, b, x == 0, False) for x, (o, a, b) in enumerate(l)]
-            a, _ = mm(ga[3] + c_sel + c_cr + [c_on, c_i32] + terms, head, job=j, cls="L", f32=72 * (r + 1) if r else 0)
+            name[0] = "vote%d%d" % (r, hf)
+            a, _ = mm(ga[3] + c_sel, lambda P, Z, r=r, hf=hf: [
+                x + (i == 0, False) for i, x in enumerate(turned(r + 1, hf, P, "SEL"))], job=j, cls="L")
+            if r:
+                a, _ = mm([fdep, c_i32, c_cr, c_on], lambda P, Z, F=F: open_([
+                    (P[0:64, 0:128], wf(I32, 64, 1, 64), wf(F, 128, 1, 64)), (P[0:64, 0:128], cb("CR", 0, 64, 0, 1), cb("ON", 0, 128, 0, 1))]),
+                    job=j, cls="L", f32=128, after=[a])
+            else:
+                a, _ = mm([], lambda P, Z, hf=hf: open_(turned(0, hf, P, "NSEL")), job=j, cls="L", after=[a])
             for k in range(3):
-                a, _ = mm([sar[k], c_n16], lambda P, Z, k=k, r=r, sc=sc, wd=wd: [
-                    (cols(P, 1, 72, 2), ch("NI" if x < wd - 72 else "ID", 0, 128), cols(T.si, sc(k) + x, 72), False, k == 2 and x == wd - 72)
-                    for x in range(0, wd, 72)], job=j, cls="L", after=[a])
-            CM = wa(144); SC = wa(144)
-            cm = vop(144, [a], lambda P, CM=CM: V.tensor_scalar(wf(CM, 144), P[:, 0:144], 0.0, 129.0, OP.is_ge, OP.mult), job=j, cls="L")
-            d1 = cols(T.d1, 288 * r + 144 * hf, 144)
-            sl = vop(144, [cm] + lim, lambda P, CM=CM, SC=SC, d1=d1: V.tensor_tensor_scan(
-                wf(SC, 144), wf(CM, 144), d1, 200.0, OP.subtract, OP.max))
-            tq = tqa(r + 1)
-            if r == 0:
-                f0, j0 = mm(ga[3] + list(sar.values()), lambda P, Z, hf=hf, sc=sc: group(
-                    [(P[:, 0:72], ch("ID", 0, 128), cols(T.si, sc(k), 72)) for k in range(3)]
-                    + [x for y in sums(0, hf, 3, lambda q: cols(P, 18 * q, 18)) for x in y]))
-                terms = [aff(72, [f0, c_tq], cols(T.tq, tqa(0), 72), lambda P: P[:, 0:72], -1.0, 0.0, job=j0)]
+                a, _ = mm([sar[k], c_n16], lambda P, Z, k=k, sc=sc, wd=wd: [
+                    (P[0:64, 0:128], cols(T.si, sc(k) + x, 64), ch("NI" if x < wd - 64 else "ID", 0, 128), False, k == 2 and x == wd - 64)
+                    for x in range(0, wd, 64)], job=j, cls="L", after=[a])
+            CM = cb("CM", 128 * (2 * r + hf), 128, 0, 72)
+            cm = vop(128, [a], lambda P, c=128 * (2 * r + hf): V.tensor_scalar(
+                cb("CM", c, 128, 0, 64), P[0:64, 0:128], 0.0, 0.5, OP.is_ge, OP.subtract), job=j, cls="L")
             if r < 2:
-                fg = ts(64, [sl, c_tq], cols(T.tq, tq + 72 + 4 * r, 4), wf(SC + 33, 4, 36), 64.0, -1.0, OP.is_ge, OP.mult)
-                nf = lambda q, tq=tq, r=r: cols(T.tq, tq + 72 + 4 * r + q, 1)
-                mk = masks(r + 2, hf, positions(r + 2, hf, [sl], lambda q, SC=SC: wf(SC + 36 * q + 33), lambda q, SC=SC: wf(SC + 36 * q + 35)))
-            else:
-                fg = aff(4, [sl, c_tq], cols(T.tq, tq + 80, 4), wf(SC + 34, 4, 36), 1.0, 0.0)
-                nf = lambda q, SC=SC: wf(SC + 36 * q + 34)
-            terms = terms + [fg] + [aff(16, [fg if r < 2 else sl, c_tq], cols(T.tq, tq + 18 * q, 16), lambda P, q=q: cols(P, 36 * q + 1, 16, 2),
-                                        nf(q), 0.0, job=j, cls="L", after=[cm]) for q in range(4)]
+                ix = ((r + 1) * 2 + hf) * 256
+                u, ju = mm([nxt[0], sar[cfg["pre"]]], lambda P, Z, ix=ix: [(P[:, 0:256], ch("ID", 0, 128), cols(T.pos2, ix, 256), True, False)], cls="U")
+                u, ju = mm([cm, c_bl, l_th], lambda P, Z, CM=CM: [(cols(P, y, 128), cb("BL", y, 128, 0, 72), CM, False, y > 0) for y in (0, 128)],
+                           job=ju, cls="U", after=[u])
+                sel = vop(256, [u, nxt[1]], lambda P, ix=ix: V.tensor_tensor(
+                    cols(T.pos2, 3072 + ix, 256), P[:, 0:256], cols(T.pos2, 1536 + ix, 256), OP.min), job=ju, cls="U")
+                mk = masks(r + 2, hf, sel)
+            name[0] = "keep%d%d" % (r, hf)
+            AC = wa(128); TQ = wa(128); FN = wa(128)
+            u, ju = mm([cm, c_bl, l_th], lambda P, Z, CM=CM: [(P[0:68, 0:128], cb("BL", 256, 68, 0, 72), CM, True, True)])
+            ac = vop(128, [u], lambda P, AC=AC: V.tensor_scalar(wf(AC, 128, 1, 68), P[0:68, 0:128], 0.0, None, OP.is_gt), job=ju)
+            flags.append((T.ya[r:r + 1, hf * 512:hf * 512 + 512], T.wf[64:68, AC:AC + 128]))
+            acs.append(ac)
             if r == 0:
-                TP = wa(16)
-                a = tt(64, [fg, dl] + c_of, wf(TP, 16), cols(T.tq, tq + 72, 8).indirect(T.of[:, 0:1]), wf(DL + 16 * hf, 16), OP.mult)
-                lim = [tt(64, [a, c_t], cols(T.d1, 288 + 144 * hf, 144).indirect(T.of[:, 2:3]), wf(TP, 16), wf(BS + 16 * hf, 16), OP.add)]
-            elif r == 1:
-                lim = lim2
-                a, j = mm(terms, lambda P, Z, tqa=tqa: group([(P[0:84, 0:128], cols(T.tq, tqa(x), 84), i32) for x in range(3)]), f32=384)
-                early = aff(128, [a, c_fb], T.ob[0:84, 256 + hf * 128:384 + hf * 128], lambda P: P[0:84, 0:128], -1.0,
-                            wf(PC + 6, 1, 1, 84), job=j)
-            else:
-                a, j = mm(terms[-5:], lambda P, Z, tq=tq: [(P[0:84, 0:128], cols(T.tq, tq, 84), i32, True, True)], f32=128)
-                a = vop(128, [a, early], lambda P, hf=hf: V.tensor_tensor(
-                    T.ob[0:84, hf * 128:hf * 128 + 128], T.ob[0:84, 256 + hf * 128:384 + hf * 128], P[0:84, 0:128], OP.subtract), job=j)
-                prs = [(T.yf[:, hf * 512 + 128 * q:hf * 512 + 128 * q + 128], T.ob[18 * q:18 * q + 16, hf * 128:hf * 128 + 128])
-                       for q in range(4)] + [(T.ya[:, hf * 512:hf * 512 + 512], T.ob[72:84, hf * 128:hf * 128 + 128])]
-                ldma("S", [a], "do", 0, 24576, prs[:3] if hf else prs)
-                if hf:
-                    ldma("A", [a], "do", 0, 14336, prs[3:])
-    assert top[0] <= 4096
+                F = wa(128)
+                f0, j0 = mm(ga[3] + list(sar.values()), lambda P, Z, hf=hf, sc=sc: group(
+                    [(P[0:64, 0:128], cols(T.si, sc(k), 64), ch("ID", 0, 128)) for k in range(3)] + turned(0, hf, P, "SEL")))
+                fdep = aff(128, [f0], wf(F, 128, 1, 64), lambda P: P[0:64, 0:128], 1.0, 6144.0, job=j0)
+                AB = wa(16); TP = wa(16)
+                u, ju = mm([cm, c_bc, l_th], lambda P, Z, CM=CM: [(P[:, 0:16], CM, cb("QR", 0, 16, 0, 72), True, True)])
+                a = vop(64, [u] + c_xy, lambda P, TP=TP, hf=hf: V.tensor_tensor(wf(TP, 16), P[:, 0:16], wf(XS + 16 * hf, 16), OP.min), job=ju)
+                a = tt(64, [a], wf(AB, 16), wf(TP, 16), wf(YS + 16 * hf, 16), OP.max)
+                a = signed([a], AB, AB, TP, 8, 2)
+                at = lambda c: (lambda q: wf(c + 4 * q))
+                nxt = both(3, hf, [a], at(AB), at(AB + 1), at(AB + 2), at(AB + 3))
+                name[0] = "keep%d%d" % (r, hf)
+            a = vop(128, [ac], lambda P, TQ=TQ, AC=AC: V.tensor_tensor(wf(TQ, 128, 1, 64), P[0:64, 0:128], wf(AC, 128, 1, 64), OP.mult),
+                    job=j, cls="L")
+            fdep = tt(256, [a, fdep], wf(FN, 128, 1, 64), wf(F, 128, 1, 64), wf(TQ, 128, 1, 64), OP.add)
+            F = FN
+        ldma("A" if hf else "S", acs, "do", 0, 6144, flags)
+        ldma("S", [fdep], "do", 0, 32768, [(T.yf[:, hf * 512:hf * 512 + 512], wf(F, 128, 1, 64))])
+    assert top[0] <= 4608
     return ops, Q, sent
 
 
@@ -459,16 +514,18 @@ def dur(op, e, p):
     if k == "dma":
         return 0.06 * op["n"]
     if k == "rem":
-        return p["iss"]
+        return p["iss"] + (p["hold"] if op["info"] == "first" else 0.0)
     if e == "P":
         return op["cyc"] * p["pc"] * 1e-3 + p["pf"] * op["n"]
-    c = (op["cya"] if e == "A" else op["cyc"]) * (p["gr"] if k == "gat" else 1.0)
+    c = (op["cya"] if e == "A" else 205 + 2 * op["cyc"] if e == "G" and op["info"] != "g" else op["cyc"]) * (p["gr"] if k == "gat" else 1.0)
     return c * 0.83e-3 * p["f"] + (p["fixa"] if e == "A" else p["fix"])
 
 
 def place(op, e, t0, p, st):
     k = op["kind"]
     if k == "larr":
+        if op["info"][0] == "do":
+            return t0 + p["ldst"] + op["info"][2] / p["lbw"]
         st["dma"] = max(t0 + p["ldst"], st["dma"]) + op["info"][2] / p["lbw"]
         return st["dma"]
     if k == "rarr":
@@ -477,6 +534,82 @@ def place(op, e, t0, p, st):
         st["dma"] = t + op["info"][2] * (p["row"] + op["info"][3] / p["bw"])
         return st["dma"] + p["wake"]
     return t0 + dur(op, e, p)
+
+
+def backfill(ops, cfg, p, succ, uses, pri):
+    n = len(ops)
+    fin, start, eng = [0.0] * n, [0.0] * n, [""] * n
+    busy = {e: [] for e in "PVAGSD"}
+    left = [len(o["deps"]) + len(o["after"]) for o in ops]
+    ready = [i for i in range(n) if left[i] == 0]
+    first = [True]
+
+    def gap(e, t, d):
+        l = busy[e]
+        x = 0
+        while x < len(l) and l[x][0] < t + d:
+            if l[x][1] > t:
+                t = l[x][1]
+            x += 1
+        return t, x
+    while ready:
+        i = max(ready, key=lambda x: pri[x] + 1e3 * (ops[x]["eng"] == ""))
+        ready.remove(i)
+        o = ops[i]
+        t = max([fin[d] + p["sem"] for d in o["deps"]] + [fin[d] for d in o["after"]] + [0.0])
+        if o["eng"] == "":
+            if o["kind"] == "larr":
+                t, d, w = t + p["ldst"], o["info"][2] / p["lbw"], 0.0
+            else:
+                t, d, w = t + p["st"] + p["first"] * first[0], o["info"][2] * (p["row"] + o["info"][3] / p["bw"]), p["wake"]
+                first[0] = False
+            opts = [(0, "D", d) + gap("D", t, d)]
+        else:
+            opts, w = [], 0.0
+            for e in o["eng"]:
+                d = dur(o, e, p) + cfg["pad"]
+                s, x = gap(e, t, d)
+                bias = cfg["eb"].get(o["name"], 0.0) + cfg["vb"] * (o["kind"] == "gat") if e == "V" else 0.0
+                opts.append((s + d + bias, e, d, s, x))
+        _, e, d, s, x = min(opts)
+        busy[e].insert(x, (s, s + d))
+        start[i], fin[i], eng[i] = s, s + d + w, o["eng"] and e
+        for y in succ[i]:
+            left[y] -= 1
+            if left[y] == 0:
+                ready.append(y)
+    todo = sorted((i for i in range(n) if eng[i]), key=lambda x: (start[x], x))
+    limit = dict(LIMIT, D=cfg["maxd"])
+    idle, num, touch = [list(range(8)), [8, 9]], dict(L=0, M=0, S=0, D=0, U=0), [{} for _ in range(11)]
+    at, done, plan = {None: None}, set(), []
+    while todo:
+        for i in todo:
+            o = ops[i]
+            if all(d in done for d in o["deps"] + o["after"]) and (
+                    o["job"] in at or idle[0] and num[o["cls"]] < limit[o["cls"]]) and (o["zj"] in at or idle[1]):
+                break
+        else:
+            raise ValueError("no bank")
+        todo.remove(i)
+        war = []
+        for x, j in enumerate((o["job"], o["zj"])):
+            if j is not None:
+                if j not in at:
+                    at[j] = idle[x].pop(0)
+                    num[o["cls"]] += 1 - x
+                war += [y for e2, y in touch[at[j]].items() if e2 != eng[i]]
+                touch[at[j]][eng[i]] = i
+                uses[j] -= 1
+                if not uses[j]:
+                    idle[x].append(at[j])
+                    num[o["cls"]] -= 1 - x
+        plan.append((i, eng[i], at[o["job"]], at[o["zj"]], war))
+        done.add(i)
+        for y in succ[i]:
+            if ops[y]["eng"] == "":
+                plan.append((y, "", None, None, []))
+                done.add(y)
+    return plan, max(fin)
 
 
 def schedule(ops, cfg, p):
@@ -498,7 +631,9 @@ def schedule(ops, cfg, p):
             c = dur(o, o["eng"][0], p) + p["sem"]
         lev[o["id"]] = c + max([lev[s] for s in succ[o["id"]]] + [0.0])
     pri = [lev[i] + cfg["ba"] * (o["tag"][0] != 1) + cfg["bo"] * (o["tag"][1] != 1) + cfg["bd"] * (o["info"] == "D")
-           - cfg["bg"] * (o["kind"] == "gat") + cfg.get("dp", {}).get(i, 0.0) for i, o in enumerate(ops)]
+           - cfg["bg"] * (o["kind"] == "gat") + cfg["pr"].get(o["name"], 0.0) for i, o in enumerate(ops)]
+    if cfg["fill"]:
+        return backfill(ops, cfg, p, succ, uses, pri)
     fin = [None] * n
     free = dict(P=0.0, V=0.0, A=0.0, G=0.0, S=0.0)
     st = dict(dma=0.0, used=False)
@@ -540,7 +675,7 @@ def schedule(ops, cfg, p):
             for e in o["eng"]:
                 war = [x for b in res if b is not None for e2, x in touch[b].items() if e2 != e]
                 t1 = max([t, free[e]] + [fin[x] + p["sem"] for x in war])
-                key = (t1 + (dur(o, e, p) if len(o["eng"]) > 1 else 0.0) + (cfg["vb"] if e == "V" and o["kind"] == "gat" else 0.0) + (cfg.get("de", {}).get(i, 0.0) if e == "V" else 0.0), e == "V")
+                key = (t1 + (dur(o, e, p) if len(o["eng"]) > 1 else 0.0) + (cfg["vb"] if e == "V" and o["kind"] == "gat" else 0.0) + (cfg["eb"].get(o["name"], 0.0) if e == "V" else 0.0), e == "V")
                 if best is None or key < best[0]:
                     best = (key, t1, e, war)
             cand.append((best[1], i, best[2], res, best[3]))
@@ -583,12 +718,12 @@ def improve(ops, plan, cfg):
     real = lambda i: i if ops[i]["eng"] else ops[i]["deps"][0]
     before = [{real(d) for d in pre[i]} for i in range(n)]
     behind = [{x for s in succ[i] for x in ([s] if ops[s]["eng"] else succ[s])} for i in range(n)]
-    limit = dict(LIMIT, D=3)
+    limit = dict(L=3, M=3, U=3, S=8, D=4)
 
     def allot(order, eng):
         at, left, out = {}, dict(uses), []
         idle = [list(range(8)), [8, 9, 10]]
-        num = dict(L=0, M=0, S=0, D=0)
+        num = dict(L=0, M=0, S=0, D=0, U=0)
         touch = [{} for _ in range(11)]
         for i in order:
             o, e = ops[i], eng[i]
@@ -642,7 +777,8 @@ def improve(ops, plan, cfg):
             i = fin.index(end)
             chain[x] = []
             while i is not None:
-                chain[x].append(real(i))
+                if why[i] is not None and why[i] not in pre[i]:
+                    chain[x].append((why[i], i))
                 i = why[i]
         return tot, (list(part), [i for c in chain for i in c])
     deps = [o["deps"] for o in ops]
@@ -657,20 +793,27 @@ def improve(ops, plan, cfg):
     low = now
     rng = np.random.RandomState(cfg["seed"])
     for it in range(cfg["iters"]):
-        a = order.index(crit[rng.randint(len(crit))]) if rng.rand() < cfg["focus"] else int(rng.randint(len(order)))
+        step = 1 if rng.rand() < 0.5 else -1
+        a = order.index(crit[rng.randint(len(crit))][step < 0]) if rng.rand() < cfg["focus"] else int(rng.randint(len(order)))
         i = order[a]
         new, old = order, eng[i]
         u = rng.rand()
         if len(ops[i]["eng"]) > 1 and u < 0.3:
-            eng[i] = "V" if old == "A" else "A"
+            eng[i] = ops[i]["eng"].replace(old, "")[-1 if u < 0.15 else 0]
         if u > 0.15 or eng[i] == old:
-            step, b, far = (1 if rng.rand() < 0.5 else -1), a, int(rng.choice([1, 1, 2, 3, 6]))
-            stop = behind[i] if step > 0 else before[i]
-            while far and 0 <= b + step < len(order) and order[b + step] not in stop:
+            b, far = a, (1, 1, 1, 2, 3, 5, 8)[rng.randint(7)]
+            tied = set(behind[i] if step > 0 else before[i])
+            take, rest = [i], []
+            while far and 0 <= b + step < len(order):
                 b += step
-                far -= eng[order[b]] == eng[i]
-            new = order[:a] + order[a + 1:]
-            new.insert(b, i)
+                x = order[b]
+                if x in tied:
+                    take.append(x)
+                    tied |= behind[x] if step > 0 else before[x]
+                else:
+                    rest.append(x)
+                    far -= eng[x] == eng[i]
+            new = order[:a] + rest + take + order[b + 1:] if step > 0 else order[:b] + take[::-1] + rest[::-1] + order[a + 1:]
         heat = cfg["heat"] * (1.0 - it / cfg["iters"]) * -math.log(rng.rand() + 1e-12)
         pl = allot(new, eng)
         c = None
@@ -686,6 +829,149 @@ def improve(ops, plan, cfg):
     return best
 
 
+def refine(ops, plan, cfg):
+    n, E, GAP = len(ops), "PVAGS", 24
+    ps = [dict(NOM, **dict(dict(pc=0.417 * v.get("f", NOM["f"])), **v)) for v in VARY]
+    du = [[[dur(o, e, p) if e in o["eng"] else 0.0 for e in E] for o in ops] for p in ps]
+    deps = [o["deps"] for o in ops]
+    pre = [o["deps"] + o["after"] for o in ops]
+    succ, land = [[] for _ in ops], [[] for _ in ops]
+    uses = [0] * (n + 1)
+    for o in ops:
+        for d in pre[o["id"]]:
+            succ[d].append(o["id"])
+        if o["eng"] == "":
+            land[o["deps"][0]].append(o["id"])
+    jobs = [[(x, j) for x, j in enumerate((o["job"], o["zj"])) if j is not None] for o in ops]
+    for l in jobs:
+        for _, j in l:
+            uses[j] += 1
+    before = [{d if ops[d]["eng"] else deps[d][0] for d in pre[i]} for i in range(n)]
+    behind = [{x for s in succ[i] for x in ([s] if ops[s]["eng"] else succ[s])} for i in range(n)]
+
+    def allot(order, eng, a, state, wait):
+        at, left, idle, touch = state[0][:], state[1][:], [state[2][0][:], state[2][1][:]], state[3][:]
+        marks = []
+        for c in range(a, len(order)):
+            if c % GAP == 0:
+                marks.append((at[:], left[:], [idle[0][:], idle[1][:]], touch[:]))
+            i = order[c]
+            w = deps[i]
+            for x, j in jobs[i]:
+                if at[j] < 0:
+                    if not idle[x]:
+                        return None
+                    at[j] = idle[x].pop(0)
+                b, e = 5 * at[j], eng[i]
+                w = w + [y for y in touch[b:b + e] + touch[b + e + 1:b + 5] if y >= 0]
+                touch[b + e] = i
+                left[j] -= 1
+                if not left[j]:
+                    idle[x].append(at[j])
+            wait[i] = w
+        return marks, at
+
+    def run(x, order, eng, a, state, wait, fin):
+        p, d, sem = ps[x], du[x], ps[x]["sem"]
+        free, st = state[0][:], dict(state[1])
+        marks = []
+        for c in range(a, len(order)):
+            if c % GAP == 0:
+                marks.append((free[:], dict(st)))
+            i = order[c]
+            e = eng[i]
+            t = free[e] - sem
+            for y in wait[i]:
+                if fin[y] > t:
+                    t = fin[y]
+            fin[i] = free[e] = t + sem + d[i][e]
+            for s in land[i]:
+                fin[s] = place(ops[s], "", fin[i], p, st)
+        return max(fin) + cfg["mean"] * sum(fin) / n, marks
+
+    def held(order, eng, wait, fins):
+        last, prior, out = [None] * 5, {}, []
+        for i in order:
+            prior[i], last[eng[i]] = last[eng[i]], i
+        for fin, p in zip(fins, ps):
+            i = fin.index(max(fin))
+            while i is not None:
+                if not ops[i]["eng"]:
+                    i = deps[i][0]
+                    continue
+                w = max(wait[i], key=lambda y: fin[y]) if wait[i] else None
+                if prior[i] is not None and (w is None or fin[prior[i]] - p["sem"] >= fin[w]):
+                    w = prior[i]
+                if w is not None and w not in pre[i]:
+                    out.append((w, i))
+                i = w
+        return out
+    order = [x[0] for x in plan if x[1]]
+    eng = {x[0]: E.index(x[1]) for x in plan if x[1]}
+    wait = [None] * n
+    bm, at = allot(order, eng, 0, ([-1] * (n + 1), uses, [list(range(8)), [8, 9, 10]], [-1] * 55), wait)
+    fins = [[0.0] * n for _ in ps]
+    res = [run(x, order, eng, 0, ([0.0] * 5, dict(dma=0.0, used=False)), wait, fins[x]) for x in range(len(ps))]
+    ref = [r[0] for r in res]
+    tm = [r[1] for r in res]
+    parts = [x + 1.0 for x in range(len(ps))]
+    low, best = parts[-1], (order, dict(eng))
+    crit = held(order, eng, wait, fins)
+    rng = np.random.RandomState(cfg["seed"])
+    for it, (u0, u1, u2, u3, u4, u5) in enumerate(rng.rand(cfg["iters"], 6).tolist()):
+        step = 1 if u0 < 0.5 else -1
+        a = order.index(crit[int(u2 * len(crit))][step < 0]) if u1 < cfg["focus"] else int(u2 * len(order))
+        i = order[a]
+        new, old, b = order, eng[i], a
+        if len(ops[i]["eng"]) > 1 and u3 < 0.3:
+            eng[i] = E.index(ops[i]["eng"].replace(E[old], "")[-1 if u3 < 0.15 else 0])
+        if u3 > 0.15 or eng[i] == old:
+            far = (1, 1, 1, 2, 3, 5, 8)[int(u4 * 7)]
+            tied = set(behind[i] if step > 0 else before[i])
+            take, rest = [i], []
+            while far and 0 <= b + step < len(order):
+                b += step
+                x = order[b]
+                if x in tied:
+                    take.append(x)
+                    tied |= behind[x] if step > 0 else before[x]
+                else:
+                    rest.append(x)
+                    far -= eng[x] == eng[i]
+            new = order[:a] + rest + take + order[b + 1:] if step > 0 else order[:b] + take[::-1] + rest[::-1] + order[a + 1:]
+        heat = cfg["heat"] * (1.0 - it / cfg["iters"]) * -math.log(u5 + 1e-12)
+        m = min(a, b) // GAP
+        w2 = wait[:]
+        got = allot(new, eng, m * GAP, bm[m], w2)
+        tot, trial = 0.0, []
+        for x in range(len(ps) if got else 0):
+            fin = fins[x][:]
+            c, marks = run(x, new, eng, m * GAP, tm[x][m], w2, fin)
+            tot += c / ref[x]
+            if tot > parts[x] + heat + 0.003 * (len(ps) - 1 - x):
+                break
+            trial.append((tot, fin, marks))
+        if len(trial) < len(ps):
+            eng[i] = old
+            continue
+        order, wait, bm = new, w2, bm[:m] + got[0]
+        parts, fins = [r[0] for r in trial], [r[1] for r in trial]
+        tm = [tm[x][:m] + trial[x][2] for x in range(len(ps))]
+        if it % 4 == 0:
+            crit = held(order, eng, wait, fins)
+        if tot < low:
+            low, best = tot, (order, dict(eng))
+    order, eng = best
+    at = allot(order, eng, 0, bm[0], wait)[1]
+    KEPT["low"] = low
+    out = []
+    for i in order:
+        o = ops[i]
+        out.append((i, E[eng[i]], o["job"] and at[o["job"]], o["zj"] and at[o["zj"]], wait[i][len(deps[i]):]))
+        out += [(s, "", None, None, []) for s in land[i]]
+    return out
+
+
 def rank_program(g, core, T, topo):
     rank = T.rank_of(core)
     if rank is None:
@@ -695,7 +981,7 @@ def rank_program(g, core, T, topo):
     know = {e: {} for e in Q}
     tag, clock = {}, {}
     if "plan" not in KEPT:
-        KEPT["plan"] = improve(ops, schedule(ops, CFG, NOM)[0], CFG)
+        KEPT["plan"] = refine(ops, schedule(ops, CFG, NOM)[0], CFG)
     for i, e, bank, zb, war in KEPT["plan"]:
         o = ops[i]
         if e == "":
@@ -718,13 +1004,11 @@ def rank_program(g, core, T, topo):
         def inc(ins, e=e):
             ins.then_inc(T.sem["e" + e], 1)
             cnt[e] += 1
-        o["fn"](e, T["ps%d" % bank] if bank is not None else None, inc, 264 * (zb - 8) if zb else 0)
+        o["fn"](e, T["ps%d" % bank] if bank is not None else None, inc, 520 * (zb - 8) if zb else 0)
         clock[i] = dict(kn)
         if o["kind"] in ("c", "gat"):
             tag[i] = ("e" + e, cnt[e])
     for e in "PVAG":
         g.sync.wait_ge(T.sem["e" + e], cnt[e])
     g.sync.wait_ge(T.sem["sent"], sent[0])
-    g.sync.wait_ge(T.sem["do"], 160)
-    if CFG["dup"]:
-        g.sync.wait_ge(T.sem["dup"], 18 * 8)
+    g.sync.wait_ge(T.sem["do"], 128)

import math
import numpy as np
from concourse.bass import DstId, RemoteDMATransfer
from concourse.mybir import AluOpType as OP, ActivationFunctionType as AF

N = 4
CB = dict(F63=0, FR=64, ID=256, NI=384, I64=512, SEL=640, NSEL=712, X=784, ON=1024, NR=1152, IR=1296, WR=1440, VR=1584,
          SA=1728, SB=1872, CR=2016, CR2=2088, CO=2152, PR=2280, QR=2344, BL=2688, CM=3032)
CH = dict(ID=0, NI=128, W=256, LA=576, NW=704, V1=752, V2=928, H=1104, SALL=2128)
WI = dict(PI=0, CAND=8, MOD=24, CO=104, POS=232)
SCRATCH = {
    "tabs": ("sbuf", [128, 8192], "bfloat16"),
    "cb": ("sbuf", [128, 3800], "bfloat16"),
    "ch": ("sbuf", [128, 2512], "float16"),
    "wi": ("sbuf", [128, 2280], "int32"),
    "wf": ("sbuf", [128, 4608], "float32"),
    "fl": ("sbuf", [128, 3072], "bfloat16"),
    "pos2": ("sbuf", [128, 4608], "float16"),
    "pz": ("sbuf", [128, 2048], "bfloat16"),
    "pt": ("sbuf", [128, 512], "bfloat16"),
    "zz": ("sbuf", [128, 8 * 1536], "float16"),
    "bb": ("sbuf", [128, 8 * 1536], "float16"),
    "zi": ("sbuf", [128, 3 * 520], "float16"),
    "gat": ("sbuf", [128, 32 * 1024], "bfloat16"),
    "mk": ("sbuf", [128, 3200], "uint16"),
    "yy": ("sbuf", [128, 3072], "float16"),
    "so": ("sbuf", [128, 1536], "float16"),
    "si": ("sbuf", [128, 1536], "float16"),
}
for _b in range(8):
    SCRATCH["ps%d" % _b] = ("psum", [128, 512], "float32")
SEMAPHORES = (["eP", "eV", "eA", "eG", "sent", "dc", "dp0", "dp1", "dp2", "dp3", "dco", "dt", "dth", "do", "sS", "left"]
              + ["%s%d%d%d" % (w, a, h, k) for w in "ms" for a in range(3) for h in range(2) for k in range(3)])

CFG = dict(tsplit=1024, tsplit2=3328, tw=1, tc=False, late=(), gc=(1, 2), g0=2, gf=(3, 6, 6), go=(1, 2, 2), bm=(0, 0, 0), ab=(0, 1, 1),
           ug=[[(0,), (1,), (2,)]] * 3, pair=((3,), (0,), (1,), (2,)), pre=1, fill=False, fe=("VA", "VA", "VA"), oe="VA", ce="VA",
           slack=0.05, maxd=3, ba=3.0, bo=-2.0, bd=0.0, vb=0.0, bg=6.0, bc=2.0, look=0.0, alpha=0.0,
           pr=dict(own=5, start3=4, start0=4, conv3=1, conv0=4, conv2=3, moves=-5, pairs=-2, pos30=-3, keep00=-5, keep01=-4, keep10=-5,
                   keep11=-5, keep20=-5, keep21=-4, look10o=4, look11o=4, look20o=4, look21o=9, look30o=4, look31o=7, look21f=-2,
                   look31f=-2, look30f=2, sum11=2),
           eb=dict(start2=-1.6, mask11=1.3, keep00=-1.1, sum20=-1.0, turn=0.8, pos21=0.7, mask30=0.6),
           seed=1, iters=70000, heat=0.001, mean=0.5, focus=0.7)
NOM = dict(f=1.05, gr=1.5, pc=0.44, pf=0.003, fix=0.033, fixa=0.048, sem=0.19, iss=0.1, st=0.9, row=0.015, bw=12e3, wake=0.3,
           first=2.8, hold=0.0, ldst=1.5, lbw=300e3)
VARY = [dict(), dict(f=1.25, gr=1.85, st=0.6, lbw=400e3, first=1.8, fix=0.05, fixa=0.065, sem=0.15),
        dict(f=1.2, gr=1.25, st=1.4, iss=0.2, wake=0.5, first=3.5, lbw=240e3, sem=0.25, fix=0.04, fixa=0.06),
        dict(f=1.0, gr=1.3, pc=0.55, st=1.1, iss=0.3, row=0.02, sem=0.28, first=0.5, hold=2.0)]
LIMIT = dict(L=2, M=2, U=2, S=8)
KEPT = {}


def build(g, T, rank, topo, cfg, NE):
    ops = []
    cur = [-1, -1]
    name = ["load"]
    Q = {"P": g.tensor, "V": g.vector, "A": g.scalar, "G": g, "S": g.sync}
    V, PE, ACT = g.vector, g.tensor, g.scalar
    top, jobs, sent = [0], [0], [0]

    def add(eng, cyc, deps, fn, job=None, cls="S", zj=None, kind="c", n=1, after=(), info=None, cya=None):
        ops.append(dict(id=len(ops), eng=eng, cyc=cyc, cya=cyc if cya is None else cya, deps=[d for d in deps if d is not None],
                        fn=fn, job=job, cls=cls, zj=zj, kind=kind, n=n, after=list(after), info=info, tag=tuple(cur), name=name[0]))
        return len(ops) - 1

    def wa(n):
        top[0] += (n + 7) // 8 * 8
        return top[0] - (n + 7) // 8 * 8

    def newjob():
        jobs[0] += 1
        return jobs[0]

    def cols(t, a, n, step=1, p0=0, p1=128):
        return t[p0:p1, a:a + (n - 1) * step + 1:step] if step > 1 else t[p0:p1, a:a + n]

    cb = lambda name, a=0, n=1, p0=0, p1=128: cols(T.cb, CB[name] + a, n, 1, p0, p1)
    ch = lambda name, a=0, n=1, p0=0, p1=128: cols(T.ch, CH[name] + a, n, 1, p0, p1)
    wi = lambda name, a=0, n=1, p0=0, p1=128: cols(T.wi, WI[name] + a, n, 1, p0, p1)
    wf = lambda a, n=1, step=1, p1=128: cols(T.wf, a, n, step, 0, p1)

    def vop(cyc, deps, fn, **kw):
        return add("V", max(cyc, 64), deps, lambda e, P, inc, Z: inc(fn(P)), **kw)

    ts = lambda cyc, deps, *a: vop(cyc, deps, lambda P: V.tensor_scalar(*a))
    tt = lambda cyc, deps, *a: vop(cyc, deps, lambda P: V.tensor_tensor(*a))
    cp = lambda cyc, deps, o, i: vop(cyc, deps, lambda P: V.tensor_copy(o, i))
    ms = lambda cyc, o, c, deps=(): vop(cyc, list(deps), lambda P: V.memset(o, c))

    def aff(n, deps, o, i, scale, bias, eng="VA", cyv=None, **kw):
        def fn(e, P, inc, Z):
            x = i(P) if "job" in kw else i
            y = o(Z) if "zj" in kw else o
            if e == "V":
                inc(V.tensor_scalar(y, x, scale, bias, OP.mult, OP.add))
            elif e == "G":
                inc(g.affine_select(y, x, [[0, n]], OP.is_ge, 0.0, 0, 0))
            else:
                inc(ACT.activation(y, x, AF.Identity, bias=bias, scale=scale))
        return add(eng, max(cyv or n, 64), deps, fn, cya=n, **kw)

    def mm(deps, lst, job=None, f32=0, **kw):
        j = job or newjob()

        def fn(e, P, inc, Z):
            for a in lst(P, Z):
                i = PE.matmul(*a)
            inc(i)
        l = lst(T.ps0, 0)
        return add("P", sum(max(64, a[2].shape[1]) for a in l) + 3 * f32, deps, fn, job=j, n=len(l), **kw), j

    def group(l):
        return [(o, a, b, x == 0, x == len(l) - 1) for x, (o, a, b) in enumerate(l)]

    def ldma(q, deps, sem, cnt, nbytes, prs, after=()):
        d = add(q, 0, deps, lambda e, P, inc, Z: [Q[e].dma_start(o, i).then_inc(T.sem[sem], 16) for o, i in prs],
                kind="dma", n=len(prs), after=after)
        return add("", 0, [d], None, kind="larr", info=(sem, cnt, nbytes))

    def iota(n, deps, o, pat, b, cm, after=()):
        return add("G", 160 + 2 * n, deps, lambda e, P, inc, Z: inc(g.iota(o, pat, b, cm, allow_small_or_imprecise_dtypes=True)),
                   after=after, info="g")

    me = T.cores[rank]
    base = 1024 * rank
    peer = lambda d: T.cores[(rank + d) % N]
    dstid = lambda c: DstId(rid=topo.addr(c)[0], pnc=topo.addr(c)[1])

    for a in range(2):
        l_cand = ldma("AS"[a], [], "dc", 64, 60000, [(wi("CAND", 8 + a, 1, 48 * t, 48 * t + 48), T.cand[:, 12 * t + 6 * a:12 * t + 6 * a + 6])
                                                     for t in range(2)], after=[0] if a else [])

    def ldpos(q, k, after):
        c0 = 1024 * ((rank - 1 - k) % N)
        return ldma(q, [], "dp%d" % k, 32, 262144, [(wi("POS", k * 512, 512, 64 * hf, 64 * hf + 64),
                    T.pos0[:, c0 + hf * 512:c0 + hf * 512 + 512]) for hf in range(2)], after=after)
    l_pos = {3: ldpos("A", 3, [l_cand - 1])}
    l_co = ldma("S", [], "dco", 48, 36864, [(wi("CO", 0, 128, 24 * a, 24 * a + 24), t[:, base:base + 1024])
                                            for a, t in enumerate((T.fac, T.inc, T.th))], after=[l_cand - 1])
    last = [l_co - 1, l_pos[3] - 1]
    for k in range(3):
        if k not in cfg["late"]:
            l_pos[k] = ldpos("AS"[k % 2], k, last)
            last = last + [l_pos[k] - 1]
    tsp = cfg["tsplit"]
    l_t0 = ldma("S", [], "dt", 0, 256 * tsp, [(T.tabs[:, 0:tsp], T.tab[:, 0:tsp])], after=last)

    c_c0 = ms(64, wi("CAND", 8, 2, 96, 128), 0)

    def fsend(e, P, inc, Z):
        g.remote_dma_fused([RemoteDMATransfer(
            dst_ids=[dstid(peer(-1 - k)) for k in range(3)], dma_engine_mask=topo.mask(me, peer(1)), remote_sem=T.sem["sS"],
            src=wi("CAND", 8, 2), dsts=[wi("CAND", 2 * k, 2) for k in range(3)])], local_sem=T.sem["left"])
    name[0] = "const"
    c_pi = add("G", 162, [], lambda e, P, inc, Z: inc(g.iota(wi("PI"), [[0, 1]], 0, 1)), info="g")
    c_ir = iota(132, [], cb("IR", 0, 132, 0, 1), [[0, 22], [1, 6]], 0, 0)
    c_f63 = iota(192, [], cb("F63", 0, 192), [[0, 3], [1, 64]], 0, 0)
    c_nr = iota(132, [], cb("NR", 0, 132, 0, 1), [[1, 22], [0, 6]], 0, 0)
    c_vr = iota(144, [], cb("VR", 0, 144, 0, 1), [[1, 3], [2, 8], [0, 6]], 48, 0)
    c_pr = iota(64, [], cb("PR", 0, 64), [[8, 2], [16, 4], [1, 8]], 0, 0)
    name[0] = "load"
    d = add("G", 0, [l_cand, c_c0], fsend, kind="rem", info="first", after=[c_pi, c_ir, c_f63, c_nr, c_vr, c_pr])
    s_arr = add("", 0, [d], None, kind="rarr", info=("sS", 3 * NE, 384 // NE, 8))
    s_left = add("", 0, [d], None, kind="rarr", info=("left", NE, 0, 0))

    def conv(k):
        name[0] = "conv%d" % k
        return aff(512, [l_pos[k]], T.pz[:, k * 512:k * 512 + 512], wi("POS", k * 512, 512), 1.0, 0.0, eng="VAG" if k in cfg["gc"] else "VA")
    cv = {k: conv(k) for k in (3, 0, 1, 2) if k in l_pos}
    ts2 = cfg["tsplit2"]
    l_t1 = ldma("S", [l_pos[cfg["tw"]]], "dt", 0, 256 * (ts2 - tsp), [(T.tabs[:, tsp:ts2], T.tab[:, tsp:ts2])], after=[l_t0 - 1, d])
    l_tab = ldma("S", [s_left], "dt", 48, 256 * (8192 - ts2), [(T.tabs[:, ts2:8192], T.tab[:, ts2:8192])], after=[l_t1 - 1])
    last = [l_tab - 1]
    for k in cfg["late"]:
        l_pos[k] = ldpos("S", k, last)
        last = [l_pos[k] - 1]
        cv[k] = conv(k)

    name[0] = "const"
    PC = wa(8); CW = wa(16); CF = wa(8); I32 = wa(128)
    c_fr = aff(64, [c_f63], cb("FR", 128, 64), cb("F63", 0, 64), 1.0, 64.0, cyv=64)
    c_qr = [iota(n, [], cb("QR", c, n), pat, 0, 0, after=[d])
            for c, n, pat in ((0, 256, [[1, 2], [2, 2], [0, 64]]), (256, 68, [[0, 17], [1, 4]]), (324, 16, [[1, 4], [0, 4]]))]
    c_cr = ms(64, cb("CR", 0, 64, 0, 1), 6144.0)
    c_cm = ms(384, cb("CM", 0, 768, 64, 96), 1.0)
    c_on = ms(64, cb("ON", 0, 128, 0, 1), 1.0)
    c_x0 = ms(168, cb("SEL", 0, 336), 0.0)
    c_zi = ms(780, T.zi[:, :], 0.0)
    c_wz = ms(128, ch("W", 192, 256), 0.0)
    bit = lambda c, s, m: ts(64, [c_pi], wi("PI", c), wi("PI"), s, m, OP.logical_shift_right, OP.bitwise_and)
    pbits = [bit(1, 0, 15), bit(2, 1, 1), bit(3, 0, 3)]
    c_p0 = cp(64, [c_pi], wf(PC), wi("PI"))
    c_pc = cp(64, pbits + [c_p0], wf(PC + 1, 3), wi("PI", 1, 3))
    c_tb = aff(1, [c_pc], wf(PC + 5), wf(PC + 2), 4096.0, 2048.0)
    up = lambda c: cols(T.wf, c, 1, 1, 64, 128)
    c_k = ts(64, [c_p0], up(PC + 7), up(PC), 68.0, 9.5 * 128, OP.is_ge, OP.mult)
    c_k = [ms(64, wf(PC + 6, 1, 1, 64), 128.0), aff(1, [c_k], up(PC + 6), up(PC + 7), 1.0, -128.0)]
    c_bl = ts(170, c_qr + c_k + [c_pc], cb("BL", 0, 340), cb("QR", 0, 340), wf(PC + 3), wf(PC + 6), OP.is_equal, OP.mult)
    c_bc = aff(16, [c_bl], cb("QR", 0, 16), cb("BL", 324, 16), 8.0, 0.0)
    c_i16 = ts(64, [c_p0, c_fr], ch("ID", 0, 128), cb("FR", 64, 128), wf(PC), None, OP.is_equal)
    eye = lambda o, s, n=128: aff(n, [c_i16], o, ch("ID", 0, n), s, 0.0, cyv=64)
    c_id, c_n16 = eye(cb("ID", 0, 128), 1.0), eye(ch("NI", 0, 128), -1.0)
    c_i32 = eye(wf(I32, 64), -1.0, 64)
    c_sel = [ts(64, [c_pc, c_fr, c_x0], cols(T.cb, CB[nm] + 3, 16, 4), cb("FR", 64, 16), wf(PC + 1), s, OP.is_equal, OP.mult)
             for nm, s in (("SEL", 1.0), ("NSEL", -1.0))]
    w1 = ts(66, [c_ir], cb("SA", 0, 132, 0, 1), cb("IR", 0, 132, 0, 1), 2.0, 2.0, OP.mult, OP.min)
    w2 = ts(66, [c_ir], cb("SB", 0, 132, 0, 1), cb("IR", 0, 132, 0, 1), 0.0, None, OP.is_equal)
    w3 = vop(66, [w1, w2], lambda P: V.tensor_tensor_scan(cb("WR", 0, 132, 0, 1), cb("SA", 0, 132, 0, 1), cb("SB", 0, 132, 0, 1),
                                                          0.0, OP.mult, OP.add))

    def column(deps, rows, c):
        a, j = mm(deps + [c_on], lambda P, Z: [(P[:, x:x + 1], cb(nm, sh, 128, 0, 1), cb("ON", 0, 1, 0, 1), True, True)
                                               for x, (nm, sh) in enumerate(rows)])
        return aff(len(rows), [a], wf(c, len(rows)), lambda P: P[:, 0:len(rows)], 1.0, 0.0, job=j)
    w5 = column([c_nr, w3], [(nm, sh) for sh in (0, 2, 4) for nm in ("NR", "WR")], CW)
    w6 = column([c_vr], [("VR", 0)], CW + 6)
    w7 = [aff(1, [w5], wf(CW + 8 + x), wf(CW + c), 1.0, b) for x, (c, b) in enumerate(((2, 21.0), (4, 42.0), (4, 10.0)))]
    wt = lambda c, a, b, d, p0=0, p1=128: ts(64, d + [c_pr], ch("W", c, 64, p0, p1), cb("PR", 0, 64, p0, p1), cols(T.wf, CW + a, 1, 1, p0, p1),
                                             cols(T.wf, CW + b, 1, 1, p0, p1), OP.is_equal, OP.mult)
    c_w = [wt(0, 0, 1, [w5]), wt(64, 8, 3, w7), wt(128, 9, 5, w7), wt(192, 8, 3, w7 + [c_wz], 0, 64), wt(256, 10, 5, w7 + [c_wz], 64, 128)]
    c_nw = aff(48, [c_w[0]], ch("NW", 0, 48), ch("W", 0, 48), -1.0, 0.0)
    c_v = [ts(88, [w6, c_f63], ch(nm, 0, 176, 0, 96), cb("F63", 0, 176, 0, 96), wf(CW + 6, 1, 1, 96), s, OP.is_equal, OP.mult)
           for nm, s in (("V1", 129.0 / 64), ("V2", 2.0))]

    h96 = lambda nm, a=0, n=128: ch(nm, a, n, 0, 96)

    def onehot(k, dep):
        return [ts(64, [dep, c_f63], h96("H", 256 * k + 128 * a), cb("F63", 0, 128, 0, 96), wf(CF + 2 * k + a, 1, 1, 96), s,
                   OP.is_equal, OP.mult) for a, s in ((0, -1.0 / 64), (1, -2.0))]

    def smat(k, o):
        w = 48 - 16 * ((rank + 1 + k) % N)
        return group([(o, x, h96("ID", 0, 96)) for x in (h96("V1", w), h96("H", 256 * k), h96("H", 256 * k + 128))])

    def lmat(k, t, o, p0=0, n=128):
        w = 48 - 16 * ((rank + 1 + k) % N)
        return [(o, x, h96("NW", 32 * t, 8)) for x in (h96("V2", w + p0, n), h96("H", 256 * k + 128 + p0, n))]
    name[0] = "own"
    s0 = onehot(3, cp(64, [l_cand], wf(CF + 6, 2, 1, 96), wi("CAND", 8, 2, 0, 96)))
    s3, j = mm(s0 + c_v[:1] + [c_i16], lambda P, Z: smat(3, P[:, 0:96]))
    s_x = [aff(96, [s3, c_x0], cb("X", 96 * h, 96, 64 * h, 64 * h + 64), lambda P, h=h: P[64 * h:64 * h + 64, 0:96],
               1.0, 0.0, job=j) for h in range(2)]
    s_all = [aff(96, [s3], ch("SALL", 288, 96), lambda P: P[:, 0:96], 1.0, 0.0, job=j, after=s_x)]
    s3, j = mm(s0 + c_v + [c_i16, c_nw], lambda P, Z: [(cols(P, c, 24), h96("V2"), h96("ID", 96, 24), c == 0, False) for c in (0, 24)] + [
        x + (False, i == 3) for h in range(2) for i, x in enumerate(
            [y for t in range(2) for y in lmat(3, t, cols(P, 32 * t + 8 * h, 8, 1, 64 * h, 64 * h + 64), 64 * h, 64)])])
    s_l0 = aff(48, [s3], cb("X", 192, 48), lambda P: P[:, 0:48], 1.0, 0.0, job=j)
    name[0] = "pairs"
    s1 = cp(64, [s_arr], wf(CF, 6, 1, 96), wi("CAND", 0, 6, 0, 96))
    s1 = [x for k in range(3) for x in onehot(k, s1)] + s0 + c_v + [c_i16, c_nw]
    s3, j = mm(s1, lambda P, Z: [x for k in range(3) for x in smat(k, P[:, 96 * k:96 * k + 96])])
    s_all.append(aff(288, [s3], ch("SALL", 0, 288), lambda P: P[:, 0:288], 1.0, 0.0, job=j))
    s3, j = mm(s1, lambda P, Z: group([(cols(P, c, 32), h96("V2"), h96("ID", 96, 32)) for c in (0, 32)] + [
        (cols(P, 8 * k, 40), x, h96("NW", 0, 40)) for k in range(4) for _, x, _ in lmat(k, 0, None)]))
    s_l = [aff(64, [s3, c_wz], ch("LA", 64 * h, 64, 64 * h, 64 * h + 64), lambda P, h=h: P[64 * h:64 * h + 64, 0:64],
               1.0, 0.0, job=j) for h in range(2)]

    def send(w, grp, hf, k, deps, a, b, nb, after):
        def fn(e, P, inc, Z):
            c = peer(1 + k) if w == "m" else peer(-1 - k)
            g.remote_dma(b, a, T.sem["%s%d%d%d" % (w, grp, hf, k)], T.sem["sent"], topo.addr(c)[1], topo.addr(c)[0], topo.mask(me, c))
            sent[0] += NE
        d = add("G", 0, deps, fn, kind="rem", after=after + c_qr)
        return add("", 0, [d], None, kind="rarr", info=("%s%d%d%d" % (w, grp, hf, k), NE, 128 // NE, nb))

    ptc = []
    name[0] = "turn"
    qc = lambda q: (q % 2) * 128 + (q // 2) * 64
    for hf in range(2):
        a, j = mm([cv[3], c_id], lambda P, Z, hf=hf: [(
            P[:, qc(q):qc(q) + 64], T.pz[64 * hf:64 * hf + 64, 1536 + q * 128:1536 + q * 128 + 128],
            cb("ID", 64 * hf, 64, 64 * hf, 64 * hf + 64), True, True) for q in range(4)])
        ptc.append(aff(256, [a], T.pt[:, hf * 256:hf * 256 + 256], lambda P: P[:, 0:256], 1.0 / 64, -0.5, job=j))
    k1 = cp(128, [l_co], cb("CO", 0, 128, 0, 72), wi("CO", 0, 128, 0, 72))
    l_th = ldma("S", [k1, c_cm], "dth", 96, 6144, [(cb("CM", 128 * x, 128, 64, 68), cb("CO", 0, 128, 48 + 4 * x, 52 + 4 * x)) for x in range(6)],
                after=[l_tab - 1])
    a0, a1, a2, b0, b1, b2, zr = 0, 8, 16, 24, 32, 40, 80
    lay = [a0, b0, a0, b0, a1, b1, a1, a1, a2, a2, a2, a2, zr, b1, zr, b2, zr, b2]
    CO = wa(144); TM = wa(64); R = wa(64); M = wa(80); B0 = wa(8); B1 = wa(32); XS = wa(32); YS = wa(32)

    def moves(x0, x1):
        k2, j = mm([k1, c_id], lambda P, Z: [(P[:, 8 * x:8 * x + 8], cb("CO", 0, 128, 0, 72), cb("ID", lay[x], 8, 0, 72), True, True)
                                             for x in range(x0, x1)])
        return aff(8 * (x1 - x0), [k2], wf(CO + 8 * x0, 8 * (x1 - x0)), lambda P: P[:, 8 * x0:8 * x1], 1.0, 0.0, job=j)
    co0 = moves(0, 2)
    name[0] = "moves"
    co = moves(2, 18)
    r1 = tt(96, [co0, co], wf(TM, 48), wf(CO, 48), wf(CO + 48, 48), OP.mult)
    r1 = tt(96, [r1], wf(R, 48), wf(TM, 48), wf(CO + 96, 48), OP.add)
    r2 = tt(64, [r1], wf(TM + 48, 16), wf(R, 16), wf(CO + 64, 16), OP.mult)
    r2 = tt(64, [r2], wf(R + 48, 16), wf(TM + 48, 16), wf(CO + 112, 16), OP.add)
    m1 = [aff(64, [r2], wi("MOD", 0, 64), wf(R, 64), 1.0, 32.0, eng="V"),
          aff(16, [co], wi("MOD", 64, 16), wf(CO + 56, 16), 1.0, 32.0, eng="V")]
    m2 = ts(80, m1, wi("MOD", 0, 80), wi("MOD", 0, 80), 63, None, OP.bitwise_and)
    m3 = aff(80, [m2], wf(M, 80), wi("MOD", 0, 80), 1.0, -32.0)

    def signed(deps, o, c, t, n, step=1):
        a = ts(64, deps, wf(t, n), wf(c, n, step), 32.0, -64.0, OP.is_gt, OP.mult)
        return tt(64, [a], wf(o, n, step), wf(c, n, step), wf(t, n), OP.add)
    quo = lambda deps, o, c, up=0.0: aff(8, deps, o, wf(c, 8), 1.0 / 64, up)
    name[0] = "turn"
    c_b0 = [quo([co0], wf(B0, 8), CO + 8), signed([co0], B1 + 16, CO, B1 + 24, 8)]
    name[0] = "moves"
    c_b1 = [quo([co], wf(B1, 8), CO + 40), quo([m3], wf(B1 + 8, 8), M + 8)]
    c_xy = [aff(8, [m3], wf(XS, 8, 4), wf(M + 16, 8), 1.0, 64.0), quo([m3], wf(XS + 1, 8, 4), M + 24, 2.0),
            aff(8, [m3], wf(XS + 2, 8, 4), wf(M + 48, 8), 1.0, 64.0), quo([m3], wf(XS + 3, 8, 4), M + 56, 2.0),
            aff(8, [m3], wf(YS, 8, 4), wf(M + 72, 8), 1.0, 0.0), quo([co], wf(YS + 1, 8, 4), CO + 120),
            aff(8, [m3], wf(YS + 2, 8, 4), wf(M + 32, 8), 1.0, 0.0), quo([m3], wf(YS + 3, 8, 4), M + 40)]

    def positions(o, hf, x, deps, acol, bcol):
        ix = ((o - 1) * 2 + hf) * 256 + 1536 * x
        iy = ix % 3072
        name[0] = "pos%d%d" % (o, hf)
        ys = [aff(64, deps + [ptc[hf]], cols(T.yy, iy + qc(q), 64), cols(T.pt, hf * 256 + qc(q), 64), acol(q), bcol(q)) for q in range(4)]
        fl = aff(256, ys, cols(T.fl, iy, 256), cols(T.yy, iy, 256), 1.0, 192.0078125, cyv=128)
        c, j = mm([fl, c_id, c_n16], lambda P, Z: [x for y in (0, 128) for x in group(
            [(cols(P, y, 128), cols(T.yy, iy + y, 128), ch("NI", 0, 128)), (cols(P, y, 128), cols(T.fl, iy + y, 128), cb("ID", 0, 128))])])
        return aff(256, [c], cols(T.pos2, ix, 256), lambda P: P[:, 0:256], -64.0, 192.0 * 64 + 1000, job=j)

    def both(o, hf, deps, aa, ba, ab, bb):
        return positions(o, hf, 0, deps, aa, ba), positions(o, hf, 1, deps, ab, bb)

    def zpass(dep, j, c, n):
        return aff(n, [dep], T.zz[:, c:c + n], lambda P: P[:, 0:n], 1.0, 1536.4921875, job=j, cls="D")

    def bpass(deps, c, n):
        return ts(n // 2, deps, T.bb[:, c:c + n], T.zz[:, c:c + n], 1538.0, 64.0, OP.is_ge, OP.mult)

    def offsets(dep, j, a, nk):
        zj = newjob()
        z = [aff(32 * nk, [dep, c_zi], lambda Z, t=t: cols(T.zi, Z + 1 + 2 * t, 32 * nk, 4), lambda P, t=t: cols(P, 128 * t, 32 * nk),
                 1.0, -98816.0, job=j, cls="M", zj=zj) for t in range(2)]
        s, j2 = mm(z + [c_i16], lambda P, Z: [x for k in range(nk) for x in group(
            [(P[:, 64 * k:64 * k + 64], cols(T.zi, Z + 1 + 128 * k - y, 128), ch("ID", 64 * y, 64)) for y in range(2)])], zj=zj)
        return aff(64 * nk, [s, c_tb], cols(T.mk, a, 64 * nk), lambda P: cols(P, 0, 64 * nk), 1.0, wf(PC + 5), eng=cfg["oe"], job=j2)

    mo = lambda o, hf, k: ((o - 1) * 2 + hf) * 256 + 64 * k
    mi = lambda o, hf, k: (1536 + 128 * ((k + 1) % 4) + 64 * hf if o == 0 else mo(o, hf, 3) if k == 3
                           else 2048 + ((o - 1) * 2 + hf) * 192 + 64 * k)
    gi = lambda o, hf, k: 16 * (mi(o, hf, k) - 1536) if o == 0 else ((o * 2 + hf) * 4 + k) * 1024

    def masks(o, hf, pdep):
        ix = (o - 1) * 2 + hf
        pc, zc = 3072 + ix * 256, (2 + ix) * 1536
        name[0] = "mask%d%d" % (o, hf)
        zat = lambda tl, h: zc + (512 * h + 256 * tl if tl < 2 else 1024 + 256 * h)

        def differ(tls, h):
            a, j = mm([pdep] + s_all, lambda P, Z: [(cols(P, 256 * x, 256), ch("SALL", 128 * tl, 128, 64 * h, 64 * h + 64), cols(
                T.pos2, pc, 256, 1, 64 * h, 64 * h + 64), True, True) for x, tl in enumerate(tls)], cls="D", info="D")
            return zpass(a, j, zat(tls[0], h), 256 * len(tls))
        zs = [[differ((0, 1), h)] for h in range(2)]
        zs.append([differ((2,), h) for h in range(2)])
        bs_ = [[bpass(zs[0] + zs[1], zc, 1024)]] * 2 if cfg["bm"][o - 1] else [[bpass(zs[h], zat(0, h), 512)] for h in range(2)]
        bs_.append([bpass(zs[2], zat(2, 0), 512)])
        out = []
        for k0, nk, tls in ((0, 2, (0, 1)), (2, 2, (1, 2))) if cfg["ab"][o - 1] else ((0, 4, (0, 1, 2)),):
            n = 32 + 8 * nk
            a, j = mm([pdep, zs[0][0]] + s_l, lambda P, Z, k0=k0, n=n: [
                (cols(P, 2 * q0 + h, n, 4), cols(T.pos2, pc + q0, 128, 2), ch("LA", 64 * h + 8 * k0, n), h + q0 == 0, False)
                for h in range(2) for q0 in range(2)], cls="M")
            parts = [(x, [(tl, x) for tl in tls if tl < 2]) for x in range(2)] + [(2, [(2, 0), (2, 1)])] * (2 in tls)
            for t, dep in ((T.zz, zs), (T.bb, bs_)):
                for x, bl in parts:
                    a, _ = mm(dep[x] + c_w[:3], lambda P, Z, t=t, bl=bl, k0=k0, n=n, end=t is T.bb and x == parts[-1][0]: [
                        (cols(P, 2 * q0 + h, n, 4), cols(t, zat(tl, h) + q0, 128, 2), ch("W", 64 * tl + 8 * k0, n), False,
                         end and (tl, h) == bl[-1] and q0 == 1) for tl, h in bl for q0 in range(2)], job=j, cls="M", after=[a])
            out += [offsets(a, j, mo(o, hf, k0), nk)] * nk
        return out

    def masks0():
        out = {}
        cur[:] = [0, 0]
        for pair in cfg["pair"]:
            jm, a = newjob(), None
            for x, k in enumerate(pair):
                zc, pc = k * 768, k * 512
                name[0] = "start%d" % k
                da, j = mm([cv[k]] + s_x, lambda P, Z, pc=pc: [(P[:, 0:512], cb("X", 0, 128), T.pz[:, pc:pc + 512], True, True)],
                           cls="D", info="D")
                za = zpass(da, j, zc, 512)
                db, j = mm([cv[k]] + s_x, lambda P, Z, pc=pc: [(P[64 * h:64 * h + 64, 0:256], cb("X", 128, 64),
                           T.pz[:, pc + 256 * h:pc + 256 * h + 256], True, True) for h in range(2)], cls="D", info="D")
                zb = zpass(db, j, zc + 512, 256)
                b = bpass([za, zb], zc, 768)

                def f(P, Z, x=x, zc=zc, pc=pc, end=18 + len(pair) if x + 1 == len(pair) else -1):
                    l = [(cols(P, 64 * x + 2 * q0 + h, w.shape[1], 4), u, w) for h in range(2) for q0 in range(2) for u, w in (
                        [(cols(t, zc + c + q0, 128, 2), ch("W", w, 64 - 16 * x)) for t in (T.zz, T.bb) for c, w in ((256 * h, 0), (512, 192 + 64 * h))]
                        + [(cols(T.pz, pc + 256 * h + q0, 128, 2), cb("X", 192, 48))])]
                    return [y + (x + i == 0, x + i == end) for i, y in enumerate(l)]
                a, _ = mm([b, s_l0] + c_w, f, job=jm, cls="M", after=[a] if a else [])
            out[pair[0]] = out[pair[-1]] = offsets(a, jm, mi(0, 0, pair[0]), 2 * len(pair))
        return out

    def lookup(o, hf, k, deps, n):
        a, gc0, w = mi(o, hf, k), gi(o, hf, k), 64 * len(deps) // n

        def fg(e, x):
            src = T.tabs[:, 0:8192].indirect(T.mk[:, a + x * w:a + x * w + w])
            dst = T.gat[:, gc0 + 16 * x * w:gc0 + 16 * (x + 1) * w]
            return V.tensor_copy(dst, src) if e == "V" else ACT.activation(dst, src, AF.Copy)
        out = [[] for _ in deps]
        for x in range(n):
            part = range(x * w // 64, ((x + 1) * w - 1) // 64 + 1)
            if o == 0:
                cur[0] = part[0]
            name[0] = "look%d%d%s" % (o, cur[0], "o" if k == 3 else "f")
            i = add("VA", 16 * w, [deps[y] for y in part] + [l_tab], lambda e, P, inc, Z, x=x: inc(fg(e, x)), kind="gat")
            for y in part:
                out[y].append(i)
        return out

    scores = lambda o, hf, k, q, t: cols(T.gat, gi(o, hf, k) + 4 * (q // 2) + 2 * t + q % 2, 128, 8)

    def sums(o, hf, k, P, c):
        return [x for q in range(4) for x in group(
            [(cols(P, c + q, 16, 4), scores(o, hf, k, q, t), cols(T.cb, CB["SEL"] + 3, 16, 4)) for t in range(2)])]

    def turned(o, hf, P, sel):
        return [(P[0:64, 0:128], cb(sel, 3 - q, 64), scores(o, hf, 3, q, t)) for q in range(4) for t in range(2)]

    mk0 = masks0()
    ga0 = {k: lookup(0, 0, k, [mk0[k]] * 2, cfg["g0"]) for k in (3, 0, 1, 2)}
    open_ = lambda l: [x + (False, False) for x in l]
    for hf in range(2):
        cur[:] = [hf, 1]
        col = lambda c, step=1, hf=hf: (lambda q: wf(c + step * (4 * hf + q)))
        mk = masks(1, hf, positions(1, hf, 2, c_b0, col(B1 + 16), col(B0)))
        nxt = both(2, hf, c_b1, col(M + 64), col(B1), col(M), col(B1 + 8))
        F = fdep = None
        flags, acs = [], []
        for r in range(3):
            os_ = (0, 1) if r == 0 else (r + 1,)
            wd = 64 * len(os_)
            sc = lambda k, r=r, hf=hf, wd=wd: (0, 768, 1152)[r] + (hf * 3 + k) * wd
            arr, sar, prev = {}, {}, []
            name[0] = "mask%d%d" % (r + 1, hf)
            for k in range(3):
                a, b = mo(r + 1, hf, k), mi(r + 1, hf, k)
                arr[k] = send("m", r, hf, k, [mk[k]], T.mk[:, a:a + 64], T.mk[:, b:b + 64], 128, prev)
                prev = [arr[k] - 1]
            ga = lookup(r + 1, hf, 0, [arr[k] for k in range(3)], cfg["gf"][r]) + lookup(r + 1, hf, 3, mk[3:], cfg["go"][r])
            g0 = [ga0[k][hf] if r == 0 else [] for k in range(4)]
            prev = []
            name[0] = "sum%d%d" % (r, hf)
            for ks in cfg["ug"][r]:
                j, us = newjob(), []
                for k in ks:
                    for i, o in enumerate(os_):
                        us.append(mm((ga[k] if o else g0[k] + ga[ks[0]]) + c_sel, lambda P, Z, k=k, o=o, hf=hf, c=wd * (k - ks[0]) + 64 * i:
                                     sums(o, hf, k, P, c), job=j, cls="U")[0])
                n = wd * len(ks)
                a = aff(n, us, cols(T.so, sc(ks[0]), n), lambda P, n=n: P[:, 0:n], 1.0, -2048.0, job=j, cls="U")
                for k in ks:
                    sar[k] = send("s", r, hf, k, [a], cols(T.so, sc(k), wd), cols(T.si, sc(k), wd), 2 * wd, prev)
                    prev = [sar[k] - 1]
            ga[3] = ga[3] + g0[3]
            j = newjob()
            name[0] = "vote%d%d" % (r, hf)
            a, _ = mm(ga[3] + c_sel, lambda P, Z, r=r, hf=hf: [
                x + (i == 0, False) for i, x in enumerate(turned(r + 1, hf, P, "SEL"))], job=j, cls="L")
            if r:
                a, _ = mm([fdep, c_i32, c_cr, c_on], lambda P, Z, F=F: open_([
                    (P[0:64, 0:128], wf(I32, 64, 1, 64), wf(F, 128, 1, 64)), (P[0:64, 0:128], cb("CR", 0, 64, 0, 1), cb("ON", 0, 128, 0, 1))]),
                    job=j, cls="L", f32=128, after=[a])
            else:
                a, _ = mm([], lambda P, Z, hf=hf: open_(turned(0, hf, P, "NSEL")), job=j, cls="L", after=[a])
            for k in range(3):
                a, _ = mm([sar[k], c_n16], lambda P, Z, k=k, sc=sc, wd=wd: [
                    (P[0:64, 0:128], cols(T.si, sc(k) + x, 64), ch("NI" if x < wd - 64 else "ID", 0, 128), False, k == 2 and x == wd - 64)
                    for x in range(0, wd, 64)], job=j, cls="L", after=[a])
            CM = cb("CM", 128 * (2 * r + hf), 128, 0, 72)
            cm = vop(128, [a], lambda P, c=128 * (2 * r + hf): V.tensor_scalar(
                cb("CM", c, 128, 0, 64), P[0:64, 0:128], 0.0, 0.5, OP.is_ge, OP.subtract), job=j, cls="L")
            if r < 2:
                ix = ((r + 1) * 2 + hf) * 256
                u, ju = mm([nxt[0], sar[cfg["pre"]]], lambda P, Z, ix=ix: [(P[:, 0:256], ch("ID", 0, 128), cols(T.pos2, ix, 256), True, False)], cls="U")
                u, ju = mm([cm, c_bl, l_th], lambda P, Z, CM=CM: [(cols(P, y, 128), cb("BL", y, 128, 0, 72), CM, False, y > 0) for y in (0, 128)],
                           job=ju, cls="U", after=[u])
                sel = vop(256, [u, nxt[1]], lambda P, ix=ix: V.tensor_tensor(
                    cols(T.pos2, 3072 + ix, 256), P[:, 0:256], cols(T.pos2, 1536 + ix, 256), OP.min), job=ju, cls="U")
                mk = masks(r + 2, hf, sel)
            name[0] = "keep%d%d" % (r, hf)
            AC = wa(128); TQ = wa(128); FN = wa(128)
            u, ju = mm([cm, c_bl, l_th], lambda P, Z, CM=CM: [(P[0:68, 0:128], cb("BL", 256, 68, 0, 72), CM, True, True)])
            ac = vop(128, [u], lambda P, AC=AC: V.tensor_scalar(wf(AC, 128, 1, 68), P[0:68, 0:128], 0.0, None, OP.is_gt), job=ju)
            flags.append((T.ya[r:r + 1, hf * 512:hf * 512 + 512], T.wf[64:68, AC:AC + 128]))
            acs.append(ac)
            if r == 0:
                F = wa(128)
                f0, j0 = mm(ga[3] + list(sar.values()), lambda P, Z, hf=hf, sc=sc: group(
                    [(P[0:64, 0:128], cols(T.si, sc(k), 64), ch("ID", 0, 128)) for k in range(3)] + turned(0, hf, P, "SEL")))
                fdep = aff(128, [f0], wf(F, 128, 1, 64), lambda P: P[0:64, 0:128], 1.0, 6144.0, job=j0)
                AB = wa(16); TP = wa(16)
                u, ju = mm([cm, c_bc, l_th], lambda P, Z, CM=CM: [(P[:, 0:16], CM, cb("QR", 0, 16, 0, 72), True, True)])
                a = vop(64, [u] + c_xy, lambda P, TP=TP, hf=hf: V.tensor_tensor(wf(TP, 16), P[:, 0:16], wf(XS + 16 * hf, 16), OP.min), job=ju)
                a = tt(64, [a], wf(AB, 16), wf(TP, 16), wf(YS + 16 * hf, 16), OP.max)
                a = signed([a], AB, AB, TP, 8, 2)
                at = lambda c: (lambda q: wf(c + 4 * q))
                nxt = both(3, hf, [a], at(AB), at(AB + 1), at(AB + 2), at(AB + 3))
                name[0] = "keep%d%d" % (r, hf)
            a = vop(128, [ac], lambda P, TQ=TQ, AC=AC: V.tensor_tensor(wf(TQ, 128, 1, 64), P[0:64, 0:128], wf(AC, 128, 1, 64), OP.mult),
                    job=j, cls="L")
            fdep = tt(256, [a, fdep], wf(FN, 128, 1, 64), wf(F, 128, 1, 64), wf(TQ, 128, 1, 64), OP.add)
            F = FN
        ldma("A" if hf else "S", acs, "do", 0, 6144, flags)
        ldma("S", [fdep], "do", 0, 32768, [(T.yf[:, hf * 512:hf * 512 + 512], wf(F, 128, 1, 64))])
    assert top[0] <= 4608
    return ops, Q, sent


def dur(op, e, p):
    k = op["kind"]
    if k == "dma":
        return 0.06 * op["n"]
    if k == "rem":
        return p["iss"] + (p["hold"] if op["info"] == "first" else 0.0)
    if e == "P":
        return op["cyc"] * p["pc"] * 1e-3 + p["pf"] * op["n"]
    c = (op["cya"] if e == "A" else 205 + 2 * op["cyc"] if e == "G" and op["info"] != "g" else op["cyc"]) * (p["gr"] if k == "gat" else 1.0)
    return c * 0.83e-3 * p["f"] + (p["fixa"] if e == "A" else p["fix"])


def place(op, e, t0, p, st):
    k = op["kind"]
    if k == "larr":
        if op["info"][0] == "do":
            return t0 + p["ldst"] + op["info"][2] / p["lbw"]
        st["dma"] = max(t0 + p["ldst"], st["dma"]) + op["info"][2] / p["lbw"]
        return st["dma"]
    if k == "rarr":
        t = max(t0 + p["st"] + (0.0 if st["used"] else p["first"]), st["dma"])
        st["used"] = True
        st["dma"] = t + op["info"][2] * (p["row"] + op["info"][3] / p["bw"])
        return st["dma"] + p["wake"]
    return t0 + dur(op, e, p)


def backfill(ops, cfg, p, succ, uses, pri):
    n = len(ops)
    fin, start, eng = [0.0] * n, [0.0] * n, [""] * n
    busy = {e: [] for e in "PVAGSD"}
    left = [len(o["deps"]) + len(o["after"]) for o in ops]
    ready = [i for i in range(n) if left[i] == 0]
    first = [True]

    def gap(e, t, d):
        l = busy[e]
        x = 0
        while x < len(l) and l[x][0] < t + d:
            if l[x][1] > t:
                t = l[x][1]
            x += 1
        return t, x
    while ready:
        i = max(ready, key=lambda x: pri[x] + 1e3 * (ops[x]["eng"] == ""))
        ready.remove(i)
        o = ops[i]
        t = max([fin[d] + p["sem"] for d in o["deps"]] + [fin[d] for d in o["after"]] + [0.0])
        if o["eng"] == "":
            if o["kind"] == "larr":
                t, d, w = t + p["ldst"], o["info"][2] / p["lbw"], 0.0
            else:
                t, d, w = t + p["st"] + p["first"] * first[0], o["info"][2] * (p["row"] + o["info"][3] / p["bw"]), p["wake"]
                first[0] = False
            opts = [(0, "D", d) + gap("D", t, d)]
        else:
            opts, w = [], 0.0
            for e in o["eng"]:
                d = dur(o, e, p) + cfg["pad"]
                s, x = gap(e, t, d)
                bias = cfg["eb"].get(o["name"], 0.0) + cfg["vb"] * (o["kind"] == "gat") if e == "V" else 0.0
                opts.append((s + d + bias, e, d, s, x))
        _, e, d, s, x = min(opts)
        busy[e].insert(x, (s, s + d))
        start[i], fin[i], eng[i] = s, s + d + w, o["eng"] and e
        for y in succ[i]:
            left[y] -= 1
            if left[y] == 0:
                ready.append(y)
    todo = sorted((i for i in range(n) if eng[i]), key=lambda x: (start[x], x))
    limit = dict(LIMIT, D=cfg["maxd"])
    idle, num, touch = [list(range(8)), [8, 9]], dict(L=0, M=0, S=0, D=0, U=0), [{} for _ in range(11)]
    at, done, plan = {None: None}, set(), []
    while todo:
        for i in todo:
            o = ops[i]
            if all(d in done for d in o["deps"] + o["after"]) and (
                    o["job"] in at or idle[0] and num[o["cls"]] < limit[o["cls"]]) and (o["zj"] in at or idle[1]):
                break
        else:
            raise ValueError("no bank")
        todo.remove(i)
        war = []
        for x, j in enumerate((o["job"], o["zj"])):
            if j is not None:
                if j not in at:
                    at[j] = idle[x].pop(0)
                    num[o["cls"]] += 1 - x
                war += [y for e2, y in touch[at[j]].items() if e2 != eng[i]]
                touch[at[j]][eng[i]] = i
                uses[j] -= 1
                if not uses[j]:
                    idle[x].append(at[j])
                    num[o["cls"]] -= 1 - x
        plan.append((i, eng[i], at[o["job"]], at[o["zj"]], war))
        done.add(i)
        for y in succ[i]:
            if ops[y]["eng"] == "":
                plan.append((y, "", None, None, []))
                done.add(y)
    return plan, max(fin)


def schedule(ops, cfg, p):
    n = len(ops)
    succ = [[] for _ in range(n)]
    uses = {}
    for o in ops:
        for d in o["deps"] + o["after"]:
            succ[d].append(o["id"])
        for j in (o["job"], o["zj"]):
            uses[j] = uses.get(j, 0) + 1
    lev = [0.0] * n
    for o in reversed(ops):
        if o["kind"] == "rarr":
            c = p["st"] + o["info"][2] * p["row"] + p["wake"] + cfg["bc"]
        elif o["kind"] == "larr":
            c = p["ldst"] + o["info"][2] / p["lbw"]
        else:
            c = dur(o, o["eng"][0], p) + p["sem"]
        lev[o["id"]] = c + max([lev[s] for s in succ[o["id"]]] + [0.0])
    pri = [lev[i] + cfg["ba"] * (o["tag"][0] != 1) + cfg["bo"] * (o["tag"][1] != 1) + cfg["bd"] * (o["info"] == "D")
           - cfg["bg"] * (o["kind"] == "gat") + cfg["pr"].get(o["name"], 0.0) for i, o in enumerate(ops)]
    if cfg["fill"]:
        return backfill(ops, cfg, p, succ, uses, pri)
    fin = [None] * n
    free = dict(P=0.0, V=0.0, A=0.0, G=0.0, S=0.0)
    st = dict(dma=0.0, used=False)
    limit = dict(LIMIT, D=cfg["maxd"])
    held = [None] * 11
    touch = [{} for _ in range(11)]
    at = {None: None}
    left = [len(o["deps"]) + len(o["after"]) for o in ops]
    ready = [o["id"] for o in ops if left[o["id"]] == 0]
    plan = []

    def done(i):
        for s in succ[i]:
            left[s] -= 1
            if left[s] == 0:
                if ops[s]["eng"] == "":
                    fin[s] = place(ops[s], "", fin[i], p, st)
                    plan.append((s, "", None, None, []))
                    done(s)
                else:
                    ready.append(s)
    while ready:
        cand = []
        for i in ready:
            o = ops[i]
            t = max([fin[d] + p["sem"] for d in o["deps"]] + [0.0])
            res = []
            for j, rng, lim in ((o["job"], range(8), limit[o["cls"]]), (o["zj"], range(8, 11), 3)):
                if j not in at:
                    fr = [b for b in rng if held[b] is None]
                    if not fr or sum(held[b] == o["cls"] for b in rng) >= lim:
                        break
                    res.append(min(fr, key=lambda b: max([fin[x] for x in touch[b].values()] + [-1.0])))
                else:
                    res.append(at[j])
            if len(res) < 2:
                continue
            best = None
            for e in o["eng"]:
                war = [x for b in res if b is not None for e2, x in touch[b].items() if e2 != e]
                t1 = max([t, free[e]] + [fin[x] + p["sem"] for x in war])
                key = (t1 + (dur(o, e, p) if len(o["eng"]) > 1 else 0.0) + (cfg["vb"] if e == "V" and o["kind"] == "gat" else 0.0) + (cfg["eb"].get(o["name"], 0.0) if e == "V" else 0.0), e == "V")
                if best is None or key < best[0]:
                    best = (key, t1, e, war)
            cand.append((best[1], i, best[2], res, best[3]))
        t0, _, e0 = min(cand, key=lambda c: (c[0] - cfg["look"] * (c[2] in "PG"), c[1]))[:3]
        mine = [c for c in cand if c[2] == e0]
        pick = max([c for c in mine if c[0] <= t0 + cfg["slack"]], key=lambda c: pri[c[1]])
        t1 = pick[0] + cfg["alpha"] * dur(ops[pick[1]], e0, p)
        t, i, e, res, war = max([c for c in mine if c[0] <= t1], key=lambda c: pri[c[1]])
        o = ops[i]
        for j, b in zip((o["job"], o["zj"]), res):
            if j is not None:
                at[j] = b
                uses[j] -= 1
                held[b] = (held[b] or o["cls"]) if uses[j] else None
                touch[b][e] = i
        fin[i] = place(o, e, t, p, st)
        free[e] = fin[i]
        plan.append((i, e, res[0], res[1], war))
        ready.remove(i)
        done(i)
    assert len(plan) == n
    return plan, max(fin)


def improve(ops, plan, cfg):
    n = len(ops)
    ps = [dict(NOM, pc=0.417 * v.get("f", NOM["f"]), **v) for v in VARY]
    du = [[{e: dur(o, e, p) for e in o["eng"]} for o in ops] for p in ps]
    pre = [o["deps"] + o["after"] for o in ops]
    succ = [[] for _ in ops]
    land = [[] for _ in ops]
    uses = {}
    for o in ops:
        for d in pre[o["id"]]:
            succ[d].append(o["id"])
        if o["eng"] == "":
            land[o["deps"][0]].append(o["id"])
        for j in (o["job"], o["zj"]):
            uses[j] = uses.get(j, 0) + 1
    real = lambda i: i if ops[i]["eng"] else ops[i]["deps"][0]
    before = [{real(d) for d in pre[i]} for i in range(n)]
    behind = [{x for s in succ[i] for x in ([s] if ops[s]["eng"] else succ[s])} for i in range(n)]
    limit = dict(L=3, M=3, U=3, S=8, D=4)

    def allot(order, eng):
        at, left, out = {}, dict(uses), []
        idle = [list(range(8)), [8, 9, 10]]
        num = dict(L=0, M=0, S=0, D=0, U=0)
        touch = [{} for _ in range(11)]
        for i in order:
            o, e = ops[i], eng[i]
            res, war = [None, None], []
            for x, j in enumerate((o["job"], o["zj"])):
                if j is not None:
                    if j not in at:
                        if not idle[x] or (x == 0 and num[o["cls"]] >= limit[o["cls"]]):
                            return None
                        at[j] = idle[x].pop(0)
                        num[o["cls"]] += 1 - x
                    b = res[x] = at[j]
                    war += [y for e2, y in touch[b].items() if e2 != e]
                    touch[b][e] = i
                    left[j] -= 1
                    if not left[j]:
                        idle[x].append(b)
                        num[o["cls"]] -= 1 - x
            out.append((i, e, res[0], res[1], war))
            out += [(s, "", None, None, []) for s in land[i]]
        return out

    def cost(pl, bound):
        tot = 0.0
        for x, p in enumerate(ps):
            fin = [0.0] * n
            free = dict(P=0.0, V=0.0, A=0.0, G=0.0, S=0.0)
            st = dict(dma=0.0, used=False)
            sem, d = p["sem"], du[x]
            last, why = {}, [None] * n
            for i, e, _, _, war in pl:
                if e:
                    t = free[e] - sem
                    w = last.get(e)
                    for y in deps[i]:
                        if fin[y] > t:
                            t, w = fin[y], y
                    for y in war:
                        if fin[y] > t:
                            t, w = fin[y], y
                    fin[i] = free[e] = t + sem + d[i][e]
                    why[i], last[e] = w, i
                else:
                    why[i] = deps[i][0]
                    fin[i] = place(ops[i], "", fin[why[i]], p, st)
            end = max(fin)
            tot += (end + cfg["mean"] * sum(fin) / n) / ref[x]
            if tot > bound[x]:
                return None, None
            part[x] = tot
            i = fin.index(end)
            chain[x] = []
            while i is not None:
                if why[i] is not None and why[i] not in pre[i]:
                    chain[x].append((why[i], i))
                i = why[i]
        return tot, (list(part), [i for c in chain for i in c])
    deps = [o["deps"] for o in ops]
    chain = [[] for _ in ps]
    order = [x[0] for x in plan if x[1]]
    eng = {x[0]: x[1] for x in plan}
    ref, part = [1.0] * len(ps), [0.0] * len(ps)
    best = allot(order, eng)
    now, (parts, crit) = cost(best, [1e9] * len(ps))
    ref = [parts[x] - (parts[x - 1] if x else 0.0) for x in range(len(ps))]
    now, (parts, crit) = cost(best, [1e9] * len(ps))
    low = now
    rng = np.random.RandomState(cfg["seed"])
    for it in range(cfg["iters"]):
        step = 1 if rng.rand() < 0.5 else -1
        a = order.index(crit[rng.randint(len(crit))][step < 0]) if rng.rand() < cfg["focus"] else int(rng.randint(len(order)))
        i = order[a]
        new, old = order, eng[i]
        u = rng.rand()
        if len(ops[i]["eng"]) > 1 and u < 0.3:
            eng[i] = ops[i]["eng"].replace(old, "")[-1 if u < 0.15 else 0]
        if u > 0.15 or eng[i] == old:
            b, far = a, (1, 1, 1, 2, 3, 5, 8)[rng.randint(7)]
            tied = set(behind[i] if step > 0 else before[i])
            take, rest = [i], []
            while far and 0 <= b + step < len(order):
                b += step
                x = order[b]
                if x in tied:
                    take.append(x)
                    tied |= behind[x] if step > 0 else before[x]
                else:
                    rest.append(x)
                    far -= eng[x] == eng[i]
            new = order[:a] + rest + take + order[b + 1:] if step > 0 else order[:b] + take[::-1] + rest[::-1] + order[a + 1:]
        heat = cfg["heat"] * (1.0 - it / cfg["iters"]) * -math.log(rng.rand() + 1e-12)
        pl = allot(new, eng)
        c = None
        if pl:
            c, pt = cost(pl, [x + heat + 0.003 * (len(ps) - 1 - y) for y, x in enumerate(parts)])
        if c is None:
            eng[i] = old
        else:
            order, now, (parts, crit) = new, c, pt
            if c < low:
                low, best = c, pl
    KEPT["low"] = low
    return best


def refine(ops, plan, cfg):
    n, E, GAP = len(ops), "PVAGS", 24
    ps = [dict(NOM, **dict(dict(pc=0.417 * v.get("f", NOM["f"])), **v)) for v in VARY]
    du = [[[dur(o, e, p) if e in o["eng"] else 0.0 for e in E] for o in ops] for p in ps]
    deps = [o["deps"] for o in ops]
    pre = [o["deps"] + o["after"] for o in ops]
    succ, land = [[] for _ in ops], [[] for _ in ops]
    uses = [0] * (n + 1)
    for o in ops:
        for d in pre[o["id"]]:
            succ[d].append(o["id"])
        if o["eng"] == "":
            land[o["deps"][0]].append(o["id"])
    jobs = [[(x, j) for x, j in enumerate((o["job"], o["zj"])) if j is not None] for o in ops]
    for l in jobs:
        for _, j in l:
            uses[j] += 1
    before = [{d if ops[d]["eng"] else deps[d][0] for d in pre[i]} for i in range(n)]
    behind = [{x for s in succ[i] for x in ([s] if ops[s]["eng"] else succ[s])} for i in range(n)]

    def allot(order, eng, a, state, wait):
        at, left, idle, touch = state[0][:], state[1][:], [state[2][0][:], state[2][1][:]], state[3][:]
        marks = []
        for c in range(a, len(order)):
            if c % GAP == 0:
                marks.append((at[:], left[:], [idle[0][:], idle[1][:]], touch[:]))
            i = order[c]
            w = deps[i]
            for x, j in jobs[i]:
                if at[j] < 0:
                    if not idle[x]:
                        return None
                    at[j] = idle[x].pop(0)
                b, e = 5 * at[j], eng[i]
                w = w + [y for y in touch[b:b + e] + touch[b + e + 1:b + 5] if y >= 0]
                touch[b + e] = i
                left[j] -= 1
                if not left[j]:
                    idle[x].append(at[j])
            wait[i] = w
        return marks, at

    def run(x, order, eng, a, state, wait, fin):
        p, d, sem = ps[x], du[x], ps[x]["sem"]
        free, st = state[0][:], dict(state[1])
        marks = []
        for c in range(a, len(order)):
            if c % GAP == 0:
                marks.append((free[:], dict(st)))
            i = order[c]
            e = eng[i]
            t = free[e] - sem
            for y in wait[i]:
                if fin[y] > t:
                    t = fin[y]
            fin[i] = free[e] = t + sem + d[i][e]
            for s in land[i]:
                fin[s] = place(ops[s], "", fin[i], p, st)
        return max(fin) + cfg["mean"] * sum(fin) / n, marks

    def held(order, eng, wait, fins):
        last, prior, out = [None] * 5, {}, []
        for i in order:
            prior[i], last[eng[i]] = last[eng[i]], i
        for fin, p in zip(fins, ps):
            i = fin.index(max(fin))
            while i is not None:
                if not ops[i]["eng"]:
                    i = deps[i][0]
                    continue
                w = max(wait[i], key=lambda y: fin[y]) if wait[i] else None
                if prior[i] is not None and (w is None or fin[prior[i]] - p["sem"] >= fin[w]):
                    w = prior[i]
                if w is not None and w not in pre[i]:
                    out.append((w, i))
                i = w
        return out
    order = [x[0] for x in plan if x[1]]
    eng = {x[0]: E.index(x[1]) for x in plan if x[1]}
    wait = [None] * n
    bm, at = allot(order, eng, 0, ([-1] * (n + 1), uses, [list(range(8)), [8, 9, 10]], [-1] * 55), wait)
    fins = [[0.0] * n for _ in ps]
    res = [run(x, order, eng, 0, ([0.0] * 5, dict(dma=0.0, used=False)), wait, fins[x]) for x in range(len(ps))]
    ref = [r[0] for r in res]
    tm = [r[1] for r in res]
    parts = [x + 1.0 for x in range(len(ps))]
    low, best = parts[-1], (order, dict(eng))
    crit = held(order, eng, wait, fins)
    rng = np.random.RandomState(cfg["seed"])
    for it, (u0, u1, u2, u3, u4, u5) in enumerate(rng.rand(cfg["iters"], 6).tolist()):
        step = 1 if u0 < 0.5 else -1
        a = order.index(crit[int(u2 * len(crit))][step < 0]) if u1 < cfg["focus"] else int(u2 * len(order))
        i = order[a]
        new, old, b = order, eng[i], a
        if len(ops[i]["eng"]) > 1 and u3 < 0.3:
            eng[i] = E.index(ops[i]["eng"].replace(E[old], "")[-1 if u3 < 0.15 else 0])
        if u3 > 0.15 or eng[i] == old:
            far = (1, 1, 1, 2, 3, 5, 8)[int(u4 * 7)]
            tied = set(behind[i] if step > 0 else before[i])
            take, rest = [i], []
            while far and 0 <= b + step < len(order):
                b += step
                x = order[b]
                if x in tied:
                    take.append(x)
                    tied |= behind[x] if step > 0 else before[x]
                else:
                    rest.append(x)
                    far -= eng[x] == eng[i]
            new = order[:a] + rest + take + order[b + 1:] if step > 0 else order[:b] + take[::-1] + rest[::-1] + order[a + 1:]
        heat = cfg["heat"] * (1.0 - it / cfg["iters"]) * -math.log(u5 + 1e-12)
        m = min(a, b) // GAP
        w2 = wait[:]
        got = allot(new, eng, m * GAP, bm[m], w2)
        tot, trial = 0.0, []
        for x in range(len(ps) if got else 0):
            fin = fins[x][:]
            c, marks = run(x, new, eng, m * GAP, tm[x][m], w2, fin)
            tot += c / ref[x]
            if tot > parts[x] + heat + 0.003 * (len(ps) - 1 - x):
                break
            trial.append((tot, fin, marks))
        if len(trial) < len(ps):
            eng[i] = old
            continue
        order, wait, bm = new, w2, bm[:m] + got[0]
        parts, fins = [r[0] for r in trial], [r[1] for r in trial]
        tm = [tm[x][:m] + trial[x][2] for x in range(len(ps))]
        if it % 4 == 0:
            crit = held(order, eng, wait, fins)
        if tot < low:
            low, best = tot, (order, dict(eng))
    order, eng = best
    at = allot(order, eng, 0, bm[0], wait)[1]
    KEPT["low"] = low
    out = []
    for i in order:
        o = ops[i]
        out.append((i, E[eng[i]], o["job"] and at[o["job"]], o["zj"] and at[o["zj"]], wait[i][len(deps[i]):]))
        out += [(s, "", None, None, []) for s in land[i]]
    return out


def rank_program(g, core, T, topo):
    rank = T.rank_of(core)
    if rank is None:
        return
    ops, Q, sent = build(g, T, rank, topo, CFG, len(topo.engines(core, T.cores[(rank + 1) % N])))
    cnt = dict(P=0, V=0, A=0, G=0)
    know = {e: {} for e in Q}
    tag, clock = {}, {}
    if "plan" not in KEPT:
        KEPT["plan"] = refine(ops, schedule(ops, CFG, NOM)[0], CFG)
    for i, e, bank, zb, war in KEPT["plan"]:
        o = ops[i]
        if e == "":
            tag[i] = (o["info"][0], o["info"][1])
            clock[i] = dict(clock[o["deps"][0]]) if o["kind"] == "larr" else {}
            continue
        kn = know[e]
        need = {}
        for d in o["deps"] + war:
            s, c = tag[d]
            if need.get(s, (0, 0))[0] < c:
                need[s] = (c, d)
        for s, (c, d) in sorted(need.items(), key=lambda x: -x[1][1]):
            if kn.get(s, 0) < c:
                Q[e].wait_ge(T.sem[s], c)
                kn[s] = c
                for s2, c2 in clock[d].items():
                    kn[s2] = max(kn.get(s2, 0), c2)

        def inc(ins, e=e):
            ins.then_inc(T.sem["e" + e], 1)
            cnt[e] += 1
        o["fn"](e, T["ps%d" % bank] if bank is not None else None, inc, 520 * (zb - 8) if zb else 0)
        clock[i] = dict(kn)
        if o["kind"] in ("c", "gat"):
            tag[i] = ("e" + e, cnt[e])
    for e in "PVAG":
        g.sync.wait_ge(T.sem["e" + e], cnt[e])
    g.sync.wait_ge(T.sem["sent"], sent[0])
    g.sync.wait_ge(T.sem["do"], 128)
